import numpy as np
import ml_dtypes


def mxq(x, axis, fmt="e4m3"):
    dtype, down = {"e4m3": (ml_dtypes.float8_e4m3fn, 7), "e5m2": (ml_dtypes.float8_e5m2, 14)}[fmt]
    v = np.moveaxis(np.asarray(x, np.float32).astype(ml_dtypes.bfloat16).astype(np.float64), axis, -1)
    blocks = v.reshape(v.shape[:-1] + (-1, 32))
    amax = np.abs(blocks).max(-1, keepdims=True)
    byte = np.maximum(np.where(amax > 0, np.frexp(amax)[1] - 1 + 127, 0) - down, 1)
    scale = np.exp2(byte - 127.0)
    codes = (blocks / scale).astype(np.float32).astype(dtype).astype(np.float64)
    return np.moveaxis((codes * scale).reshape(v.shape), -1, axis)


WIDE = False


def mx_kscale(k):
    if not WIDE:
        return np.ones(k)
    levels = np.array([10, -10, 5, -5, 0])
    if k % 512:
        return np.exp2(np.random.permutation(np.resize(levels, k // 32))).repeat(32)
    a = np.empty((k // 512, 16))
    for p in range(k // 512):
        a[p, :8] = np.random.permutation(np.resize(levels, 8))
        for g in range(8):
            far = levels[np.abs(levels - a[p, g]) >= 10]
            a[p, g + 8] = far[np.random.randint(len(far))]
    return np.exp2(a.ravel()).repeat(32)


BF16 = ml_dtypes.bfloat16


def bf(x):
    return np.asarray(x, np.float32).astype(BF16)


def f64(x):
    return np.asarray(x).astype(np.float64)


N, V, D = 512, 4, 512
VD = V * D
D2 = 2 * D


def elu(z):
    return np.where(z > 0, z, np.exp(np.minimum(z, 0.0)) - 1.0)


def sigmoid(z):
    return 1.0 / (1.0 + np.exp(-z))


def draw0():
    s = mx_kscale(VD)
    sv = s.reshape(V, D)
    t = mx_kscale(VD).reshape(V, D)
    return {
        "x": bf(np.random.standard_normal((N, V, D)) * sv[None, :, :]),
        "wl": bf(np.random.standard_normal((VD, VD)) * (1.3 / np.sqrt(VD)) / s[:, None]),
        "w1": bf(np.random.standard_normal((V, D, D)) * (1.3 / np.sqrt(D)) / sv[:, :, None]),
        "g1": bf((1.0 + 0.1 * np.random.standard_normal((V, D))) * t),
        "w2": bf(np.random.standard_normal((V, D, D2)) * (1.5 / np.sqrt(D)) / t[:, :, None]),
        "gs": bf((1.0 + 0.1 * np.random.standard_normal((V, D))) / sv),
    }


def core(x, wl, w1, g1, w2, gs):
    x, g1, gs = f64(x), f64(g1), f64(gs)
    n, v, d = x.shape

    xq = mxq(x.reshape(n, v * d), 1, "e4m3")
    lg = (xq @ mxq(f64(wl), 0, "e4m3")).reshape(n, v, d)
    pe = np.exp(lg - lg.max(axis=1, keepdims=True))
    p = pe / pe.sum(axis=1, keepdims=True)

    xv = xq.reshape(n, v, d).transpose(1, 0, 2)
    h = xv @ mxq(f64(w1), 1, "e4m3")
    e = elu(h) * g1[:, None, :]
    u = (mxq(e, 2, "e4m3") @ mxq(f64(w2), 1, "e4m3")).transpose(1, 0, 2)
    t = u[:, :, :d] * sigmoid(u[:, :, d:])
    r = x * gs[None, :, :] + t

    return np.sum(p * r, axis=1)


def e4m3fn_bytes(y):
    return np.clip(np.asarray(y, np.float64), -448.0, 448.0).astype(np.float32).astype(ml_dtypes.float8_e4m3fn).view(np.uint8)


def e4m3fn_values(b):
    return np.asarray(b, np.uint8).view(ml_dtypes.float8_e4m3fn).astype(np.float64)


def setup_inputs():
    d = draw0()
    x0 = np.asarray(d['wl']).astype(np.float64)
    s = (np.max(np.abs(x0), axis=(1,), keepdims=True) / 448.0).astype(np.float32)
    out = {}
    for k, v in d.items():
        if k == 'wl':
            out['wl_bytes'] = e4m3fn_bytes(x0 / s.astype(np.float64))
            out['wl_scale'] = s
        else:
            out[k] = v
    return out


def reference(x, wl_bytes, wl_scale, w1, g1, w2, gs):
    return core(x, e4m3fn_values(wl_bytes) * wl_scale.astype(np.float64), w1, g1, w2, gs)

@@ -1,0 +1,249 @@
+from contextlib import ExitStack
+
+import concourse.mybir as mybir
+from concourse.masks import make_identity
+
+N, V, D = 512, 4, 512
+VD = V * D
+FLOPS = 2 * (N * VD * VD + V * N * D * D + V * N * D * 2 * D)
+
+F32 = mybir.dt.float32
+BF16 = mybir.dt.bfloat16
+U32 = mybir.dt.uint32
+U8 = mybir.dt.uint8
+E4M3 = mybir.dt.float8_e4m3fn
+FP8X4 = mybir.dt.float8_e4m3fn_x4
+ACT = mybir.ActivationFunctionType
+ALU = mybir.AluOpType
+
+P = 128
+T = 4
+NB = N // P
+J = D // P
+
+SCALAR_UNITS = (3, 7, 11, 14, 15)
+
+
+def tile_tftchannelwisevariableselection_kernel(tc, x, wl_bytes, wl_scale, w1, g1, w2, gs, out):
+    nc = tc.nc
+    with ExitStack() as ctx:
+        keep = ctx.enter_context(tc.tile_pool(name="keep", bufs=1))
+        psum = ctx.enter_context(tc.psum_pool(name="psum", bufs=4))
+
+        def bank(tag, shape, dtype, name):
+            return psum.tile(shape, dtype, name=name, tag=tag)
+
+        def interleave(on_scalar, dst, src):
+            if on_scalar:
+                nc.scalar.copy(out=dst, in_=src)
+            else:
+                nc.vector.tensor_copy(out=dst, in_=src)
+
+        def quantize(codes, scales, grouped):
+            nc.vector.quantize_mx(out=codes.bitcast(FP8X4), scales=scales, in_=grouped.rearrange("p c t -> p (c t)"))
+
+        def mx(out_ap, weights, wcols, moving, start, stop):
+            nc.tensor.matmul_mx(
+                out=out_ap,
+                lhsT=weights[0][:, wcols].bitcast(FP8X4),
+                lhsT_scale=weights[1][:, wcols],
+                rhs=moving[0][:].bitcast(FP8X4),
+                rhs_scale=moving[1][:],
+                start=start,
+                stop=stop,
+            )
+
+        def operand(pool, width, name, tag=None, bufs=1):
+            codes = pool.tile([P, width], U32, name=name + "_codes", tag=(tag or name) + "_codes", bufs=bufs, align_bytes=64)
+            scales = pool.tile([P, width], U8, name=name + "_scales", tag=(tag or name) + "_scales", bufs=bufs, align_bytes=64)
+            return codes, scales
+
+        ident_f = keep.tile([P, P], F32, name="ident_f")
+        make_identity(nc, ident_f[:])
+        warm = keep.tile([P, 1], F32, name="warm")
+        nc.vector.memset(warm[:], 0.0)
+        nc.scalar.activation(out=warm[:], in_=warm[:], func=ACT.Exp)
+        wl_s = keep.tile([P, V, T], F32, name="wl_s")
+        nc.gpsimd.dma_start(out=wl_s[:], in_=wl_scale.rearrange("(g p t) o -> p g (t o)", p=P, t=T))
+        g1_b = keep.tile([P, V, T], BF16, name="g1_b")
+        nc.gpsimd.dma_start(out=g1_b[:], in_=g1.rearrange("v (p t) -> p v t", t=T))
+        gs_rows = keep.tile([P, P], BF16, name="gs_rows")
+        nc.gpsimd.memset(gs_rows[:], 0.0)
+        nc.gpsimd.dma_start(out=gs_rows[0 : V * J, :], in_=gs.rearrange("v (j p) -> (v j) p", p=P))
+        ident_b = keep.tile([P, P], BF16, name="ident_b")
+        make_identity(nc, ident_b[:])
+        g1_f = keep.tile([P, V, T], F32, name="g1_f")
+        nc.gpsimd.tensor_copy(out=g1_f[:], in_=g1_b[:])
+
+        x_raw = []
+        xq = []
+        eq = []
+        wlq = []
+        w2q = []
+        for v in range(V):
+            xr = keep.tile([P, NB, D], BF16, name="x_raw%d" % v)
+            x_raw.append(xr)
+            xq.append(operand(keep, N, "xq%d" % v))
+            eq.append(operand(keep, N, "eq%d" % v))
+            wlq.append(operand(keep, VD, "wlq%d" % v))
+            w2q.append(operand(keep, 2 * D, "w2q%d" % v))
+
+        w2raw_pool = ctx.enter_context(tc.tile_pool(name="w2raw", bufs=2))
+
+        with ExitStack() as ctx_a:
+            a = ctx_a.enter_context(tc.tile_pool(name="a", bufs=2))
+            w1_raw = []
+            wl_raw = []
+            for v in range(V):
+                nc.sync.dma_start(out=x_raw[v][:], in_=x[:, v, :].rearrange("(b p) c -> p b c", p=P))
+                w1r = a.tile([P, T, D], BF16, name="w1_raw")
+                w1_raw.append(w1r)
+                nc.sync.dma_start(out=w1r[:], in_=w1[v].rearrange("(p j) c -> p j c", j=T))
+                wlr = a.tile([P, T, VD], U8, name="wl_raw", bufs=3)
+                wl_raw.append(wlr)
+                rows = wl_bytes[v * D : (v + 1) * D, :].rearrange("(p j) c -> p j c", j=T)
+                nc.sync.dma_start(out=wlr[:, 0:2, :], in_=rows[:, 0:2, :])
+                nc.sync.dma_start(out=wlr[:, 2:4, :], in_=rows[:, 2:4, :])
+
+            def wl_unit(g, c):
+                cols = slice(c * D, (c + 1) * D)
+                wide = a.tile([P, T, D], BF16, name="wl_wide", bufs=3)
+                for t in range(T):
+                    nc.scalar.activation(
+                        out=wide[:, t, :],
+                        in_=wl_raw[g][:, t, cols].bitcast(E4M3),
+                        func=ACT.Copy,
+                        scale=wl_s[:, g, t : t + 1],
+                    )
+                grouped = a.tile([P, D, T], BF16, name="wl_grouped", bufs=3, align_bytes=64)
+                interleave(g * V + c in SCALAR_UNITS, grouped[:], wide[:].rearrange("p t c -> p c t"))
+                quantize(wlq[g][0][:, cols], wlq[g][1][:, cols], grouped[:])
+
+            for v in range(V):
+                xg = a.tile([P, N, T], BF16, name="xg", align_bytes=64)
+                words = x_raw[v][:].bitcast(F32)
+                xg_words = xg[:].rearrange("p n t -> p (n t)").bitcast(F32).rearrange("p (n u) -> p n u", u=2)
+                for half in range(2):
+                    xt = bank("hi", [P, 2, 2 * P], F32, "xt")
+                    for u in range(2):
+                        for b in range(2):
+                            nc.tensor.transpose(xt[:, u, b * P : (b + 1) * P], words[:, 2 * half + b, u::2], ident_f[:])
+                    nc.scalar.copy(out=xg_words[:, half * 2 * P : (half + 1) * 2 * P, :], in_=xt[:].rearrange("p u n -> p n u"))
+                quantize(xq[v][0][:], xq[v][1][:], xg[:])
+
+                w1g = a.tile([P, D, T], BF16, name="w1g", align_bytes=64)
+                nc.vector.tensor_copy(
+                    out=w1g[:].rearrange("p (t m) j -> p t m j", t=T),
+                    in_=w1_raw[v][:].rearrange("p j (m t) -> p t m j", t=T),
+                )
+                w1q = operand(a, D, "w1q", bufs=2)
+                quantize(w1q[0][:], w1q[1][:], w1g[:])
+
+                ex = a.tile([P, T, N], F32, name="ex")
+                h = []
+                for t in range(T):
+                    ht = bank("hi", [P, N], F32, "h")
+                    h.append(ht)
+                    mx(ht[:], w1q, slice(t * P, (t + 1) * P), xq[v], True, True)
+                    nc.scalar.activation(out=ex[:, t, :], in_=ht[:], func=ACT.Exp)
+                wl_unit(v, 0)
+                wl_unit(v, 1)
+                nc.vector.tensor_scalar(out=ex[:], in0=ex[:], scalar1=1.0, scalar2=None, op0=ALU.min)
+                for t in range(T):
+                    nc.vector.scalar_tensor_tensor(
+                        out=ex[:, t, :], in0=h[t][:], scalar=1.0, in1=ex[:, t, :], op0=ALU.add, op1=ALU.max
+                    )
+                wl_unit(v, 2)
+                eb = a.tile([P, T, N], BF16, name="eb")
+                for t in range(T):
+                    nc.vector.tensor_scalar(
+                        out=eb[:, t, :],
+                        in0=ex[:, t, :],
+                        scalar1=-1.0,
+                        scalar2=g1_f[:, v, t : t + 1],
+                        op0=ALU.add,
+                        op1=ALU.mult,
+                    )
+                wl_unit(v, 3)
+                eg = a.tile([P, N, T], BF16, name="eg", align_bytes=64)
+                nc.vector.tensor_copy(out=eg[:], in_=eb[:].rearrange("p t n -> p n t"))
+                quantize(eq[v][0][:], eq[v][1][:], eg[:])
+
+        c = ctx.enter_context(tc.tile_pool(name="c", bufs=2))
+        gs_t = bank("hi", [P, P], BF16, "gs_t")
+        nc.tensor.transpose(gs_t[:], gs_rows[:], ident_b[:])
+        gs2 = keep.tile([P, V * J], F32, name="gs2")
+        nc.vector.tensor_scalar(out=gs2[:], in0=gs_t[:, 0 : V * J], scalar1=2.0, scalar2=None, op0=ALU.mult)
+
+        def w2_unit(v, half):
+            cols = slice(half * D, (half + 1) * D)
+            grouped = c.tile([P, D, T], BF16, name="w2g", align_bytes=64)
+            interleave(True, grouped[:], w2_raw[v][:, :, cols].rearrange("p j c -> p c j"))
+            quantize(w2q[v][0][:, cols], w2q[v][1][:, cols], grouped[:])
+
+        w2_raw = []
+        for v in range(V):
+            w2r = w2raw_pool.tile([P, T, 2 * D], BF16, name="w2_raw")
+            w2_raw.append(w2r)
+            nc.sync.dma_start(out=w2r[:], in_=w2[v].rearrange("(p j) c -> p j c", j=T))
+
+        den = c.tile([P, J, N], F32, name="den", bufs=1)
+        e_all = []
+        for j in range(J):
+            lg = []
+            for v in range(V):
+                lv = bank(("lo", "hi")[j % 2], [P, N], F32, "lg")
+                lg.append(lv)
+                for g in range(V):
+                    mx(lv[:], wlq[g], slice(v * D + j * P, v * D + (j + 1) * P), xq[g], g == 0, g == V - 1)
+            l0 = c.tile([P, N], F32, name="l0")
+            nc.scalar.copy(out=l0[:], in_=lg[0][:])
+            top = c.tile([P, N], F32, name="top")
+            nc.vector.tensor_tensor(out=top[:], in0=lg[1][:], in1=l0[:], op=ALU.max)
+            nc.vector.tensor_tensor(out=top[:], in0=lg[2][:], in1=top[:], op=ALU.max)
+            nc.vector.tensor_tensor(out=top[:], in0=lg[3][:], in1=top[:], op=ALU.max)
+            ej = c.tile([P, V, N], F32, name="e%d" % j, bufs=1)
+            e_all.append(ej)
+            for v in range(V):
+                nc.vector.tensor_tensor(out=ej[:, v, :], in0=(l0[:] if v == 0 else lg[v][:]), in1=top[:], op=ALU.subtract)
+                if v % 2 == 1:
+                    nc.scalar.activation(out=ej[:, v - 1 : v + 1, :], in_=ej[:, v - 1 : v + 1, :], func=ACT.Exp)
+            pair = c.tile([P, 2, N], F32, name="pair", bufs=1)
+            nc.gpsimd.tensor_tensor(out=pair[:], in0=ej[:, 0:2, :], in1=ej[:, 2:4, :], op=ALU.add)
+            nc.gpsimd.tensor_tensor(out=den[:, j, :], in0=pair[:, 0, :], in1=pair[:, 1, :], op=ALU.add)
+            w2_unit(j, 0)
+            w2_unit(j, 1)
+        nc.scalar.activation(out=den[:], in_=den[:], func=ACT.Ln, scale=2.0)
+        nc.scalar.activation(out=den[:], in_=den[:], func=ACT.Exp, scale=-1.0)
+
+        for j in range(J):
+            num = bank("lo", [P, N], F32, "num")
+            for v in range(V):
+                if v % 2 == 0:
+                    xt = bank("lo", [P, 2, N], BF16, "xt_b")
+                    for w in range(2):
+                        for b in range(NB):
+                            nc.tensor.transpose(
+                                xt[:, w, b * P : (b + 1) * P], x_raw[v + w][:, b, j * P : (j + 1) * P], ident_b[:]
+                            )
+                u1 = bank("hi", [P, N], F32, "u1")
+                u2 = bank("hi", [P, N], F32, "u2")
+                mx(u2[:], w2q[v], slice(D + j * P, D + (j + 1) * P), eq[v], True, True)
+                mx(u1[:], w2q[v], slice(j * P, (j + 1) * P), eq[v], True, True)
+                th = c.tile([P, N], F32, name="th", bufs=3)
+                nc.scalar.activation(out=th[:], in_=u2[:], func=ACT.Tanh, scale=0.5)
+                r = c.tile([P, N], F32, name="r", bufs=4)
+                nc.vector.scalar_tensor_tensor(out=r[:], in0=th[:], scalar=1.0, in1=u1[:], op0=ALU.add, op1=ALU.mult)
+                nc.vector.scalar_tensor_tensor(
+                    out=r[:], in0=xt[:, v % 2, :], scalar=gs2[:, v * J + j : v * J + j + 1], in1=r[:], op0=ALU.mult, op1=ALU.add
+                )
+                nc.vector.tensor_tensor(out=r[:], in0=e_all[j][:, v, :], in1=r[:], op=ALU.mult)
+                nc.tensor.matmul(num[:], lhsT=ident_f[:], rhs=r[:], start=(v == 0), stop=(v == V - 1))
+            o = c.tile([P, N], F32, name="o")
+            nc.vector.tensor_tensor(out=o[:], in0=num[:], in1=den[:, j, :], op=ALU.mult)
+            ot = bank("lo", [P, NB, P], F32, "ot")
+            for b in range(NB):
+                nc.tensor.transpose(ot[:, b, :], o[:, b * P : (b + 1) * P], ident_f[:])
+            rows = c.tile([P, NB, P], F32, name="rows")
+            nc.scalar.copy(out=rows[:], in_=ot[:])
+            nc.sync.dma_start(out=out[:, j * P : (j + 1) * P].rearrange("(b p) c -> p b c", p=P), in_=rows[:])

@@ -1,249 +1,989 @@
 from contextlib import ExitStack
-
 import concourse.mybir as mybir
 from concourse.masks import make_identity
-
-N, V, D = 512, 4, 512
-VD = V * D
-FLOPS = 2 * (N * VD * VD + V * N * D * D + V * N * D * 2 * D)
-
-F32 = mybir.dt.float32
-BF16 = mybir.dt.bfloat16
-U32 = mybir.dt.uint32
-U8 = mybir.dt.uint8
-E4M3 = mybir.dt.float8_e4m3fn
-FP8X4 = mybir.dt.float8_e4m3fn_x4
+FLOPS = 7516192768
 ACT = mybir.ActivationFunctionType
 ALU = mybir.AluOpType
-
-P = 128
-T = 4
-NB = N // P
-J = D // P
-
-SCALAR_UNITS = (3, 7, 11, 14, 15)
-
+F = mybir.dt.float32
+B = mybir.dt.bfloat16
+U = mybir.dt.uint32
+U8 = mybir.dt.uint8
+X = mybir.dt.float8_e4m3fn_x4
+E4 = mybir.dt.float8_e4m3fn
+S0 = '(g p t) o -> p g (t o)'
+S1 = '(p j) c -> p j c'
+S2 = 'v (p t) -> p v t'
+S3 = '(b p) c -> p b c'
+S4 = '(p t) (v h c) -> p t v h c'
+S5 = 'v (j p) -> (v j) p'
+S6 = 'p (t m) j -> p t m j'
+S7 = 'p j (m t) -> p t m j'
+S8 = 'p t v c -> p t (v c)'
+S9 = 'p c t -> p (c t)'
+S10 = 'p n t -> p (n t)'
+S11 = 'p (n u) -> p n u'
+S12 = 'p u n -> p n u'
+S13 = 'p t c -> p c t'
+S14 = 'p t n -> p n t'
 
 def tile_tftchannelwisevariableselection_kernel(tc, x, wl_bytes, wl_scale, w1, g1, w2, gs, out):
-    nc = tc.nc
-    with ExitStack() as ctx:
-        keep = ctx.enter_context(tc.tile_pool(name="keep", bufs=1))
-        psum = ctx.enter_context(tc.psum_pool(name="psum", bufs=4))
-
-        def bank(tag, shape, dtype, name):
-            return psum.tile(shape, dtype, name=name, tag=tag)
-
-        def interleave(on_scalar, dst, src):
-            if on_scalar:
-                nc.scalar.copy(out=dst, in_=src)
-            else:
-                nc.vector.tensor_copy(out=dst, in_=src)
-
-        def quantize(codes, scales, grouped):
-            nc.vector.quantize_mx(out=codes.bitcast(FP8X4), scales=scales, in_=grouped.rearrange("p c t -> p (c t)"))
-
-        def mx(out_ap, weights, wcols, moving, start, stop):
-            nc.tensor.matmul_mx(
-                out=out_ap,
-                lhsT=weights[0][:, wcols].bitcast(FP8X4),
-                lhsT_scale=weights[1][:, wcols],
-                rhs=moving[0][:].bitcast(FP8X4),
-                rhs_scale=moving[1][:],
-                start=start,
-                stop=stop,
-            )
-
-        def operand(pool, width, name, tag=None, bufs=1):
-            codes = pool.tile([P, width], U32, name=name + "_codes", tag=(tag or name) + "_codes", bufs=bufs, align_bytes=64)
-            scales = pool.tile([P, width], U8, name=name + "_scales", tag=(tag or name) + "_scales", bufs=bufs, align_bytes=64)
-            return codes, scales
-
-        ident_f = keep.tile([P, P], F32, name="ident_f")
-        make_identity(nc, ident_f[:])
-        warm = keep.tile([P, 1], F32, name="warm")
-        nc.vector.memset(warm[:], 0.0)
-        nc.scalar.activation(out=warm[:], in_=warm[:], func=ACT.Exp)
-        wl_s = keep.tile([P, V, T], F32, name="wl_s")
-        nc.gpsimd.dma_start(out=wl_s[:], in_=wl_scale.rearrange("(g p t) o -> p g (t o)", p=P, t=T))
-        g1_b = keep.tile([P, V, T], BF16, name="g1_b")
-        nc.gpsimd.dma_start(out=g1_b[:], in_=g1.rearrange("v (p t) -> p v t", t=T))
-        gs_rows = keep.tile([P, P], BF16, name="gs_rows")
-        nc.gpsimd.memset(gs_rows[:], 0.0)
-        nc.gpsimd.dma_start(out=gs_rows[0 : V * J, :], in_=gs.rearrange("v (j p) -> (v j) p", p=P))
-        ident_b = keep.tile([P, P], BF16, name="ident_b")
-        make_identity(nc, ident_b[:])
-        g1_f = keep.tile([P, V, T], F32, name="g1_f")
-        nc.gpsimd.tensor_copy(out=g1_f[:], in_=g1_b[:])
-
-        x_raw = []
-        xq = []
-        eq = []
-        wlq = []
-        w2q = []
-        for v in range(V):
-            xr = keep.tile([P, NB, D], BF16, name="x_raw%d" % v)
-            x_raw.append(xr)
-            xq.append(operand(keep, N, "xq%d" % v))
-            eq.append(operand(keep, N, "eq%d" % v))
-            wlq.append(operand(keep, VD, "wlq%d" % v))
-            w2q.append(operand(keep, 2 * D, "w2q%d" % v))
-
-        w2raw_pool = ctx.enter_context(tc.tile_pool(name="w2raw", bufs=2))
-
-        with ExitStack() as ctx_a:
-            a = ctx_a.enter_context(tc.tile_pool(name="a", bufs=2))
-            w1_raw = []
-            wl_raw = []
-            for v in range(V):
-                nc.sync.dma_start(out=x_raw[v][:], in_=x[:, v, :].rearrange("(b p) c -> p b c", p=P))
-                w1r = a.tile([P, T, D], BF16, name="w1_raw")
-                w1_raw.append(w1r)
-                nc.sync.dma_start(out=w1r[:], in_=w1[v].rearrange("(p j) c -> p j c", j=T))
-                wlr = a.tile([P, T, VD], U8, name="wl_raw", bufs=3)
-                wl_raw.append(wlr)
-                rows = wl_bytes[v * D : (v + 1) * D, :].rearrange("(p j) c -> p j c", j=T)
-                nc.sync.dma_start(out=wlr[:, 0:2, :], in_=rows[:, 0:2, :])
-                nc.sync.dma_start(out=wlr[:, 2:4, :], in_=rows[:, 2:4, :])
-
-            def wl_unit(g, c):
-                cols = slice(c * D, (c + 1) * D)
-                wide = a.tile([P, T, D], BF16, name="wl_wide", bufs=3)
-                for t in range(T):
-                    nc.scalar.activation(
-                        out=wide[:, t, :],
-                        in_=wl_raw[g][:, t, cols].bitcast(E4M3),
-                        func=ACT.Copy,
-                        scale=wl_s[:, g, t : t + 1],
-                    )
-                grouped = a.tile([P, D, T], BF16, name="wl_grouped", bufs=3, align_bytes=64)
-                interleave(g * V + c in SCALAR_UNITS, grouped[:], wide[:].rearrange("p t c -> p c t"))
-                quantize(wlq[g][0][:, cols], wlq[g][1][:, cols], grouped[:])
-
-            for v in range(V):
-                xg = a.tile([P, N, T], BF16, name="xg", align_bytes=64)
-                words = x_raw[v][:].bitcast(F32)
-                xg_words = xg[:].rearrange("p n t -> p (n t)").bitcast(F32).rearrange("p (n u) -> p n u", u=2)
-                for half in range(2):
-                    xt = bank("hi", [P, 2, 2 * P], F32, "xt")
-                    for u in range(2):
-                        for b in range(2):
-                            nc.tensor.transpose(xt[:, u, b * P : (b + 1) * P], words[:, 2 * half + b, u::2], ident_f[:])
-                    nc.scalar.copy(out=xg_words[:, half * 2 * P : (half + 1) * 2 * P, :], in_=xt[:].rearrange("p u n -> p n u"))
-                quantize(xq[v][0][:], xq[v][1][:], xg[:])
-
-                w1g = a.tile([P, D, T], BF16, name="w1g", align_bytes=64)
-                nc.vector.tensor_copy(
-                    out=w1g[:].rearrange("p (t m) j -> p t m j", t=T),
-                    in_=w1_raw[v][:].rearrange("p j (m t) -> p t m j", t=T),
-                )
-                w1q = operand(a, D, "w1q", bufs=2)
-                quantize(w1q[0][:], w1q[1][:], w1g[:])
-
-                ex = a.tile([P, T, N], F32, name="ex")
-                h = []
-                for t in range(T):
-                    ht = bank("hi", [P, N], F32, "h")
-                    h.append(ht)
-                    mx(ht[:], w1q, slice(t * P, (t + 1) * P), xq[v], True, True)
-                    nc.scalar.activation(out=ex[:, t, :], in_=ht[:], func=ACT.Exp)
-                wl_unit(v, 0)
-                wl_unit(v, 1)
-                nc.vector.tensor_scalar(out=ex[:], in0=ex[:], scalar1=1.0, scalar2=None, op0=ALU.min)
-                for t in range(T):
-                    nc.vector.scalar_tensor_tensor(
-                        out=ex[:, t, :], in0=h[t][:], scalar=1.0, in1=ex[:, t, :], op0=ALU.add, op1=ALU.max
-                    )
-                wl_unit(v, 2)
-                eb = a.tile([P, T, N], BF16, name="eb")
-                for t in range(T):
-                    nc.vector.tensor_scalar(
-                        out=eb[:, t, :],
-                        in0=ex[:, t, :],
-                        scalar1=-1.0,
-                        scalar2=g1_f[:, v, t : t + 1],
-                        op0=ALU.add,
-                        op1=ALU.mult,
-                    )
-                wl_unit(v, 3)
-                eg = a.tile([P, N, T], BF16, name="eg", align_bytes=64)
-                nc.vector.tensor_copy(out=eg[:], in_=eb[:].rearrange("p t n -> p n t"))
-                quantize(eq[v][0][:], eq[v][1][:], eg[:])
-
-        c = ctx.enter_context(tc.tile_pool(name="c", bufs=2))
-        gs_t = bank("hi", [P, P], BF16, "gs_t")
-        nc.tensor.transpose(gs_t[:], gs_rows[:], ident_b[:])
-        gs2 = keep.tile([P, V * J], F32, name="gs2")
-        nc.vector.tensor_scalar(out=gs2[:], in0=gs_t[:, 0 : V * J], scalar1=2.0, scalar2=None, op0=ALU.mult)
-
-        def w2_unit(v, half):
-            cols = slice(half * D, (half + 1) * D)
-            grouped = c.tile([P, D, T], BF16, name="w2g", align_bytes=64)
-            interleave(True, grouped[:], w2_raw[v][:, :, cols].rearrange("p j c -> p c j"))
-            quantize(w2q[v][0][:, cols], w2q[v][1][:, cols], grouped[:])
-
-        w2_raw = []
-        for v in range(V):
-            w2r = w2raw_pool.tile([P, T, 2 * D], BF16, name="w2_raw")
-            w2_raw.append(w2r)
-            nc.sync.dma_start(out=w2r[:], in_=w2[v].rearrange("(p j) c -> p j c", j=T))
-
-        den = c.tile([P, J, N], F32, name="den", bufs=1)
-        e_all = []
-        for j in range(J):
-            lg = []
-            for v in range(V):
-                lv = bank(("lo", "hi")[j % 2], [P, N], F32, "lg")
-                lg.append(lv)
-                for g in range(V):
-                    mx(lv[:], wlq[g], slice(v * D + j * P, v * D + (j + 1) * P), xq[g], g == 0, g == V - 1)
-            l0 = c.tile([P, N], F32, name="l0")
-            nc.scalar.copy(out=l0[:], in_=lg[0][:])
-            top = c.tile([P, N], F32, name="top")
-            nc.vector.tensor_tensor(out=top[:], in0=lg[1][:], in1=l0[:], op=ALU.max)
-            nc.vector.tensor_tensor(out=top[:], in0=lg[2][:], in1=top[:], op=ALU.max)
-            nc.vector.tensor_tensor(out=top[:], in0=lg[3][:], in1=top[:], op=ALU.max)
-            ej = c.tile([P, V, N], F32, name="e%d" % j, bufs=1)
-            e_all.append(ej)
-            for v in range(V):
-                nc.vector.tensor_tensor(out=ej[:, v, :], in0=(l0[:] if v == 0 else lg[v][:]), in1=top[:], op=ALU.subtract)
-                if v % 2 == 1:
-                    nc.scalar.activation(out=ej[:, v - 1 : v + 1, :], in_=ej[:, v - 1 : v + 1, :], func=ACT.Exp)
-            pair = c.tile([P, 2, N], F32, name="pair", bufs=1)
-            nc.gpsimd.tensor_tensor(out=pair[:], in0=ej[:, 0:2, :], in1=ej[:, 2:4, :], op=ALU.add)
-            nc.gpsimd.tensor_tensor(out=den[:, j, :], in0=pair[:, 0, :], in1=pair[:, 1, :], op=ALU.add)
-            w2_unit(j, 0)
-            w2_unit(j, 1)
-        nc.scalar.activation(out=den[:], in_=den[:], func=ACT.Ln, scale=2.0)
-        nc.scalar.activation(out=den[:], in_=den[:], func=ACT.Exp, scale=-1.0)
-
-        for j in range(J):
-            num = bank("lo", [P, N], F32, "num")
-            for v in range(V):
-                if v % 2 == 0:
-                    xt = bank("lo", [P, 2, N], BF16, "xt_b")
-                    for w in range(2):
-                        for b in range(NB):
-                            nc.tensor.transpose(
-                                xt[:, w, b * P : (b + 1) * P], x_raw[v + w][:, b, j * P : (j + 1) * P], ident_b[:]
-                            )
-                u1 = bank("hi", [P, N], F32, "u1")
-                u2 = bank("hi", [P, N], F32, "u2")
-                mx(u2[:], w2q[v], slice(D + j * P, D + (j + 1) * P), eq[v], True, True)
-                mx(u1[:], w2q[v], slice(j * P, (j + 1) * P), eq[v], True, True)
-                th = c.tile([P, N], F32, name="th", bufs=3)
-                nc.scalar.activation(out=th[:], in_=u2[:], func=ACT.Tanh, scale=0.5)
-                r = c.tile([P, N], F32, name="r", bufs=4)
-                nc.vector.scalar_tensor_tensor(out=r[:], in0=th[:], scalar=1.0, in1=u1[:], op0=ALU.add, op1=ALU.mult)
-                nc.vector.scalar_tensor_tensor(
-                    out=r[:], in0=xt[:, v % 2, :], scalar=gs2[:, v * J + j : v * J + j + 1], in1=r[:], op0=ALU.mult, op1=ALU.add
-                )
-                nc.vector.tensor_tensor(out=r[:], in0=e_all[j][:, v, :], in1=r[:], op=ALU.mult)
-                nc.tensor.matmul(num[:], lhsT=ident_f[:], rhs=r[:], start=(v == 0), stop=(v == V - 1))
-            o = c.tile([P, N], F32, name="o")
-            nc.vector.tensor_tensor(out=o[:], in0=num[:], in1=den[:, j, :], op=ALU.mult)
-            ot = bank("lo", [P, NB, P], F32, "ot")
-            for b in range(NB):
-                nc.tensor.transpose(ot[:, b, :], o[:, b * P : (b + 1) * P], ident_f[:])
-            rows = c.tile([P, NB, P], F32, name="rows")
-            nc.scalar.copy(out=rows[:], in_=ot[:])
-            nc.sync.dma_start(out=out[:, j * P : (j + 1) * P].rearrange("(b p) c -> p b c", p=P), in_=rows[:])
+ nc = tc.nc
+ ve = nc.vector
+ sc = nc.scalar
+ te = nc.tensor
+ TR = te.transpose
+ def M(o, a, b, k, c, d, x, y):
+  te.matmul_mx(out=o, lhsT=a[:, k:k+128].bitcast(X), lhsT_scale=b[:, k:k+128], rhs=c[:].bitcast(X), rhs_scale=d[:], start=x == 1, stop=y == 1)
+ def Q(o, s, i):
+  ve.quantize_mx(out=o.bitcast(X), scales=s, in_=i)
+ with ExitStack() as ctx:
+  keep_pool = ctx.enter_context(tc.tile_pool(name='keep_pool', bufs=1))
+  AQ = ctx.enter_context(tc.tile_pool(name='AQ', bufs=2))
+  psum_pool = ctx.enter_context(tc.psum_pool(name='psum_pool', bufs=1))
+  ctx.enter_context(tc.manual_schedule())
+  KP = keep_pool.tile
+  PP = psum_pool.tile
+  ST = ve.scalar_tensor_tensor
+  TT = ve.tensor_tensor
+  DM = nc.sync.dma_start
+  MT = te.matmul
+  def AC(o, i, f, scale=1.0):
+   sc.activation(out=o, in_=i, func=f, scale=scale)
+  def SC(o, i):
+   sc.copy(out=o, in_=i)
+  T0 = KP([128, 128], F, tag='ident_f', bufs=1)
+  make_identity(nc, T0[:])
+  T1 = KP([128, 1], F, tag='warm', bufs=1)
+  ve.memset(T1[:], 0.0)
+  T2 = KP([128, 4, 4], F, tag='wl_s', bufs=1)
+  nc.gpsimd.dma_start(out=T2[:], in_=wl_scale.rearrange(S0, p=128, t=4))
+  T43 = AQ.tile([128, 4, 512], B, tag='w1_raw_0', bufs=1)
+  DM(out=T43[:], in_=w1[0].rearrange(S1, j=4))
+  T4 = KP([128, 4, 4], B, tag='g1_b', bufs=1)
+  nc.gpsimd.dma_start(out=T4[:], in_=g1.rearrange(S2, t=4))
+  T7 = KP([128, 4, 512], B, tag='x_raw0', bufs=1)
+  DM(out=T7[:], in_=x[:, 0, :].rearrange(S3, p=128))
+  T44 = AQ.tile([128, 4, 4, 256], U8, tag='wl_raw_0', bufs=1)
+  DM(out=T44[:, 0, :, :], in_=wl_bytes[0:512, :].rearrange(S4, t=4, v=4, h=2)[:, 0, :, 0, :])
+  AC(T1[:], T1[:], ACT.Exp)
+  DM(out=T44[:, 1, :, :], in_=wl_bytes[0:512, :].rearrange(S4, t=4, v=4, h=2)[:, 1, :, 0, :])
+  DM(out=T44[:, 2, :, :], in_=wl_bytes[0:512, :].rearrange(S4, t=4, v=4, h=2)[:, 2, :, 0, :])
+  DM(out=T44[:, 3, :, :], in_=wl_bytes[0:512, :].rearrange(S4, t=4, v=4, h=2)[:, 3, :, 0, :])
+  T45 = AQ.tile([128, 4, 512], B, tag='w1_raw_1', bufs=1)
+  DM(out=T45[:], in_=w1[1].rearrange(S1, j=4))
+  T3 = KP([128, 128], B, tag='ident_b', bufs=1)
+  make_identity(nc, T3[:])
+  T16 = KP([128, 4, 512], B, tag='x_raw1', bufs=1)
+  DM(out=T16[:], in_=x[:, 1, :].rearrange(S3, p=128))
+  T46 = AQ.tile([128, 4, 4, 256], U8, tag='wl_raw_1', bufs=1)
+  DM(out=T46[:, 0, :, :], in_=wl_bytes[512:1024, :].rearrange(S4, t=4, v=4, h=2)[:, 0, :, 0, :])
+  DM(out=T46[:, 1, :, :], in_=wl_bytes[512:1024, :].rearrange(S4, t=4, v=4, h=2)[:, 1, :, 0, :])
+  DM(out=T46[:, 2, :, :], in_=wl_bytes[512:1024, :].rearrange(S4, t=4, v=4, h=2)[:, 2, :, 0, :])
+  DM(out=T46[:, 3, :, :], in_=wl_bytes[512:1024, :].rearrange(S4, t=4, v=4, h=2)[:, 3, :, 0, :])
+  T25 = KP([128, 4, 512], B, tag='x_raw2', bufs=1)
+  DM(out=T25[:], in_=x[:, 2, :].rearrange(S3, p=128))
+  T34 = KP([128, 4, 512], B, tag='x_raw3', bufs=1)
+  DM(out=T34[:], in_=x[:, 3, :].rearrange(S3, p=128))
+  T5 = KP([128, 128], B, tag='gs_rows', bufs=1)
+  nc.gpsimd.memset(T5[:], 0.0)
+  nc.gpsimd.dma_start(out=T5[0:16, :], in_=gs.rearrange(S5, p=128))
+  T49 = AQ.tile([128, 512, 4], B, tag='w1g', bufs=1, align_bytes=64)
+  ve.tensor_copy(out=T49[:].rearrange(S6, t=4), in_=T43[:].rearrange(S7, t=4))
+  T6 = KP([128, 4, 4], F, tag='g1_f', bufs=1)
+  nc.gpsimd.tensor_copy(out=T6[:], in_=T4[:])
+  T51 = PP([128, 2, 256], F, tag='l_0', bufs=1)
+  TR(T51[:, 0, 0:128], T7[:].bitcast(F)[:, 0, 0::2], T0[:])
+  TR(T51[:, 0, 128:256], T7[:].bitcast(F)[:, 1, 0::2], T0[:])
+  TR(T51[:, 1, 0:128], T7[:].bitcast(F)[:, 0, 1::2], T0[:])
+  T53 = AQ.tile([128, 4, 512], B, tag='wl_wide_0', bufs=1)
+  AC(T53[:, 0, :], T44[:].rearrange(S8)[:, 0, 0:512].bitcast(E4), ACT.Copy, scale=T2[:, 0, 0:1])
+  T47 = AQ.tile([128, 512], U, tag='w1q_codes_0', bufs=1, align_bytes=64)
+  T48 = AQ.tile([128, 512], U8, tag='w1q_scales_0', bufs=1, align_bytes=64)
+  Q(T47[:, 0:512], T48[:, 0:512], T49[:].rearrange(S9))
+  T59 = AQ.tile([128, 4, 512], B, tag='w1_raw_0', bufs=1)
+  DM(out=T59[:], in_=w1[2].rearrange(S1, j=4))
+  TR(T51[:, 1, 128:256], T7[:].bitcast(F)[:, 1, 1::2], T0[:])
+  T60 = AQ.tile([128, 4, 4, 256], U8, tag='wl_raw_2', bufs=1)
+  DM(out=T60[:, 0, :, :], in_=wl_bytes[1024:1536, :].rearrange(S4, t=4, v=4, h=2)[:, 0, :, 0, :])
+  T52 = PP([128, 2, 256], F, tag='l_1', bufs=1)
+  TR(T52[:, 0, 0:128], T7[:].bitcast(F)[:, 2, 0::2], T0[:])
+  DM(out=T60[:, 1, :, :], in_=wl_bytes[1024:1536, :].rearrange(S4, t=4, v=4, h=2)[:, 1, :, 0, :])
+  DM(out=T60[:, 2, :, :], in_=wl_bytes[1024:1536, :].rearrange(S4, t=4, v=4, h=2)[:, 2, :, 0, :])
+  TR(T52[:, 0, 128:256], T7[:].bitcast(F)[:, 3, 0::2], T0[:])
+  DM(out=T60[:, 3, :, :], in_=wl_bytes[1024:1536, :].rearrange(S4, t=4, v=4, h=2)[:, 3, :, 0, :])
+  TR(T52[:, 1, 0:128], T7[:].bitcast(F)[:, 2, 1::2], T0[:])
+  T50 = AQ.tile([128, 512, 4], B, tag='xg', bufs=1, align_bytes=64)
+  SC(T50[:].rearrange(S10).bitcast(F).rearrange(S11, u=2)[:, 0:256, :], T51[:].rearrange(S12))
+  TR(T52[:, 1, 128:256], T7[:].bitcast(F)[:, 3, 1::2], T0[:])
+  SC(T50[:].rearrange(S10).bitcast(F).rearrange(S11, u=2)[:, 256:512, :], T52[:].rearrange(S12))
+  AC(T53[:, 1, :], T44[:].rearrange(S8)[:, 1, 0:512].bitcast(E4), ACT.Copy, scale=T2[:, 0, 1:2])
+  T8 = KP([128, 512], U, tag='xq0_codes', bufs=1, align_bytes=64)
+  T9 = KP([128, 512], U8, tag='xq0_scales', bufs=1, align_bytes=64)
+  Q(T8[:, 0:512], T9[:, 0:512], T50[:].rearrange(S9))
+  AC(T53[:, 2, :], T44[:].rearrange(S8)[:, 2, 0:512].bitcast(E4), ACT.Copy, scale=T2[:, 0, 2:3])
+  T63 = AQ.tile([128, 512, 4], B, tag='w1g', bufs=1, align_bytes=64)
+  ve.tensor_copy(out=T63[:].rearrange(S6, t=4), in_=T45[:].rearrange(S7, t=4))
+  T55 = PP([128, 512], F, tag='h_0', bufs=1)
+  M(T55[:], T47, T48, 0, T8, T9, 1, 1)
+  AC(T53[:, 3, :], T44[:].rearrange(S8)[:, 3, 0:512].bitcast(E4), ACT.Copy, scale=T2[:, 0, 3:4])
+  T56 = PP([128, 512], F, tag='h_1', bufs=1)
+  M(T56[:], T47, T48, 128, T8, T9, 1, 1)
+  T57 = PP([128, 512], F, tag='h_2', bufs=1)
+  M(T57[:], T47, T48, 256, T8, T9, 1, 1)
+  T54 = AQ.tile([128, 4, 512], F, tag='f8_0', bufs=1)
+  AC(T54[:, 0, :], T55[:], ACT.Exp)
+  T58 = PP([128, 512], F, tag='h_3', bufs=1)
+  M(T58[:], T47, T48, 384, T8, T9, 1, 1)
+  T65 = PP([128, 2, 256], F, tag='l_2', bufs=1)
+  TR(T65[:, 0, 0:128], T16[:].bitcast(F)[:, 0, 0::2], T0[:])
+  T61 = AQ.tile([128, 512], U, tag='w1q_codes_1', bufs=1, align_bytes=64)
+  T62 = AQ.tile([128, 512], U8, tag='w1q_scales_1', bufs=1, align_bytes=64)
+  Q(T61[:, 0:512], T62[:, 0:512], T63[:].rearrange(S9))
+  T81 = AQ.tile([128, 4, 512], B, tag='w1_raw_1', bufs=1)
+  DM(out=T81[:], in_=w1[3].rearrange(S1, j=4))
+  AC(T54[:, 1, :], T56[:], ACT.Exp)
+  TR(T65[:, 0, 128:256], T16[:].bitcast(F)[:, 1, 0::2], T0[:])
+  TR(T65[:, 1, 0:128], T16[:].bitcast(F)[:, 0, 1::2], T0[:])
+  TR(T65[:, 1, 128:256], T16[:].bitcast(F)[:, 1, 1::2], T0[:])
+  T66 = PP([128, 2, 256], F, tag='l_0', bufs=1)
+  TR(T66[:, 0, 0:128], T16[:].bitcast(F)[:, 2, 0::2], T0[:])
+  AC(T54[:, 2, :], T57[:], ACT.Exp)
+  TR(T66[:, 0, 128:256], T16[:].bitcast(F)[:, 3, 0::2], T0[:])
+  TR(T66[:, 1, 0:128], T16[:].bitcast(F)[:, 2, 1::2], T0[:])
+  TR(T66[:, 1, 128:256], T16[:].bitcast(F)[:, 3, 1::2], T0[:])
+  T68 = PP([128, 256, 4], B, tag='l_1', bufs=1)
+  MT(T68[:, 0:128, :], lhsT=T3[:], rhs=T53[:, :, 0:128].rearrange(S13), start=True, stop=True)
+  AC(T54[:, 3, :], T58[:], ACT.Exp)
+  MT(T68[:, 128:256, :], lhsT=T3[:], rhs=T53[:, :, 128:256].rearrange(S13), start=True, stop=True)
+  T64 = AQ.tile([128, 512, 4], B, tag='xg', bufs=1, align_bytes=64)
+  SC(T64[:].rearrange(S10).bitcast(F).rearrange(S11, u=2)[:, 0:256, :], T65[:].rearrange(S12))
+  ve.tensor_scalar(out=T54[:], in0=T54[:], scalar1=1.0, scalar2=None, op0=ALU.min)
+  SC(T64[:].rearrange(S10).bitcast(F).rearrange(S11, u=2)[:, 256:512, :], T66[:].rearrange(S12))
+  T69 = PP([128, 256, 4], B, tag='l_2', bufs=1)
+  MT(T69[:, 0:128, :], lhsT=T3[:], rhs=T53[:, :, 256:384].rearrange(S13), start=True, stop=True)
+  MT(T69[:, 128:256, :], lhsT=T3[:], rhs=T53[:, :, 384:512].rearrange(S13), start=True, stop=True)
+  T67 = AQ.tile([128, 512, 4], B, tag='grouped_0', bufs=1, align_bytes=64)
+  SC(T67[:, 0:256, :], T68[:])
+  T133 = PP([128, 128], B, tag='x', bufs=1)
+  TR(T133[:], T5[:], T3[:])
+  T17 = KP([128, 512], U, tag='xq1_codes', bufs=1, align_bytes=64)
+  T18 = KP([128, 512], U8, tag='xq1_scales', bufs=1, align_bytes=64)
+  Q(T17[:, 0:512], T18[:, 0:512], T64[:].rearrange(S9))
+  SC(T67[:, 256:512, :], T69[:])
+  ST(out=T54[:, 0, :], in0=T55[:], scalar=1.0, in1=T54[:, 0, :], op0=ALU.add, op1=ALU.max)
+  T70 = AQ.tile([128, 4, 512], B, tag='wl_wide_1', bufs=1)
+  AC(T70[:, 0, :], T44[:].rearrange(S8)[:, 0, 512:1024].bitcast(E4), ACT.Copy, scale=T2[:, 0, 0:1])
+  T87 = PP([128, 2, 256], F, tag='l_2', bufs=1)
+  TR(T87[:, 0, 0:128], T25[:].bitcast(F)[:, 0, 0::2], T0[:])
+  ST(out=T54[:, 1, :], in0=T56[:], scalar=1.0, in1=T54[:, 1, :], op0=ALU.add, op1=ALU.max)
+  T76 = PP([128, 512], F, tag='h_0', bufs=1)
+  M(T76[:], T61, T62, 0, T17, T18, 1, 1)
+  AC(T70[:, 1, :], T44[:].rearrange(S8)[:, 1, 512:1024].bitcast(E4), ACT.Copy, scale=T2[:, 0, 1:2])
+  TR(T87[:, 0, 128:256], T25[:].bitcast(F)[:, 1, 0::2], T0[:])
+  ST(out=T54[:, 2, :], in0=T57[:], scalar=1.0, in1=T54[:, 2, :], op0=ALU.add, op1=ALU.max)
+  TR(T87[:, 1, 0:128], T25[:].bitcast(F)[:, 0, 1::2], T0[:])
+  T77 = PP([128, 512], F, tag='h_1', bufs=1)
+  M(T77[:], T61, T62, 128, T17, T18, 1, 1)
+  AC(T70[:, 2, :], T44[:].rearrange(S8)[:, 2, 512:1024].bitcast(E4), ACT.Copy, scale=T2[:, 0, 2:3])
+  TR(T87[:, 1, 128:256], T25[:].bitcast(F)[:, 1, 1::2], T0[:])
+  ST(out=T54[:, 3, :], in0=T58[:], scalar=1.0, in1=T54[:, 3, :], op0=ALU.add, op1=ALU.max)
+  T78 = PP([128, 512], F, tag='h_2', bufs=1)
+  M(T78[:], T61, T62, 256, T17, T18, 1, 1)
+  AC(T70[:, 3, :], T44[:].rearrange(S8)[:, 3, 512:1024].bitcast(E4), ACT.Copy, scale=T2[:, 0, 3:4])
+  T12 = KP([128, 2048], U, tag='wlq0_codes', bufs=1, align_bytes=64)
+  T13 = KP([128, 2048], U8, tag='wlq0_scales', bufs=1, align_bytes=64)
+  Q(T12[:, 0:512], T13[:, 0:512], T67[:].rearrange(S9))
+  T79 = PP([128, 512], F, tag='h_3', bufs=1)
+  M(T79[:], T61, T62, 384, T17, T18, 1, 1)
+  T75 = AQ.tile([128, 4, 512], F, tag='f8_1', bufs=1)
+  AC(T75[:, 0, :], T76[:], ACT.Exp)
+  T72 = PP([128, 256, 4], B, tag='l_0', bufs=1)
+  MT(T72[:, 0:128, :], lhsT=T3[:], rhs=T70[:, :, 0:128].rearrange(S13), start=True, stop=True)
+  T82 = AQ.tile([128, 4, 4, 256], U8, tag='wl_raw_0', bufs=1)
+  DM(out=T82[:, 0, :, :], in_=wl_bytes[1536:2048, :].rearrange(S4, t=4, v=4, h=2)[:, 0, :, 0, :])
+  T74 = AQ.tile([128, 512, 4], B, tag='eg', bufs=1, align_bytes=64)
+  ST(out=T74[:], in0=T54[:].rearrange(S14), scalar=-1.0, in1=T6[:, 0:1, :].broadcast_to([128, 512, 4]), op0=ALU.add, op1=ALU.mult)
+  DM(out=T82[:, 1, :, :], in_=wl_bytes[1536:2048, :].rearrange(S4, t=4, v=4, h=2)[:, 1, :, 0, :])
+  DM(out=T82[:, 2, :, :], in_=wl_bytes[1536:2048, :].rearrange(S4, t=4, v=4, h=2)[:, 2, :, 0, :])
+  DM(out=T82[:, 3, :, :], in_=wl_bytes[1536:2048, :].rearrange(S4, t=4, v=4, h=2)[:, 3, :, 0, :])
+  MT(T72[:, 128:256, :], lhsT=T3[:], rhs=T70[:, :, 128:256].rearrange(S13), start=True, stop=True)
+  AC(T75[:, 1, :], T77[:], ACT.Exp)
+  T73 = PP([128, 256, 4], B, tag='l_1', bufs=1)
+  MT(T73[:, 0:128, :], lhsT=T3[:], rhs=T70[:, :, 256:384].rearrange(S13), start=True, stop=True)
+  MT(T73[:, 128:256, :], lhsT=T3[:], rhs=T70[:, :, 384:512].rearrange(S13), start=True, stop=True)
+  T71 = AQ.tile([128, 512, 4], B, tag='grouped_1', bufs=1, align_bytes=64)
+  SC(T71[:, 0:256, :], T72[:])
+  SC(T71[:, 256:512, :], T73[:])
+  T88 = PP([128, 2, 256], F, tag='l_0', bufs=1)
+  TR(T88[:, 0, 0:128], T25[:].bitcast(F)[:, 2, 0::2], T0[:])
+  TR(T88[:, 0, 128:256], T25[:].bitcast(F)[:, 3, 0::2], T0[:])
+  TR(T88[:, 1, 0:128], T25[:].bitcast(F)[:, 2, 1::2], T0[:])
+  TR(T88[:, 1, 128:256], T25[:].bitcast(F)[:, 3, 1::2], T0[:])
+  AC(T75[:, 2, :], T78[:], ACT.Exp)
+  Q(T12[:, 512:1024], T13[:, 512:1024], T71[:].rearrange(S9))
+  AC(T75[:, 3, :], T79[:], ACT.Exp)
+  T10 = KP([128, 512], U, tag='eq0_codes', bufs=1, align_bytes=64)
+  T11 = KP([128, 512], U8, tag='eq0_scales', bufs=1, align_bytes=64)
+  Q(T10[:, 0:512], T11[:, 0:512], T74[:].rearrange(S9))
+  T80 = AQ.tile([128, 4, 512], B, tag='wl_wide_0', bufs=1)
+  AC(T80[:, 0, :], T46[:].rearrange(S8)[:, 0, 0:512].bitcast(E4), ACT.Copy, scale=T2[:, 1, 0:1])
+  T85 = AQ.tile([128, 512, 4], B, tag='w1g', bufs=1, align_bytes=64)
+  ve.tensor_copy(out=T85[:].rearrange(S6, t=4), in_=T59[:].rearrange(S7, t=4))
+  AC(T80[:, 1, :], T46[:].rearrange(S8)[:, 1, 0:512].bitcast(E4), ACT.Copy, scale=T2[:, 1, 1:2])
+  AC(T80[:, 2, :], T46[:].rearrange(S8)[:, 2, 0:512].bitcast(E4), ACT.Copy, scale=T2[:, 1, 2:3])
+  ve.tensor_scalar(out=T75[:], in0=T75[:], scalar1=1.0, scalar2=None, op0=ALU.min)
+  AC(T80[:, 3, :], T46[:].rearrange(S8)[:, 3, 0:512].bitcast(E4), ACT.Copy, scale=T2[:, 1, 3:4])
+  T86 = AQ.tile([128, 512, 4], B, tag='xg', bufs=1, align_bytes=64)
+  SC(T86[:].rearrange(S10).bitcast(F).rearrange(S11, u=2)[:, 0:256, :], T87[:].rearrange(S12))
+  T90 = PP([128, 256, 4], B, tag='l_1', bufs=1)
+  MT(T90[:, 0:128, :], lhsT=T3[:], rhs=T80[:, :, 0:128].rearrange(S13), start=True, stop=True)
+  T83 = AQ.tile([128, 512], U, tag='w1q_codes_0', bufs=1, align_bytes=64)
+  T84 = AQ.tile([128, 512], U8, tag='w1q_scales_0', bufs=1, align_bytes=64)
+  Q(T83[:, 0:512], T84[:, 0:512], T85[:].rearrange(S9))
+  MT(T90[:, 128:256, :], lhsT=T3[:], rhs=T80[:, :, 128:256].rearrange(S13), start=True, stop=True)
+  SC(T86[:].rearrange(S10).bitcast(F).rearrange(S11, u=2)[:, 256:512, :], T88[:].rearrange(S12))
+  T91 = PP([128, 256, 4], B, tag='l_2', bufs=1)
+  MT(T91[:, 0:128, :], lhsT=T3[:], rhs=T80[:, :, 256:384].rearrange(S13), start=True, stop=True)
+  ST(out=T75[:, 0, :], in0=T76[:], scalar=1.0, in1=T75[:, 0, :], op0=ALU.add, op1=ALU.max)
+  MT(T91[:, 128:256, :], lhsT=T3[:], rhs=T80[:, :, 384:512].rearrange(S13), start=True, stop=True)
+  T89 = AQ.tile([128, 512, 4], B, tag='grouped_2', bufs=1, align_bytes=64)
+  SC(T89[:, 0:256, :], T90[:])
+  ST(out=T75[:, 1, :], in0=T77[:], scalar=1.0, in1=T75[:, 1, :], op0=ALU.add, op1=ALU.max)
+  SC(T89[:, 256:512, :], T91[:])
+  ST(out=T75[:, 2, :], in0=T78[:], scalar=1.0, in1=T75[:, 2, :], op0=ALU.add, op1=ALU.max)
+  T92 = AQ.tile([128, 4, 512], B, tag='wl_wide_1', bufs=1)
+  AC(T92[:, 0, :], T46[:].rearrange(S8)[:, 0, 512:1024].bitcast(E4), ACT.Copy, scale=T2[:, 1, 0:1])
+  T108 = PP([128, 2, 256], F, tag='l_2', bufs=1)
+  TR(T108[:, 0, 0:128], T34[:].bitcast(F)[:, 0, 0::2], T0[:])
+  TR(T108[:, 0, 128:256], T34[:].bitcast(F)[:, 1, 0::2], T0[:])
+  ST(out=T75[:, 3, :], in0=T79[:], scalar=1.0, in1=T75[:, 3, :], op0=ALU.add, op1=ALU.max)
+  TR(T108[:, 1, 0:128], T34[:].bitcast(F)[:, 0, 1::2], T0[:])
+  AC(T92[:, 1, :], T46[:].rearrange(S8)[:, 1, 512:1024].bitcast(E4), ACT.Copy, scale=T2[:, 1, 1:2])
+  TR(T108[:, 1, 128:256], T34[:].bitcast(F)[:, 1, 1::2], T0[:])
+  T26 = KP([128, 512], U, tag='xq2_codes', bufs=1, align_bytes=64)
+  T27 = KP([128, 512], U8, tag='xq2_scales', bufs=1, align_bytes=64)
+  Q(T26[:, 0:512], T27[:, 0:512], T86[:].rearrange(S9))
+  AC(T92[:, 2, :], T46[:].rearrange(S8)[:, 2, 512:1024].bitcast(E4), ACT.Copy, scale=T2[:, 1, 2:3])
+  T96 = AQ.tile([128, 512, 4], B, tag='eg', bufs=1, align_bytes=64)
+  ST(out=T96[:], in0=T75[:].rearrange(S14), scalar=-1.0, in1=T6[:, 1:2, :].broadcast_to([128, 512, 4]), op0=ALU.add, op1=ALU.mult)
+  AC(T92[:, 3, :], T46[:].rearrange(S8)[:, 3, 512:1024].bitcast(E4), ACT.Copy, scale=T2[:, 1, 3:4])
+  T98 = PP([128, 512], F, tag='h_0', bufs=1)
+  M(T98[:], T83, T84, 0, T26, T27, 1, 1)
+  T99 = PP([128, 512], F, tag='h_1', bufs=1)
+  M(T99[:], T83, T84, 128, T26, T27, 1, 1)
+  T102 = AQ.tile([128, 4, 512], B, tag='wl_wide_0', bufs=1)
+  AC(T102[:, 0, :], T60[:].rearrange(S8)[:, 0, 0:512].bitcast(E4), ACT.Copy, scale=T2[:, 2, 0:1])
+  T100 = PP([128, 512], F, tag='h_2', bufs=1)
+  M(T100[:], T83, T84, 256, T26, T27, 1, 1)
+  T103 = AQ.tile([128, 4, 4, 256], U8, tag='wl_raw_1', bufs=1)
+  DM(out=T103[:, 0, :, :], in_=wl_bytes[0:512, :].rearrange(S4, t=4, v=4, h=2)[:, 0, :, 1, :])
+  DM(out=T103[:, 1, :, :], in_=wl_bytes[0:512, :].rearrange(S4, t=4, v=4, h=2)[:, 1, :, 1, :])
+  DM(out=T103[:, 2, :, :], in_=wl_bytes[0:512, :].rearrange(S4, t=4, v=4, h=2)[:, 2, :, 1, :])
+  DM(out=T103[:, 3, :, :], in_=wl_bytes[0:512, :].rearrange(S4, t=4, v=4, h=2)[:, 3, :, 1, :])
+  T94 = PP([128, 256, 4], B, tag='l_0', bufs=1)
+  MT(T94[:, 0:128, :], lhsT=T3[:], rhs=T92[:, :, 0:128].rearrange(S13), start=True, stop=True)
+  T97 = AQ.tile([128, 4, 512], F, tag='f8_2', bufs=1)
+  AC(T97[:, 0, :], T98[:], ACT.Exp)
+  MT(T94[:, 128:256, :], lhsT=T3[:], rhs=T92[:, :, 128:256].rearrange(S13), start=True, stop=True)
+  T95 = PP([128, 256, 4], B, tag='l_1', bufs=1)
+  MT(T95[:, 0:128, :], lhsT=T3[:], rhs=T92[:, :, 256:384].rearrange(S13), start=True, stop=True)
+  T93 = AQ.tile([128, 512, 4], B, tag='grouped_0', bufs=1, align_bytes=64)
+  SC(T93[:, 0:256, :], T94[:])
+  MT(T95[:, 128:256, :], lhsT=T3[:], rhs=T92[:, :, 384:512].rearrange(S13), start=True, stop=True)
+  T101 = PP([128, 512], F, tag='h_3', bufs=1)
+  M(T101[:], T83, T84, 384, T26, T27, 1, 1)
+  T21 = KP([128, 2048], U, tag='wlq1_codes', bufs=1, align_bytes=64)
+  T22 = KP([128, 2048], U8, tag='wlq1_scales', bufs=1, align_bytes=64)
+  Q(T21[:, 0:512], T22[:, 0:512], T89[:].rearrange(S9))
+  SC(T93[:, 256:512, :], T95[:])
+  T109 = PP([128, 2, 256], F, tag='l_0', bufs=1)
+  TR(T109[:, 0, 0:128], T34[:].bitcast(F)[:, 2, 0::2], T0[:])
+  TR(T109[:, 0, 128:256], T34[:].bitcast(F)[:, 3, 0::2], T0[:])
+  TR(T109[:, 1, 0:128], T34[:].bitcast(F)[:, 2, 1::2], T0[:])
+  T19 = KP([128, 512], U, tag='eq1_codes', bufs=1, align_bytes=64)
+  T20 = KP([128, 512], U8, tag='eq1_scales', bufs=1, align_bytes=64)
+  Q(T19[:, 0:512], T20[:, 0:512], T96[:].rearrange(S9))
+  TR(T109[:, 1, 128:256], T34[:].bitcast(F)[:, 3, 1::2], T0[:])
+  AC(T97[:, 1, :], T99[:], ACT.Exp)
+  Q(T21[:, 512:1024], T22[:, 512:1024], T93[:].rearrange(S9))
+  AC(T97[:, 2, :], T100[:], ACT.Exp)
+  T106 = AQ.tile([128, 512, 4], B, tag='w1g', bufs=1, align_bytes=64)
+  ve.tensor_copy(out=T106[:].rearrange(S6, t=4), in_=T81[:].rearrange(S7, t=4))
+  AC(T97[:, 3, :], T101[:], ACT.Exp)
+  AC(T102[:, 1, :], T60[:].rearrange(S8)[:, 1, 0:512].bitcast(E4), ACT.Copy, scale=T2[:, 2, 1:2])
+  AC(T102[:, 2, :], T60[:].rearrange(S8)[:, 2, 0:512].bitcast(E4), ACT.Copy, scale=T2[:, 2, 2:3])
+  ve.tensor_scalar(out=T97[:], in0=T97[:], scalar1=1.0, scalar2=None, op0=ALU.min)
+  AC(T102[:, 3, :], T60[:].rearrange(S8)[:, 3, 0:512].bitcast(E4), ACT.Copy, scale=T2[:, 2, 3:4])
+  T107 = AQ.tile([128, 512, 4], B, tag='xg', bufs=1, align_bytes=64)
+  SC(T107[:].rearrange(S10).bitcast(F).rearrange(S11, u=2)[:, 0:256, :], T108[:].rearrange(S12))
+  T111 = PP([128, 256, 4], B, tag='l_1', bufs=1)
+  MT(T111[:, 0:128, :], lhsT=T3[:], rhs=T102[:, :, 0:128].rearrange(S13), start=True, stop=True)
+  T104 = AQ.tile([128, 512], U, tag='w1q_codes_1', bufs=1, align_bytes=64)
+  T105 = AQ.tile([128, 512], U8, tag='w1q_scales_1', bufs=1, align_bytes=64)
+  Q(T104[:, 0:512], T105[:, 0:512], T106[:].rearrange(S9))
+  MT(T111[:, 128:256, :], lhsT=T3[:], rhs=T102[:, :, 128:256].rearrange(S13), start=True, stop=True)
+  SC(T107[:].rearrange(S10).bitcast(F).rearrange(S11, u=2)[:, 256:512, :], T109[:].rearrange(S12))
+  ST(out=T97[:, 0, :], in0=T98[:], scalar=1.0, in1=T97[:, 0, :], op0=ALU.add, op1=ALU.max)
+  T112 = PP([128, 256, 4], B, tag='l_2', bufs=1)
+  MT(T112[:, 0:128, :], lhsT=T3[:], rhs=T102[:, :, 256:384].rearrange(S13), start=True, stop=True)
+  MT(T112[:, 128:256, :], lhsT=T3[:], rhs=T102[:, :, 384:512].rearrange(S13), start=True, stop=True)
+  T110 = AQ.tile([128, 512, 4], B, tag='grouped_1', bufs=1, align_bytes=64)
+  SC(T110[:, 0:256, :], T111[:])
+  ST(out=T97[:, 1, :], in0=T99[:], scalar=1.0, in1=T97[:, 1, :], op0=ALU.add, op1=ALU.max)
+  SC(T110[:, 256:512, :], T112[:])
+  ST(out=T97[:, 2, :], in0=T100[:], scalar=1.0, in1=T97[:, 2, :], op0=ALU.add, op1=ALU.max)
+  T113 = AQ.tile([128, 4, 512], B, tag='wl_wide_1', bufs=1)
+  AC(T113[:, 0, :], T60[:].rearrange(S8)[:, 0, 512:1024].bitcast(E4), ACT.Copy, scale=T2[:, 2, 0:1])
+  ST(out=T97[:, 3, :], in0=T101[:], scalar=1.0, in1=T97[:, 3, :], op0=ALU.add, op1=ALU.max)
+  AC(T113[:, 1, :], T60[:].rearrange(S8)[:, 1, 512:1024].bitcast(E4), ACT.Copy, scale=T2[:, 2, 1:2])
+  T35 = KP([128, 512], U, tag='xq3_codes', bufs=1, align_bytes=64)
+  T36 = KP([128, 512], U8, tag='xq3_scales', bufs=1, align_bytes=64)
+  Q(T35[:, 0:512], T36[:, 0:512], T107[:].rearrange(S9))
+  AC(T113[:, 2, :], T60[:].rearrange(S8)[:, 2, 512:1024].bitcast(E4), ACT.Copy, scale=T2[:, 2, 2:3])
+  T117 = AQ.tile([128, 512, 4], B, tag='eg', bufs=1, align_bytes=64)
+  ST(out=T117[:], in0=T97[:].rearrange(S14), scalar=-1.0, in1=T6[:, 2:3, :].broadcast_to([128, 512, 4]), op0=ALU.add, op1=ALU.mult)
+  T119 = PP([128, 512], F, tag='h_0', bufs=1)
+  M(T119[:], T104, T105, 0, T35, T36, 1, 1)
+  AC(T113[:, 3, :], T60[:].rearrange(S8)[:, 3, 512:1024].bitcast(E4), ACT.Copy, scale=T2[:, 2, 3:4])
+  T120 = PP([128, 512], F, tag='h_1', bufs=1)
+  M(T120[:], T104, T105, 128, T35, T36, 1, 1)
+  T121 = PP([128, 512], F, tag='h_2', bufs=1)
+  M(T121[:], T104, T105, 256, T35, T36, 1, 1)
+  T118 = AQ.tile([128, 4, 512], F, tag='f8_3', bufs=1)
+  AC(T118[:, 0, :], T119[:], ACT.Exp)
+  T124 = AQ.tile([128, 4, 4, 256], U8, tag='wl_raw_2', bufs=1)
+  DM(out=T124[:, 0, :, :], in_=wl_bytes[512:1024, :].rearrange(S4, t=4, v=4, h=2)[:, 0, :, 1, :])
+  T115 = PP([128, 256, 4], B, tag='l_0', bufs=1)
+  MT(T115[:, 0:128, :], lhsT=T3[:], rhs=T113[:, :, 0:128].rearrange(S13), start=True, stop=True)
+  DM(out=T124[:, 1, :, :], in_=wl_bytes[512:1024, :].rearrange(S4, t=4, v=4, h=2)[:, 1, :, 1, :])
+  DM(out=T124[:, 2, :, :], in_=wl_bytes[512:1024, :].rearrange(S4, t=4, v=4, h=2)[:, 2, :, 1, :])
+  DM(out=T124[:, 3, :, :], in_=wl_bytes[512:1024, :].rearrange(S4, t=4, v=4, h=2)[:, 3, :, 1, :])
+  MT(T115[:, 128:256, :], lhsT=T3[:], rhs=T113[:, :, 128:256].rearrange(S13), start=True, stop=True)
+  AC(T118[:, 1, :], T120[:], ACT.Exp)
+  T116 = PP([128, 256, 4], B, tag='l_1', bufs=1)
+  MT(T116[:, 0:128, :], lhsT=T3[:], rhs=T113[:, :, 256:384].rearrange(S13), start=True, stop=True)
+  MT(T116[:, 128:256, :], lhsT=T3[:], rhs=T113[:, :, 384:512].rearrange(S13), start=True, stop=True)
+  T114 = AQ.tile([128, 512, 4], B, tag='grouped_2', bufs=1, align_bytes=64)
+  SC(T114[:, 0:256, :], T115[:])
+  T122 = PP([128, 512], F, tag='h_3', bufs=1)
+  M(T122[:], T104, T105, 384, T35, T36, 1, 1)
+  T30 = KP([128, 2048], U, tag='wlq2_codes', bufs=1, align_bytes=64)
+  T31 = KP([128, 2048], U8, tag='wlq2_scales', bufs=1, align_bytes=64)
+  Q(T30[:, 0:512], T31[:, 0:512], T110[:].rearrange(S9))
+  SC(T114[:, 256:512, :], T116[:])
+  T28 = KP([128, 512], U, tag='eq2_codes', bufs=1, align_bytes=64)
+  T29 = KP([128, 512], U8, tag='eq2_scales', bufs=1, align_bytes=64)
+  Q(T28[:, 0:512], T29[:, 0:512], T117[:].rearrange(S9))
+  AC(T118[:, 2, :], T121[:], ACT.Exp)
+  Q(T30[:, 512:1024], T31[:, 512:1024], T114[:].rearrange(S9))
+  AC(T118[:, 3, :], T122[:], ACT.Exp)
+  T134 = KP([128, 16], F, tag='gs2', bufs=1)
+  ve.tensor_scalar(out=T134[:], in0=T133[:, 0:16], scalar1=2.0, scalar2=None, op0=ALU.mult)
+  T188 = PP([128, 2, 512], B, tag='x', bufs=1)
+  TR(T188[:, 0, 0:128], T7[:, 0, 0:128], T3[:])
+  T123 = AQ.tile([128, 4, 512], B, tag='wl_wide_0', bufs=1)
+  AC(T123[:, 0, :], T82[:].rearrange(S8)[:, 0, 0:512].bitcast(E4), ACT.Copy, scale=T2[:, 3, 0:1])
+  ve.tensor_scalar(out=T118[:], in0=T118[:], scalar1=1.0, scalar2=None, op0=ALU.min)
+  TR(T188[:, 0, 128:256], T7[:, 1, 0:128], T3[:])
+  TR(T188[:, 0, 256:384], T7[:, 2, 0:128], T3[:])
+  TR(T188[:, 0, 384:512], T7[:, 3, 0:128], T3[:])
+  TR(T188[:, 1, 0:128], T7[:, 0, 128:256], T3[:])
+  TR(T188[:, 1, 128:256], T7[:, 1, 128:256], T3[:])
+  TR(T188[:, 1, 256:384], T7[:, 2, 128:256], T3[:])
+  TR(T188[:, 1, 384:512], T7[:, 3, 128:256], T3[:])
+  AC(T123[:, 1, :], T82[:].rearrange(S8)[:, 1, 0:512].bitcast(E4), ACT.Copy, scale=T2[:, 3, 1:2])
+  AC(T123[:, 2, :], T82[:].rearrange(S8)[:, 2, 0:512].bitcast(E4), ACT.Copy, scale=T2[:, 3, 2:3])
+  ST(out=T118[:, 0, :], in0=T119[:], scalar=1.0, in1=T118[:, 0, :], op0=ALU.add, op1=ALU.max)
+  AC(T123[:, 3, :], T82[:].rearrange(S8)[:, 3, 0:512].bitcast(E4), ACT.Copy, scale=T2[:, 3, 3:4])
+  ST(out=T118[:, 1, :], in0=T120[:], scalar=1.0, in1=T118[:, 1, :], op0=ALU.add, op1=ALU.max)
+  T128 = AQ.tile([128, 4, 512], B, tag='wl_wide_1', bufs=1)
+  AC(T128[:, 0, :], T82[:].rearrange(S8)[:, 0, 512:1024].bitcast(E4), ACT.Copy, scale=T2[:, 3, 0:1])
+  T126 = PP([128, 256, 4], B, tag='l_2', bufs=1)
+  MT(T126[:, 0:128, :], lhsT=T3[:], rhs=T123[:, :, 0:128].rearrange(S13), start=True, stop=True)
+  ST(out=T118[:, 2, :], in0=T121[:], scalar=1.0, in1=T118[:, 2, :], op0=ALU.add, op1=ALU.max)
+  MT(T126[:, 128:256, :], lhsT=T3[:], rhs=T123[:, :, 128:256].rearrange(S13), start=True, stop=True)
+  AC(T128[:, 1, :], T82[:].rearrange(S8)[:, 1, 512:1024].bitcast(E4), ACT.Copy, scale=T2[:, 3, 1:2])
+  T127 = PP([128, 256, 4], B, tag='l_0', bufs=1)
+  MT(T127[:, 0:128, :], lhsT=T3[:], rhs=T123[:, :, 256:384].rearrange(S13), start=True, stop=True)
+  ST(out=T118[:, 3, :], in0=T122[:], scalar=1.0, in1=T118[:, 3, :], op0=ALU.add, op1=ALU.max)
+  MT(T127[:, 128:256, :], lhsT=T3[:], rhs=T123[:, :, 384:512].rearrange(S13), start=True, stop=True)
+  T125 = AQ.tile([128, 512, 4], B, tag='grouped_0', bufs=1, align_bytes=64)
+  SC(T125[:, 0:256, :], T126[:])
+  T132 = AQ.tile([128, 512, 4], B, tag='eg', bufs=1, align_bytes=64)
+  ST(out=T132[:], in0=T118[:].rearrange(S14), scalar=-1.0, in1=T6[:, 3:4, :].broadcast_to([128, 512, 4]), op0=ALU.add, op1=ALU.mult)
+  SC(T125[:, 256:512, :], T127[:])
+  AC(T128[:, 2, :], T82[:].rearrange(S8)[:, 2, 512:1024].bitcast(E4), ACT.Copy, scale=T2[:, 3, 2:3])
+  T144 = PP([128, 512], F, tag='l_0', bufs=1)
+  M(T144[:], T12, T13, 0, T8, T9, 1, 0)
+  M(T144[:], T21, T22, 0, T17, T18, 0, 0)
+  AC(T128[:, 3, :], T82[:].rearrange(S8)[:, 3, 512:1024].bitcast(E4), ACT.Copy, scale=T2[:, 3, 3:4])
+  M(T144[:], T30, T31, 0, T26, T27, 0, 0)
+  T142 = AQ.tile([128, 4, 512], B, tag='wl_wide_0', bufs=1)
+  AC(T142[:, 0, :], T103[:].rearrange(S8)[:, 0, 0:512].bitcast(E4), ACT.Copy, scale=T2[:, 0, 0:1])
+  T130 = PP([128, 256, 4], B, tag='l_1', bufs=1)
+  MT(T130[:, 0:128, :], lhsT=T3[:], rhs=T128[:, :, 0:128].rearrange(S13), start=True, stop=True)
+  T136 = AQ.tile([128, 4, 4, 256], U8, tag='wl_raw_0', bufs=1)
+  DM(out=T136[:, 0, :, :], in_=wl_bytes[1024:1536, :].rearrange(S4, t=4, v=4, h=2)[:, 0, :, 1, :])
+  DM(out=T136[:, 1, :, :], in_=wl_bytes[1024:1536, :].rearrange(S4, t=4, v=4, h=2)[:, 1, :, 1, :])
+  DM(out=T136[:, 2, :, :], in_=wl_bytes[1024:1536, :].rearrange(S4, t=4, v=4, h=2)[:, 2, :, 1, :])
+  DM(out=T136[:, 3, :, :], in_=wl_bytes[1024:1536, :].rearrange(S4, t=4, v=4, h=2)[:, 3, :, 1, :])
+  T39 = KP([128, 2048], U, tag='wlq3_codes', bufs=1, align_bytes=64)
+  T40 = KP([128, 2048], U8, tag='wlq3_scales', bufs=1, align_bytes=64)
+  Q(T39[:, 0:512], T40[:, 0:512], T125[:].rearrange(S9))
+  MT(T130[:, 128:256, :], lhsT=T3[:], rhs=T128[:, :, 128:256].rearrange(S13), start=True, stop=True)
+  AC(T142[:, 1, :], T103[:].rearrange(S8)[:, 1, 0:512].bitcast(E4), ACT.Copy, scale=T2[:, 0, 1:2])
+  T131 = PP([128, 256, 4], B, tag='l_2', bufs=1)
+  MT(T131[:, 0:128, :], lhsT=T3[:], rhs=T128[:, :, 256:384].rearrange(S13), start=True, stop=True)
+  MT(T131[:, 128:256, :], lhsT=T3[:], rhs=T128[:, :, 384:512].rearrange(S13), start=True, stop=True)
+  T37 = KP([128, 512], U, tag='eq3_codes', bufs=1, align_bytes=64)
+  T38 = KP([128, 512], U8, tag='eq3_scales', bufs=1, align_bytes=64)
+  Q(T37[:, 0:512], T38[:, 0:512], T132[:].rearrange(S9))
+  T129 = AQ.tile([128, 512, 4], B, tag='grouped_1', bufs=1, align_bytes=64)
+  SC(T129[:, 0:256, :], T130[:])
+  M(T144[:], T39, T40, 0, T35, T36, 0, 1)
+  SC(T129[:, 256:512, :], T131[:])
+  T145 = PP([128, 512], F, tag='l_1', bufs=1)
+  M(T145[:], T12, T13, 256, T8, T9, 1, 0)
+  M(T145[:], T21, T22, 256, T17, T18, 0, 0)
+  AC(T142[:, 2, :], T103[:].rearrange(S8)[:, 2, 0:512].bitcast(E4), ACT.Copy, scale=T2[:, 0, 2:3])
+  Q(T39[:, 512:1024], T40[:, 512:1024], T129[:].rearrange(S9))
+  M(T145[:], T30, T31, 256, T26, T27, 0, 0)
+  M(T145[:], T39, T40, 256, T35, T36, 0, 1)
+  AC(T142[:, 3, :], T103[:].rearrange(S8)[:, 3, 0:512].bitcast(E4), ACT.Copy, scale=T2[:, 0, 3:4])
+  T146 = PP([128, 512], F, tag='l_2', bufs=1)
+  M(T146[:], T12, T13, 512, T8, T9, 1, 0)
+  M(T146[:], T21, T22, 512, T17, T18, 0, 0)
+  T143 = AQ.tile([128, 512], F, tag='l0_0', bufs=1)
+  SC(T143[:], T144[:])
+  M(T146[:], T30, T31, 512, T26, T27, 0, 0)
+  T150 = AQ.tile([128, 512, 4], B, tag='grouped_2', bufs=1, align_bytes=64)
+  ve.tensor_copy(out=T150[:], in_=T142[:].rearrange(S13))
+  M(T146[:], T39, T40, 512, T35, T36, 0, 1)
+  T148 = AQ.tile([128, 4, 512], B, tag='wl_wide_1', bufs=1)
+  AC(T148[:, 0, :], T103[:].rearrange(S8)[:, 0, 512:1024].bitcast(E4), ACT.Copy, scale=T2[:, 0, 0:1])
+  T147 = PP([128, 512], F, tag='l_0', bufs=1)
+  M(T147[:], T12, T13, 768, T8, T9, 1, 0)
+  M(T147[:], T21, T22, 768, T17, T18, 0, 0)
+  AC(T148[:, 1, :], T103[:].rearrange(S8)[:, 1, 512:1024].bitcast(E4), ACT.Copy, scale=T2[:, 0, 1:2])
+  M(T147[:], T30, T31, 768, T26, T27, 0, 0)
+  T149 = AQ.tile([128, 512], F, tag='top_0', bufs=1)
+  TT(out=T149[:], in0=T145[:], in1=T143[:], op=ALU.max)
+  M(T147[:], T39, T40, 768, T35, T36, 0, 1)
+  AC(T148[:, 2, :], T103[:].rearrange(S8)[:, 2, 512:1024].bitcast(E4), ACT.Copy, scale=T2[:, 0, 2:3])
+  Q(T12[:, 1024:1536], T13[:, 1024:1536], T150[:].rearrange(S9))
+  AC(T148[:, 3, :], T103[:].rearrange(S8)[:, 3, 512:1024].bitcast(E4), ACT.Copy, scale=T2[:, 0, 3:4])
+  TT(out=T149[:], in0=T146[:], in1=T149[:], op=ALU.max)
+  T157 = AQ.tile([128, 4, 512], B, tag='wl_wide_0', bufs=1)
+  AC(T157[:, 0, :], T124[:].rearrange(S8)[:, 0, 0:512].bitcast(E4), ACT.Copy, scale=T2[:, 1, 0:1])
+  T137 = AQ.tile([128, 4, 4, 256], U8, tag='wl_raw_1', bufs=1)
+  DM(out=T137[:, 0, :, :], in_=wl_bytes[1536:2048, :].rearrange(S4, t=4, v=4, h=2)[:, 0, :, 1, :])
+  DM(out=T137[:, 1, :, :], in_=wl_bytes[1536:2048, :].rearrange(S4, t=4, v=4, h=2)[:, 1, :, 1, :])
+  DM(out=T137[:, 2, :, :], in_=wl_bytes[1536:2048, :].rearrange(S4, t=4, v=4, h=2)[:, 2, :, 1, :])
+  DM(out=T137[:, 3, :, :], in_=wl_bytes[1536:2048, :].rearrange(S4, t=4, v=4, h=2)[:, 3, :, 1, :])
+  T158 = AQ.tile([128, 512, 4], B, tag='grouped_0', bufs=1, align_bytes=64)
+  ve.tensor_copy(out=T158[:], in_=T148[:].rearrange(S13))
+  T138 = AQ.tile([128, 4, 512], B, tag='w2_raw_0', bufs=1)
+  DM(out=T138[:], in_=w2[0, :, 0:512].rearrange(S1, j=4))
+  T139 = AQ.tile([128, 4, 512], B, tag='w2_raw_1', bufs=1)
+  DM(out=T139[:], in_=w2[0, :, 512:1024].rearrange(S1, j=4))
+  T140 = AQ.tile([128, 4, 512], B, tag='w2_raw_2', bufs=1)
+  DM(out=T140[:], in_=w2[1, :, 0:512].rearrange(S1, j=4))
+  AC(T157[:, 1, :], T124[:].rearrange(S8)[:, 1, 0:512].bitcast(E4), ACT.Copy, scale=T2[:, 1, 1:2])
+  AC(T157[:, 2, :], T124[:].rearrange(S8)[:, 2, 0:512].bitcast(E4), ACT.Copy, scale=T2[:, 1, 2:3])
+  TT(out=T149[:], in0=T147[:], in1=T149[:], op=ALU.max)
+  AC(T157[:, 3, :], T124[:].rearrange(S8)[:, 3, 0:512].bitcast(E4), ACT.Copy, scale=T2[:, 1, 3:4])
+  Q(T12[:, 1536:2048], T13[:, 1536:2048], T158[:].rearrange(S9))
+  T159 = AQ.tile([128, 4, 512], B, tag='wl_wide_1', bufs=1)
+  AC(T159[:, 0, :], T124[:].rearrange(S8)[:, 0, 512:1024].bitcast(E4), ACT.Copy, scale=T2[:, 1, 0:1])
+  AC(T159[:, 1, :], T124[:].rearrange(S8)[:, 1, 512:1024].bitcast(E4), ACT.Copy, scale=T2[:, 1, 1:2])
+  T151 = AQ.tile([128, 4, 512], F, tag='f8_0', bufs=1)
+  TT(out=T151[:, 1, :], in0=T145[:], in1=T149[:], op=ALU.subtract)
+  AC(T159[:, 2, :], T124[:].rearrange(S8)[:, 2, 512:1024].bitcast(E4), ACT.Copy, scale=T2[:, 1, 2:3])
+  TT(out=T151[:, 2, :], in0=T146[:], in1=T149[:], op=ALU.subtract)
+  T153 = PP([128, 512], F, tag='l_1', bufs=1)
+  M(T153[:], T12, T13, 128, T8, T9, 1, 0)
+  M(T153[:], T21, T22, 128, T17, T18, 0, 0)
+  TT(out=T151[:, 3, :], in0=T147[:], in1=T149[:], op=ALU.subtract)
+  AC(T159[:, 3, :], T124[:].rearrange(S8)[:, 3, 512:1024].bitcast(E4), ACT.Copy, scale=T2[:, 1, 3:4])
+  M(T153[:], T30, T31, 128, T26, T27, 0, 0)
+  M(T153[:], T39, T40, 128, T35, T36, 0, 1)
+  TT(out=T151[:, 0, :], in0=T143[:], in1=T149[:], op=ALU.subtract)
+  T154 = PP([128, 512], F, tag='l_2', bufs=1)
+  M(T154[:], T12, T13, 384, T8, T9, 1, 0)
+  T152 = AQ.tile([128, 512], F, tag='l0_1', bufs=1)
+  SC(T152[:], T153[:])
+  M(T154[:], T21, T22, 384, T17, T18, 0, 0)
+  T160 = AQ.tile([128, 512, 4], B, tag='grouped_1', bufs=1, align_bytes=64)
+  ve.tensor_copy(out=T160[:], in_=T157[:].rearrange(S13))
+  M(T154[:], T30, T31, 384, T26, T27, 0, 0)
+  AC(T151[:], T151[:], ACT.Exp)
+  M(T154[:], T39, T40, 384, T35, T36, 0, 1)
+  T155 = PP([128, 512], F, tag='l_0', bufs=1)
+  M(T155[:], T12, T13, 640, T8, T9, 1, 0)
+  M(T155[:], T21, T22, 640, T17, T18, 0, 0)
+  M(T155[:], T30, T31, 640, T26, T27, 0, 0)
+  T161 = AQ.tile([128, 512], F, tag='top_1', bufs=1)
+  TT(out=T161[:], in0=T154[:], in1=T152[:], op=ALU.max)
+  M(T155[:], T39, T40, 640, T35, T36, 0, 1)
+  T156 = PP([128, 512], F, tag='l_1', bufs=1)
+  M(T156[:], T12, T13, 896, T8, T9, 1, 0)
+  T164 = AQ.tile([128, 512, 4], B, tag='grouped_2', bufs=1, align_bytes=64)
+  ve.tensor_copy(out=T164[:], in_=T159[:].rearrange(S13))
+  M(T156[:], T21, T22, 896, T17, T18, 0, 0)
+  M(T156[:], T30, T31, 896, T26, T27, 0, 0)
+  T163 = AQ.tile([128, 4, 512], B, tag='wl_wide_0', bufs=1)
+  AC(T163[:, 0, :], T136[:].rearrange(S8)[:, 0, 0:512].bitcast(E4), ACT.Copy, scale=T2[:, 2, 0:1])
+  T135 = KP([128, 4, 512], F, tag='den', bufs=1)
+  nc.gpsimd.tensor_tensor(out=T135[:, 0, :], in0=T151[:, 0, :], in1=T151[:, 1, :], op=ALU.add)
+  M(T156[:], T39, T40, 896, T35, T36, 0, 1)
+  AC(T163[:, 1, :], T136[:].rearrange(S8)[:, 1, 0:512].bitcast(E4), ACT.Copy, scale=T2[:, 2, 1:2])
+  TT(out=T161[:], in0=T155[:], in1=T161[:], op=ALU.max)
+  AC(T163[:, 2, :], T136[:].rearrange(S8)[:, 2, 0:512].bitcast(E4), ACT.Copy, scale=T2[:, 2, 2:3])
+  Q(T21[:, 1024:1536], T22[:, 1024:1536], T160[:].rearrange(S9))
+  nc.gpsimd.tensor_tensor(out=T135[:, 0, :], in0=T135[:, 0, :], in1=T151[:, 2, :], op=ALU.add)
+  AC(T163[:, 3, :], T136[:].rearrange(S8)[:, 3, 0:512].bitcast(E4), ACT.Copy, scale=T2[:, 2, 3:4])
+  TT(out=T161[:], in0=T156[:], in1=T161[:], op=ALU.max)
+  T165 = AQ.tile([128, 4, 512], B, tag='wl_wide_1', bufs=1)
+  AC(T165[:, 0, :], T136[:].rearrange(S8)[:, 0, 512:1024].bitcast(E4), ACT.Copy, scale=T2[:, 2, 0:1])
+  T166 = AQ.tile([128, 512, 4], B, tag='grouped_0', bufs=1, align_bytes=64)
+  ve.tensor_copy(out=T166[:], in_=T163[:].rearrange(S13))
+  nc.gpsimd.tensor_tensor(out=T135[:, 0, :], in0=T135[:, 0, :], in1=T151[:, 3, :], op=ALU.add)
+  AC(T165[:, 1, :], T136[:].rearrange(S8)[:, 1, 512:1024].bitcast(E4), ACT.Copy, scale=T2[:, 2, 1:2])
+  AC(T165[:, 2, :], T136[:].rearrange(S8)[:, 2, 512:1024].bitcast(E4), ACT.Copy, scale=T2[:, 2, 2:3])
+  T162 = AQ.tile([128, 4, 512], F, tag='f8_1', bufs=1)
+  TT(out=T162[:, 1, :], in0=T154[:], in1=T161[:], op=ALU.subtract)
+  AC(T165[:, 3, :], T136[:].rearrange(S8)[:, 3, 512:1024].bitcast(E4), ACT.Copy, scale=T2[:, 2, 3:4])
+  TT(out=T162[:, 2, :], in0=T155[:], in1=T161[:], op=ALU.subtract)
+  T174 = PP([128, 256, 4], B, tag='l_2', bufs=1)
+  MT(T174[:, 0:128, :], lhsT=T3[:], rhs=T139[:, :, 0:128].rearrange(S13), start=True, stop=True)
+  T167 = AQ.tile([128, 4, 512], B, tag='wl_wide_0', bufs=1)
+  AC(T167[:, 0, :], T137[:].rearrange(S8)[:, 0, 0:512].bitcast(E4), ACT.Copy, scale=T2[:, 3, 0:1])
+  MT(T174[:, 128:256, :], lhsT=T3[:], rhs=T139[:, :, 128:256].rearrange(S13), start=True, stop=True)
+  TT(out=T162[:, 3, :], in0=T156[:], in1=T161[:], op=ALU.subtract)
+  T175 = PP([128, 256, 4], B, tag='l_0', bufs=1)
+  MT(T175[:, 0:128, :], lhsT=T3[:], rhs=T139[:, :, 256:384].rearrange(S13), start=True, stop=True)
+  AC(T167[:, 1, :], T137[:].rearrange(S8)[:, 1, 0:512].bitcast(E4), ACT.Copy, scale=T2[:, 3, 1:2])
+  MT(T175[:, 128:256, :], lhsT=T3[:], rhs=T139[:, :, 384:512].rearrange(S13), start=True, stop=True)
+  TT(out=T162[:, 0, :], in0=T152[:], in1=T161[:], op=ALU.subtract)
+  T177 = PP([128, 512], F, tag='l_1', bufs=1)
+  M(T177[:], T12, T13, 1024, T8, T9, 1, 0)
+  AC(T167[:, 2, :], T137[:].rearrange(S8)[:, 2, 0:512].bitcast(E4), ACT.Copy, scale=T2[:, 3, 2:3])
+  M(T177[:], T21, T22, 1024, T17, T18, 0, 0)
+  Q(T21[:, 1536:2048], T22[:, 1536:2048], T164[:].rearrange(S9))
+  AC(T162[:], T162[:], ACT.Exp)
+  T168 = AQ.tile([128, 512, 4], B, tag='grouped_1', bufs=1, align_bytes=64)
+  ve.tensor_copy(out=T168[:], in_=T165[:].rearrange(S13))
+  Q(T30[:, 1024:1536], T31[:, 1024:1536], T166[:].rearrange(S9))
+  AC(T167[:, 3, :], T137[:].rearrange(S8)[:, 3, 0:512].bitcast(E4), ACT.Copy, scale=T2[:, 3, 3:4])
+  nc.gpsimd.tensor_tensor(out=T135[:, 1, :], in0=T162[:, 0, :], in1=T162[:, 1, :], op=ALU.add)
+  Q(T30[:, 1536:2048], T31[:, 1536:2048], T168[:].rearrange(S9))
+  M(T177[:], T30, T31, 1024, T26, T27, 0, 0)
+  T169 = AQ.tile([128, 4, 512], B, tag='wl_wide_1', bufs=1)
+  AC(T169[:, 0, :], T137[:].rearrange(S8)[:, 0, 512:1024].bitcast(E4), ACT.Copy, scale=T2[:, 3, 0:1])
+  T170 = AQ.tile([128, 512, 4], B, tag='grouped_2', bufs=1, align_bytes=64)
+  ve.tensor_copy(out=T170[:], in_=T167[:].rearrange(S13))
+  AC(T169[:, 1, :], T137[:].rearrange(S8)[:, 1, 512:1024].bitcast(E4), ACT.Copy, scale=T2[:, 3, 1:2])
+  nc.gpsimd.tensor_tensor(out=T135[:, 1, :], in0=T135[:, 1, :], in1=T162[:, 2, :], op=ALU.add)
+  AC(T169[:, 2, :], T137[:].rearrange(S8)[:, 2, 512:1024].bitcast(E4), ACT.Copy, scale=T2[:, 3, 2:3])
+  Q(T39[:, 1024:1536], T40[:, 1024:1536], T170[:].rearrange(S9))
+  AC(T169[:, 3, :], T137[:].rearrange(S8)[:, 3, 512:1024].bitcast(E4), ACT.Copy, scale=T2[:, 3, 3:4])
+  nc.gpsimd.tensor_tensor(out=T135[:, 1, :], in0=T135[:, 1, :], in1=T162[:, 3, :], op=ALU.add)
+  T171 = AQ.tile([128, 512, 4], B, tag='grouped_0', bufs=1, align_bytes=64)
+  SC(T171[:], T138[:].rearrange(S13))
+  T172 = AQ.tile([128, 512, 4], B, tag='grouped_1', bufs=1, align_bytes=64)
+  ve.tensor_copy(out=T172[:], in_=T169[:].rearrange(S13))
+  M(T177[:], T39, T40, 1024, T35, T36, 0, 1)
+  Q(T39[:, 1536:2048], T40[:, 1536:2048], T172[:].rearrange(S9))
+  T173 = AQ.tile([128, 512, 4], B, tag='grouped_2', bufs=1, align_bytes=64)
+  SC(T173[:, 0:256, :], T174[:])
+  T141 = AQ.tile([128, 4, 512], B, tag='w2_raw_0', bufs=1)
+  DM(out=T141[:], in_=w2[1, :, 512:1024].rearrange(S1, j=4))
+  T14 = KP([128, 1024], U, tag='w2q0_codes', bufs=1, align_bytes=64)
+  T15 = KP([128, 1024], U8, tag='w2q0_scales', bufs=1, align_bytes=64)
+  Q(T14[:, 0:512], T15[:, 0:512], T171[:].rearrange(S9))
+  T211 = AQ.tile([128, 4, 512], B, tag='w2_raw_1', bufs=1)
+  DM(out=T211[:], in_=w2[2, :, 0:512].rearrange(S1, j=4))
+  SC(T173[:, 256:512, :], T175[:])
+  T178 = PP([128, 512], F, tag='l_2', bufs=1)
+  M(T178[:], T12, T13, 1280, T8, T9, 1, 0)
+  M(T178[:], T21, T22, 1280, T17, T18, 0, 0)
+  T176 = AQ.tile([128, 512], F, tag='l0_0', bufs=1)
+  SC(T176[:], T177[:])
+  Q(T14[:, 512:1024], T15[:, 512:1024], T173[:].rearrange(S9))
+  M(T178[:], T30, T31, 1280, T26, T27, 0, 0)
+  M(T178[:], T39, T40, 1280, T35, T36, 0, 1)
+  T196 = AQ.tile([128, 512, 4], B, tag='grouped_0', bufs=1, align_bytes=64)
+  SC(T196[:], T140[:].rearrange(S13))
+  T179 = PP([128, 512], F, tag='l_0', bufs=1)
+  M(T179[:], T12, T13, 1536, T8, T9, 1, 0)
+  T181 = AQ.tile([128, 512], F, tag='top_0', bufs=1)
+  TT(out=T181[:], in0=T178[:], in1=T176[:], op=ALU.max)
+  M(T179[:], T21, T22, 1536, T17, T18, 0, 0)
+  M(T179[:], T30, T31, 1536, T26, T27, 0, 0)
+  M(T179[:], T39, T40, 1536, T35, T36, 0, 1)
+  T180 = PP([128, 512], F, tag='l_1', bufs=1)
+  M(T180[:], T12, T13, 1792, T8, T9, 1, 0)
+  TT(out=T181[:], in0=T179[:], in1=T181[:], op=ALU.max)
+  M(T180[:], T21, T22, 1792, T17, T18, 0, 0)
+  M(T180[:], T30, T31, 1792, T26, T27, 0, 0)
+  M(T180[:], T39, T40, 1792, T35, T36, 0, 1)
+  T189 = PP([128, 512], F, tag='h_0', bufs=1)
+  M(T189[:], T14, T15, 512, T10, T11, 1, 1)
+  TT(out=T181[:], in0=T180[:], in1=T181[:], op=ALU.max)
+  T212 = AQ.tile([128, 4, 512], B, tag='w2_raw_2', bufs=1)
+  DM(out=T212[:], in_=w2[2, :, 512:1024].rearrange(S1, j=4))
+  T190 = PP([128, 512], F, tag='h_1', bufs=1)
+  M(T190[:], T14, T15, 0, T10, T11, 1, 1)
+  T191 = AQ.tile([128, 512], F, tag='th_0', bufs=1)
+  AC(T191[:], T189[:], ACT.Tanh, scale=0.5)
+  T193 = PP([128, 512], F, tag='h_2', bufs=1)
+  M(T193[:], T14, T15, 640, T10, T11, 1, 1)
+  T23 = KP([128, 1024], U, tag='w2q1_codes', bufs=1, align_bytes=64)
+  T24 = KP([128, 1024], U8, tag='w2q1_scales', bufs=1, align_bytes=64)
+  Q(T23[:, 0:512], T24[:, 0:512], T196[:].rearrange(S9))
+  T194 = PP([128, 512], F, tag='h_3', bufs=1)
+  M(T194[:], T14, T15, 128, T10, T11, 1, 1)
+  T222 = AQ.tile([128, 512, 4], B, tag='grouped_2', bufs=1, align_bytes=64)
+  SC(T222[:], T211[:].rearrange(S13))
+  T200 = PP([128, 512], F, tag='h_0', bufs=1)
+  M(T200[:], T14, T15, 768, T10, T11, 1, 1)
+  T182 = AQ.tile([128, 4, 512], F, tag='f8_2', bufs=1)
+  TT(out=T182[:, 1, :], in0=T178[:], in1=T181[:], op=ALU.subtract)
+  TT(out=T182[:, 2, :], in0=T179[:], in1=T181[:], op=ALU.subtract)
+  T184 = PP([128, 512], F, tag='l_2', bufs=1)
+  M(T184[:], T12, T13, 1152, T8, T9, 1, 0)
+  M(T184[:], T21, T22, 1152, T17, T18, 0, 0)
+  TT(out=T182[:, 3, :], in0=T180[:], in1=T181[:], op=ALU.subtract)
+  M(T184[:], T30, T31, 1152, T26, T27, 0, 0)
+  M(T184[:], T39, T40, 1152, T35, T36, 0, 1)
+  TT(out=T182[:, 0, :], in0=T176[:], in1=T181[:], op=ALU.subtract)
+  T185 = PP([128, 512], F, tag='l_0', bufs=1)
+  M(T185[:], T12, T13, 1408, T8, T9, 1, 0)
+  M(T185[:], T21, T22, 1408, T17, T18, 0, 0)
+  T192 = AQ.tile([128, 512], F, tag='r_0', bufs=1)
+  ST(out=T192[:], in0=T191[:], scalar=1.0, in1=T190[:], op0=ALU.add, op1=ALU.mult)
+  T183 = AQ.tile([128, 512], F, tag='l0_1', bufs=1)
+  SC(T183[:], T184[:])
+  M(T185[:], T30, T31, 1408, T26, T27, 0, 0)
+  M(T185[:], T39, T40, 1408, T35, T36, 0, 1)
+  T32 = KP([128, 1024], U, tag='w2q2_codes', bufs=1, align_bytes=64)
+  T33 = KP([128, 1024], U8, tag='w2q2_scales', bufs=1, align_bytes=64)
+  Q(T32[:, 0:512], T33[:, 0:512], T222[:].rearrange(S9))
+  AC(T182[:], T182[:], ACT.Exp)
+  T186 = PP([128, 512], F, tag='l_1', bufs=1)
+  M(T186[:], T12, T13, 1664, T8, T9, 1, 0)
+  M(T186[:], T21, T22, 1664, T17, T18, 0, 0)
+  T197 = AQ.tile([128, 512], F, tag='top_1', bufs=1)
+  TT(out=T197[:], in0=T185[:], in1=T183[:], op=ALU.max)
+  M(T186[:], T30, T31, 1664, T26, T27, 0, 0)
+  M(T186[:], T39, T40, 1664, T35, T36, 0, 1)
+  ST(out=T192[:], in0=T188[:, 0, :], scalar=T134[:, 0:1], in1=T192[:], op0=ALU.mult, op1=ALU.add)
+  T187 = PP([128, 512], F, tag='l_2', bufs=1)
+  M(T187[:], T12, T13, 1920, T8, T9, 1, 0)
+  M(T187[:], T21, T22, 1920, T17, T18, 0, 0)
+  TT(out=T197[:], in0=T186[:], in1=T197[:], op=ALU.max)
+  M(T187[:], T30, T31, 1920, T26, T27, 0, 0)
+  M(T187[:], T39, T40, 1920, T35, T36, 0, 1)
+  TT(out=T151[:, 0, :], in0=T151[:, 0, :], in1=T192[:], op=ALU.mult)
+  T195 = AQ.tile([128, 512], F, tag='th_1', bufs=1)
+  AC(T195[:], T193[:], ACT.Tanh, scale=0.5)
+  nc.gpsimd.tensor_tensor(out=T135[:, 2, :], in0=T182[:, 0, :], in1=T182[:, 1, :], op=ALU.add)
+  T201 = PP([128, 512], F, tag='h_1', bufs=1)
+  M(T201[:], T14, T15, 256, T10, T11, 1, 1)
+  TT(out=T197[:], in0=T187[:], in1=T197[:], op=ALU.max)
+  T202 = AQ.tile([128, 512], F, tag='th_2', bufs=1)
+  AC(T202[:], T200[:], ACT.Tanh, scale=0.5)
+  T208 = PP([128, 512], F, tag='h_2', bufs=1)
+  M(T208[:], T14, T15, 896, T10, T11, 1, 1)
+  T198 = AQ.tile([128, 512], F, tag='r_1', bufs=1)
+  ST(out=T198[:], in0=T195[:], scalar=1.0, in1=T194[:], op0=ALU.add, op1=ALU.mult)
+  T228 = AQ.tile([128, 512, 4], B, tag='grouped_0', bufs=1, align_bytes=64)
+  SC(T228[:], T212[:].rearrange(S13))
+  nc.gpsimd.tensor_tensor(out=T135[:, 2, :], in0=T135[:, 2, :], in1=T182[:, 2, :], op=ALU.add)
+  T206 = AQ.tile([128, 4, 512], F, tag='f8_3', bufs=1)
+  TT(out=T206[:, 1, :], in0=T185[:], in1=T197[:], op=ALU.subtract)
+  T209 = PP([128, 512], F, tag='h_3', bufs=1)
+  M(T209[:], T14, T15, 384, T10, T11, 1, 1)
+  TT(out=T206[:, 2, :], in0=T186[:], in1=T197[:], op=ALU.subtract)
+  T204 = PP([128, 256, 4], B, tag='l_0', bufs=1)
+  MT(T204[:, 0:128, :], lhsT=T3[:], rhs=T141[:, :, 0:128].rearrange(S13), start=True, stop=True)
+  MT(T204[:, 128:256, :], lhsT=T3[:], rhs=T141[:, :, 128:256].rearrange(S13), start=True, stop=True)
+  nc.gpsimd.tensor_tensor(out=T135[:, 2, :], in0=T135[:, 2, :], in1=T182[:, 3, :], op=ALU.add)
+  TT(out=T206[:, 3, :], in0=T187[:], in1=T197[:], op=ALU.subtract)
+  T205 = PP([128, 256, 4], B, tag='l_1', bufs=1)
+  MT(T205[:, 0:128, :], lhsT=T3[:], rhs=T141[:, :, 256:384].rearrange(S13), start=True, stop=True)
+  MT(T205[:, 128:256, :], lhsT=T3[:], rhs=T141[:, :, 384:512].rearrange(S13), start=True, stop=True)
+  TT(out=T206[:, 0, :], in0=T183[:], in1=T197[:], op=ALU.subtract)
+  T203 = AQ.tile([128, 512, 4], B, tag='grouped_1', bufs=1, align_bytes=64)
+  SC(T203[:, 0:256, :], T204[:])
+  T233 = AQ.tile([128, 4, 512], B, tag='w2_raw_0', bufs=1)
+  DM(out=T233[:], in_=w2[3, :, 0:512].rearrange(S1, j=4))
+  T234 = AQ.tile([128, 4, 512], B, tag='w2_raw_1', bufs=1)
+  DM(out=T234[:], in_=w2[3, :, 512:1024].rearrange(S1, j=4))
+  T207 = AQ.tile([128, 512], F, tag='r_2', bufs=1)
+  ST(out=T207[:], in0=T202[:], scalar=1.0, in1=T201[:], op0=ALU.add, op1=ALU.mult)
+  SC(T203[:, 256:512, :], T205[:])
+  ST(out=T198[:], in0=T188[:, 1, :], scalar=T134[:, 1:2], in1=T198[:], op0=ALU.mult, op1=ALU.add)
+  T216 = PP([128, 512], F, tag='h_1', bufs=1)
+  M(T216[:], T23, T24, 0, T19, T20, 1, 1)
+  T210 = AQ.tile([128, 512], F, tag='th_0', bufs=1)
+  AC(T210[:], T208[:], ACT.Tanh, scale=0.5)
+  Q(T23[:, 512:1024], T24[:, 512:1024], T203[:].rearrange(S9))
+  T199 = PP([128, 2, 512], B, tag='x', bufs=1)
+  TR(T199[:, 0, 0:128], T7[:, 0, 256:384], T3[:])
+  AC(T206[:], T206[:], ACT.Exp)
+  TR(T199[:, 0, 128:256], T7[:, 1, 256:384], T3[:])
+  TR(T199[:, 0, 256:384], T7[:, 2, 256:384], T3[:])
+  TR(T199[:, 0, 384:512], T7[:, 3, 256:384], T3[:])
+  TR(T199[:, 1, 0:128], T7[:, 0, 384:512], T3[:])
+  T213 = AQ.tile([128, 512], F, tag='r_3', bufs=1)
+  ST(out=T213[:], in0=T210[:], scalar=1.0, in1=T209[:], op0=ALU.add, op1=ALU.mult)
+  TR(T199[:, 1, 128:256], T7[:, 1, 384:512], T3[:])
+  TR(T199[:, 1, 256:384], T7[:, 2, 384:512], T3[:])
+  TR(T199[:, 1, 384:512], T7[:, 3, 384:512], T3[:])
+  T215 = PP([128, 512], F, tag='h_0', bufs=1)
+  M(T215[:], T23, T24, 512, T19, T20, 1, 1)
+  ST(out=T207[:], in0=T199[:, 0, :], scalar=T134[:, 2:3], in1=T207[:], op0=ALU.mult, op1=ALU.add)
+  T219 = PP([128, 512], F, tag='h_2', bufs=1)
+  M(T219[:], T23, T24, 640, T19, T20, 1, 1)
+  T220 = PP([128, 512], F, tag='h_3', bufs=1)
+  M(T220[:], T23, T24, 128, T19, T20, 1, 1)
+  TT(out=T162[:, 0, :], in0=T162[:, 0, :], in1=T198[:], op=ALU.mult)
+  ST(out=T213[:], in0=T199[:, 1, :], scalar=T134[:, 3:4], in1=T213[:], op0=ALU.mult, op1=ALU.add)
+  T245 = PP([128, 256, 4], B, tag='l_2', bufs=1)
+  MT(T245[:, 0:128, :], lhsT=T3[:], rhs=T233[:, :, 0:128].rearrange(S13), start=True, stop=True)
+  T217 = AQ.tile([128, 512], F, tag='th_1', bufs=1)
+  AC(T217[:], T215[:], ACT.Tanh, scale=0.5)
+  nc.gpsimd.tensor_tensor(out=T135[:, 3, :], in0=T206[:, 0, :], in1=T206[:, 1, :], op=ALU.add)
+  MT(T245[:, 128:256, :], lhsT=T3[:], rhs=T233[:, :, 128:256].rearrange(S13), start=True, stop=True)
+  TT(out=T182[:, 0, :], in0=T182[:, 0, :], in1=T207[:], op=ALU.mult)
+  T246 = PP([128, 256, 4], B, tag='l_0', bufs=1)
+  MT(T246[:, 0:128, :], lhsT=T3[:], rhs=T233[:, :, 256:384].rearrange(S13), start=True, stop=True)
+  T221 = AQ.tile([128, 512], F, tag='th_2', bufs=1)
+  AC(T221[:], T219[:], ACT.Tanh, scale=0.5)
+  T214 = PP([128, 2, 512], B, tag='x', bufs=1)
+  TR(T214[:, 0, 0:128], T16[:, 0, 0:128], T3[:])
+  TR(T214[:, 0, 128:256], T16[:, 1, 0:128], T3[:])
+  T218 = AQ.tile([128, 512], F, tag='r_0', bufs=1)
+  ST(out=T218[:], in0=T217[:], scalar=1.0, in1=T216[:], op0=ALU.add, op1=ALU.mult)
+  TR(T214[:, 0, 256:384], T16[:, 2, 0:128], T3[:])
+  TR(T214[:, 0, 384:512], T16[:, 3, 0:128], T3[:])
+  TR(T214[:, 1, 0:128], T16[:, 0, 128:256], T3[:])
+  T244 = AQ.tile([128, 512, 4], B, tag='grouped_1', bufs=1, align_bytes=64)
+  SC(T244[:, 0:256, :], T245[:])
+  TR(T214[:, 1, 128:256], T16[:, 1, 128:256], T3[:])
+  TR(T214[:, 1, 256:384], T16[:, 2, 128:256], T3[:])
+  TR(T214[:, 1, 384:512], T16[:, 3, 128:256], T3[:])
+  T225 = PP([128, 512], F, tag='h_0', bufs=1)
+  M(T225[:], T23, T24, 768, T19, T20, 1, 1)
+  nc.gpsimd.tensor_tensor(out=T135[:, 3, :], in0=T135[:, 3, :], in1=T206[:, 2, :], op=ALU.add)
+  T223 = AQ.tile([128, 512], F, tag='r_1', bufs=1)
+  ST(out=T223[:], in0=T221[:], scalar=1.0, in1=T220[:], op0=ALU.add, op1=ALU.mult)
+  T252 = AQ.tile([128, 512, 4], B, tag='grouped_2', bufs=1, align_bytes=64)
+  SC(T252[:], T234[:].rearrange(S13))
+  T226 = PP([128, 512], F, tag='h_1', bufs=1)
+  M(T226[:], T23, T24, 256, T19, T20, 1, 1)
+  T230 = PP([128, 512], F, tag='h_2', bufs=1)
+  M(T230[:], T23, T24, 896, T19, T20, 1, 1)
+  ST(out=T218[:], in0=T214[:, 0, :], scalar=T134[:, 4:5], in1=T218[:], op0=ALU.mult, op1=ALU.add)
+  T231 = PP([128, 512], F, tag='h_3', bufs=1)
+  M(T231[:], T23, T24, 384, T19, T20, 1, 1)
+  MT(T246[:, 128:256, :], lhsT=T3[:], rhs=T233[:, :, 384:512].rearrange(S13), start=True, stop=True)
+  TT(out=T206[:, 0, :], in0=T206[:, 0, :], in1=T213[:], op=ALU.mult)
+  nc.gpsimd.tensor_tensor(out=T135[:, 3, :], in0=T135[:, 3, :], in1=T206[:, 3, :], op=ALU.add)
+  ST(out=T223[:], in0=T214[:, 1, :], scalar=T134[:, 5:6], in1=T223[:], op0=ALU.mult, op1=ALU.add)
+  Q(T32[:, 512:1024], T33[:, 512:1024], T228[:].rearrange(S9))
+  T224 = PP([128, 2, 512], B, tag='x', bufs=1)
+  TR(T224[:, 0, 0:128], T16[:, 0, 256:384], T3[:])
+  TR(T224[:, 0, 128:256], T16[:, 1, 256:384], T3[:])
+  TR(T224[:, 0, 256:384], T16[:, 2, 256:384], T3[:])
+  T227 = AQ.tile([128, 512], F, tag='th_0', bufs=1)
+  AC(T227[:], T225[:], ACT.Tanh, scale=0.5)
+  TR(T224[:, 0, 384:512], T16[:, 3, 256:384], T3[:])
+  TR(T224[:, 1, 0:128], T16[:, 0, 384:512], T3[:])
+  TT(out=T151[:, 1, :], in0=T151[:, 1, :], in1=T218[:], op=ALU.mult)
+  TR(T224[:, 1, 128:256], T16[:, 1, 384:512], T3[:])
+  TR(T224[:, 1, 256:384], T16[:, 2, 384:512], T3[:])
+  TR(T224[:, 1, 384:512], T16[:, 3, 384:512], T3[:])
+  T232 = AQ.tile([128, 512], F, tag='th_1', bufs=1)
+  AC(T232[:], T230[:], ACT.Tanh, scale=0.5)
+  T237 = PP([128, 512], F, tag='h_0', bufs=1)
+  M(T237[:], T32, T33, 512, T28, T29, 1, 1)
+  T229 = AQ.tile([128, 512], F, tag='r_2', bufs=1)
+  ST(out=T229[:], in0=T227[:], scalar=1.0, in1=T226[:], op0=ALU.add, op1=ALU.mult)
+  nc.gpsimd.tensor_tensor(out=T151[:, 0, :], in0=T151[:, 0, :], in1=T151[:, 1, :], op=ALU.add)
+  SC(T244[:, 256:512, :], T246[:])
+  T241 = PP([128, 512], F, tag='h_2', bufs=1)
+  M(T241[:], T32, T33, 640, T28, T29, 1, 1)
+  T235 = AQ.tile([128, 512], F, tag='r_3', bufs=1)
+  ST(out=T235[:], in0=T232[:], scalar=1.0, in1=T231[:], op0=ALU.add, op1=ALU.mult)
+  T238 = PP([128, 512], F, tag='h_1', bufs=1)
+  M(T238[:], T32, T33, 0, T28, T29, 1, 1)
+  T239 = AQ.tile([128, 512], F, tag='th_2', bufs=1)
+  AC(T239[:], T237[:], ACT.Tanh, scale=0.5)
+  ST(out=T229[:], in0=T224[:, 0, :], scalar=T134[:, 6:7], in1=T229[:], op0=ALU.mult, op1=ALU.add)
+  T242 = PP([128, 512], F, tag='h_3', bufs=1)
+  M(T242[:], T32, T33, 128, T28, T29, 1, 1)
+  T243 = AQ.tile([128, 512], F, tag='th_0', bufs=1)
+  AC(T243[:], T241[:], ACT.Tanh, scale=0.5)
+  T249 = PP([128, 512], F, tag='h_0', bufs=1)
+  M(T249[:], T32, T33, 768, T28, T29, 1, 1)
+  TT(out=T162[:, 1, :], in0=T162[:, 1, :], in1=T223[:], op=ALU.mult)
+  T254 = PP([128, 512], F, tag='h_2', bufs=1)
+  M(T254[:], T32, T33, 896, T28, T29, 1, 1)
+  T251 = AQ.tile([128, 512], F, tag='th_1', bufs=1)
+  AC(T251[:], T249[:], ACT.Tanh, scale=0.5)
+  T240 = AQ.tile([128, 512], F, tag='r_0', bufs=1)
+  ST(out=T240[:], in0=T239[:], scalar=1.0, in1=T238[:], op0=ALU.add, op1=ALU.mult)
+  nc.gpsimd.tensor_tensor(out=T162[:, 0, :], in0=T162[:, 0, :], in1=T162[:, 1, :], op=ALU.add)
+  ST(out=T235[:], in0=T224[:, 1, :], scalar=T134[:, 7:8], in1=T235[:], op0=ALU.mult, op1=ALU.add)
+  T250 = PP([128, 512], F, tag='h_1', bufs=1)
+  M(T250[:], T32, T33, 256, T28, T29, 1, 1)
+  T256 = AQ.tile([128, 512], F, tag='th_2', bufs=1)
+  AC(T256[:], T254[:], ACT.Tanh, scale=0.5)
+  TT(out=T182[:, 1, :], in0=T182[:, 1, :], in1=T229[:], op=ALU.mult)
+  T236 = PP([128, 2, 512], B, tag='x', bufs=1)
+  TR(T236[:, 0, 0:128], T25[:, 0, 0:128], T3[:])
+  AC(T135[:, 0:4, :], T135[:, 0:4, :], ACT.Ln, scale=2.0)
+  TR(T236[:, 0, 128:256], T25[:, 1, 0:128], T3[:])
+  TR(T236[:, 0, 256:384], T25[:, 2, 0:128], T3[:])
+  TR(T236[:, 0, 384:512], T25[:, 3, 0:128], T3[:])
+  TR(T236[:, 1, 0:128], T25[:, 0, 128:256], T3[:])
+  T247 = AQ.tile([128, 512], F, tag='r_1', bufs=1)
+  ST(out=T247[:], in0=T243[:], scalar=1.0, in1=T242[:], op0=ALU.add, op1=ALU.mult)
+  TR(T236[:, 1, 128:256], T25[:, 1, 128:256], T3[:])
+  TR(T236[:, 1, 256:384], T25[:, 2, 128:256], T3[:])
+  nc.gpsimd.tensor_tensor(out=T182[:, 0, :], in0=T182[:, 0, :], in1=T182[:, 1, :], op=ALU.add)
+  TR(T236[:, 1, 384:512], T25[:, 3, 128:256], T3[:])
+  ST(out=T240[:], in0=T236[:, 0, :], scalar=T134[:, 8:9], in1=T240[:], op0=ALU.mult, op1=ALU.add)
+  T255 = PP([128, 512], F, tag='h_3', bufs=1)
+  M(T255[:], T32, T33, 384, T28, T29, 1, 1)
+  TT(out=T206[:, 1, :], in0=T206[:, 1, :], in1=T235[:], op=ALU.mult)
+  T253 = AQ.tile([128, 512], F, tag='r_2', bufs=1)
+  ST(out=T253[:], in0=T251[:], scalar=1.0, in1=T250[:], op0=ALU.add, op1=ALU.mult)
+  nc.gpsimd.tensor_tensor(out=T206[:, 0, :], in0=T206[:, 0, :], in1=T206[:, 1, :], op=ALU.add)
+  T41 = KP([128, 1024], U, tag='w2q3_codes', bufs=1, align_bytes=64)
+  T42 = KP([128, 1024], U8, tag='w2q3_scales', bufs=1, align_bytes=64)
+  Q(T41[:, 0:512], T42[:, 0:512], T244[:].rearrange(S9))
+  ST(out=T247[:], in0=T236[:, 1, :], scalar=T134[:, 9:10], in1=T247[:], op0=ALU.mult, op1=ALU.add)
+  T260 = PP([128, 512], F, tag='h_1', bufs=1)
+  M(T260[:], T41, T42, 0, T37, T38, 1, 1)
+  Q(T41[:, 512:1024], T42[:, 512:1024], T252[:].rearrange(S9))
+  T248 = PP([128, 2, 512], B, tag='x', bufs=1)
+  TR(T248[:, 0, 0:128], T25[:, 0, 256:384], T3[:])
+  AC(T135[:, 0:4, :], T135[:, 0:4, :], ACT.Exp, scale=-1.0)
+  TR(T248[:, 0, 128:256], T25[:, 1, 256:384], T3[:])
+  TR(T248[:, 0, 256:384], T25[:, 2, 256:384], T3[:])
+  TR(T248[:, 0, 384:512], T25[:, 3, 256:384], T3[:])
+  TR(T248[:, 1, 0:128], T25[:, 0, 384:512], T3[:])
+  TT(out=T151[:, 2, :], in0=T151[:, 2, :], in1=T240[:], op=ALU.mult)
+  TR(T248[:, 1, 128:256], T25[:, 1, 384:512], T3[:])
+  TR(T248[:, 1, 256:384], T25[:, 2, 384:512], T3[:])
+  TR(T248[:, 1, 384:512], T25[:, 3, 384:512], T3[:])
+  T259 = PP([128, 512], F, tag='h_0', bufs=1)
+  M(T259[:], T41, T42, 512, T37, T38, 1, 1)
+  T257 = AQ.tile([128, 512], F, tag='r_3', bufs=1)
+  ST(out=T257[:], in0=T256[:], scalar=1.0, in1=T255[:], op0=ALU.add, op1=ALU.mult)
+  T263 = PP([128, 512], F, tag='h_2', bufs=1)
+  M(T263[:], T41, T42, 640, T37, T38, 1, 1)
+  nc.gpsimd.tensor_tensor(out=T151[:, 0, :], in0=T151[:, 0, :], in1=T151[:, 2, :], op=ALU.add)
+  ST(out=T253[:], in0=T248[:, 0, :], scalar=T134[:, 10:11], in1=T253[:], op0=ALU.mult, op1=ALU.add)
+  T264 = PP([128, 512], F, tag='h_3', bufs=1)
+  M(T264[:], T41, T42, 128, T37, T38, 1, 1)
+  TT(out=T162[:, 2, :], in0=T162[:, 2, :], in1=T247[:], op=ALU.mult)
+  ST(out=T257[:], in0=T248[:, 1, :], scalar=T134[:, 11:12], in1=T257[:], op0=ALU.mult, op1=ALU.add)
+  nc.gpsimd.tensor_tensor(out=T162[:, 0, :], in0=T162[:, 0, :], in1=T162[:, 2, :], op=ALU.add)
+  TT(out=T182[:, 2, :], in0=T182[:, 2, :], in1=T253[:], op=ALU.mult)
+  T258 = PP([128, 2, 512], B, tag='x', bufs=1)
+  TR(T258[:, 0, 0:128], T34[:, 0, 0:128], T3[:])
+  TR(T258[:, 0, 128:256], T34[:, 1, 0:128], T3[:])
+  TR(T258[:, 0, 256:384], T34[:, 2, 0:128], T3[:])
+  TR(T258[:, 0, 384:512], T34[:, 3, 0:128], T3[:])
+  TR(T258[:, 1, 0:128], T34[:, 0, 128:256], T3[:])
+  TT(out=T206[:, 2, :], in0=T206[:, 2, :], in1=T257[:], op=ALU.mult)
+  TR(T258[:, 1, 128:256], T34[:, 1, 128:256], T3[:])
+  T261 = AQ.tile([128, 512], F, tag='th_0', bufs=1)
+  AC(T261[:], T259[:], ACT.Tanh, scale=0.5)
+  TR(T258[:, 1, 256:384], T34[:, 2, 128:256], T3[:])
+  TR(T258[:, 1, 384:512], T34[:, 3, 128:256], T3[:])
+  nc.gpsimd.tensor_tensor(out=T182[:, 0, :], in0=T182[:, 0, :], in1=T182[:, 2, :], op=ALU.add)
+  T265 = AQ.tile([128, 512], F, tag='th_1', bufs=1)
+  AC(T265[:], T263[:], ACT.Tanh, scale=0.5)
+  T262 = AQ.tile([128, 512], F, tag='r_0', bufs=1)
+  ST(out=T262[:], in0=T261[:], scalar=1.0, in1=T260[:], op0=ALU.add, op1=ALU.mult)
+  T268 = PP([128, 512], F, tag='h_0', bufs=1)
+  M(T268[:], T41, T42, 768, T37, T38, 1, 1)
+  T272 = PP([128, 512], F, tag='h_2', bufs=1)
+  M(T272[:], T41, T42, 896, T37, T38, 1, 1)
+  T266 = AQ.tile([128, 512], F, tag='r_1', bufs=1)
+  ST(out=T266[:], in0=T265[:], scalar=1.0, in1=T264[:], op0=ALU.add, op1=ALU.mult)
+  T270 = AQ.tile([128, 512], F, tag='th_2', bufs=1)
+  AC(T270[:], T268[:], ACT.Tanh, scale=0.5)
+  nc.gpsimd.tensor_tensor(out=T206[:, 0, :], in0=T206[:, 0, :], in1=T206[:, 2, :], op=ALU.add)
+  T269 = PP([128, 512], F, tag='h_1', bufs=1)
+  M(T269[:], T41, T42, 256, T37, T38, 1, 1)
+  ST(out=T262[:], in0=T258[:, 0, :], scalar=T134[:, 12:13], in1=T262[:], op0=ALU.mult, op1=ALU.add)
+  T274 = AQ.tile([128, 512], F, tag='th_0', bufs=1)
+  AC(T274[:], T272[:], ACT.Tanh, scale=0.5)
+  T273 = PP([128, 512], F, tag='h_3', bufs=1)
+  M(T273[:], T41, T42, 384, T37, T38, 1, 1)
+  T271 = AQ.tile([128, 512], F, tag='r_2', bufs=1)
+  ST(out=T271[:], in0=T270[:], scalar=1.0, in1=T269[:], op0=ALU.add, op1=ALU.mult)
+  ST(out=T266[:], in0=T258[:, 1, :], scalar=T134[:, 13:14], in1=T266[:], op0=ALU.mult, op1=ALU.add)
+  TT(out=T151[:, 3, :], in0=T151[:, 3, :], in1=T262[:], op=ALU.mult)
+  T267 = PP([128, 2, 512], B, tag='x', bufs=1)
+  TR(T267[:, 0, 0:128], T34[:, 0, 256:384], T3[:])
+  TR(T267[:, 0, 128:256], T34[:, 1, 256:384], T3[:])
+  TR(T267[:, 0, 256:384], T34[:, 2, 256:384], T3[:])
+  TR(T267[:, 0, 384:512], T34[:, 3, 256:384], T3[:])
+  TR(T267[:, 1, 0:128], T34[:, 0, 384:512], T3[:])
+  T275 = AQ.tile([128, 512], F, tag='r_3', bufs=1)
+  ST(out=T275[:], in0=T274[:], scalar=1.0, in1=T273[:], op0=ALU.add, op1=ALU.mult)
+  TR(T267[:, 1, 128:256], T34[:, 1, 384:512], T3[:])
+  TR(T267[:, 1, 256:384], T34[:, 2, 384:512], T3[:])
+  TR(T267[:, 1, 384:512], T34[:, 3, 384:512], T3[:])
+  ST(out=T271[:], in0=T267[:, 0, :], scalar=T134[:, 14:15], in1=T271[:], op0=ALU.mult, op1=ALU.add)
+  TT(out=T162[:, 3, :], in0=T162[:, 3, :], in1=T266[:], op=ALU.mult)
+  TT(out=T151[:, 3, :], in0=T151[:, 0, :], in1=T151[:, 3, :], op=ALU.add)
+  ST(out=T275[:], in0=T267[:, 1, :], scalar=T134[:, 15:16], in1=T275[:], op0=ALU.mult, op1=ALU.add)
+  TT(out=T182[:, 3, :], in0=T182[:, 3, :], in1=T271[:], op=ALU.mult)
+  TT(out=T162[:, 3, :], in0=T162[:, 0, :], in1=T162[:, 3, :], op=ALU.add)
+  TT(out=T151[:, 3, :], in0=T151[:, 3, :], in1=T135[:, 0, :], op=ALU.mult)
+  TT(out=T206[:, 3, :], in0=T206[:, 3, :], in1=T275[:], op=ALU.mult)
+  T276 = PP([128, 4, 128], F, tag='l_1', bufs=1)
+  TR(T276[:, 0, :], T151[:, 3, 0:128], T0[:])
+  TR(T276[:, 1, :], T151[:, 3, 128:256], T0[:])
+  TR(T276[:, 2, :], T151[:, 3, 256:384], T0[:])
+  TR(T276[:, 3, :], T151[:, 3, 384:512], T0[:])
+  TT(out=T182[:, 3, :], in0=T182[:, 0, :], in1=T182[:, 3, :], op=ALU.add)
+  T277 = AQ.tile([128, 4, 128], F, tag='rows_0', bufs=1)
+  SC(T277[:], T276[:])
+  TT(out=T162[:, 3, :], in0=T162[:, 3, :], in1=T135[:, 1, :], op=ALU.mult)
+  DM(out=out[:, 0:128].rearrange(S3, p=128), in_=T277[:])
+  TT(out=T206[:, 3, :], in0=T206[:, 0, :], in1=T206[:, 3, :], op=ALU.add)
+  T278 = PP([128, 4, 128], F, tag='l_2', bufs=1)
+  TR(T278[:, 0, :], T162[:, 3, 0:128], T0[:])
+  TR(T278[:, 1, :], T162[:, 3, 128:256], T0[:])
+  TR(T278[:, 2, :], T162[:, 3, 256:384], T0[:])
+  TR(T278[:, 3, :], T162[:, 3, 384:512], T0[:])
+  TT(out=T182[:, 3, :], in0=T182[:, 3, :], in1=T135[:, 2, :], op=ALU.mult)
+  T279 = AQ.tile([128, 4, 128], F, tag='rows_1', bufs=1)
+  SC(T279[:], T278[:])
+  TT(out=T206[:, 3, :], in0=T206[:, 3, :], in1=T135[:, 3, :], op=ALU.mult)
+  T280 = PP([128, 4, 128], F, tag='l_0', bufs=1)
+  TR(T280[:, 0, :], T182[:, 3, 0:128], T0[:])
+  DM(out=out[:, 128:256].rearrange(S3, p=128), in_=T279[:])
+  TR(T280[:, 1, :], T182[:, 3, 128:256], T0[:])
+  TR(T280[:, 2, :], T182[:, 3, 256:384], T0[:])
+  TR(T280[:, 3, :], T182[:, 3, 384:512], T0[:])
+  T282 = PP([128, 4, 128], F, tag='l_1', bufs=1)
+  TR(T282[:, 0, :], T206[:, 3, 0:128], T0[:])
+  TR(T282[:, 1, :], T206[:, 3, 128:256], T0[:])
+  TR(T282[:, 2, :], T206[:, 3, 256:384], T0[:])
+  TR(T282[:, 3, :], T206[:, 3, 384:512], T0[:])
+  T281 = AQ.tile([128, 4, 128], F, tag='rows_0', bufs=1)
+  SC(T281[:], T280[:])
+  DM(out=out[:, 256:384].rearrange(S3, p=128), in_=T281[:])
+  T283 = AQ.tile([128, 4, 128], F, tag='rows_1', bufs=1)
+  SC(T283[:], T282[:])
+  DM(out=out[:, 384:512].rearrange(S3, p=128), in_=T283[:])

@@ -23,8 +23,9 @@ S9 = 'p c t -> p (c t)'
 S10 = 'p n t -> p (n t)'
 S11 = 'p (n u) -> p n u'
 S12 = 'p u n -> p n u'
-S13 = 'p t c -> p c t'
-S14 = 'p t n -> p n t'
+S13 = 'p (c i) t -> p c t i'
+S14 = 'p t (c i) -> p c t i'
+S15 = 'p t n -> p n t'
 
 def tile_tftchannelwisevariableselection_kernel(tc, x, wl_bytes, wl_scale, w1, g1, w2, gs, out):
  nc = tc.nc
@@ -134,13 +135,12 @@ def tile_tftchannelwisevariableselection_kernel(tc, x, wl_bytes, wl_scale, w1, g
   AC(T54[:, 0, :], T55[:], ACT.Exp)
   T58 = PP([128, 512], F, tag='h_3', bufs=1)
   M(T58[:], T47, T48, 384, T8, T9, 1, 1)
+  T67 = AQ.tile([128, 512, 4], B, tag='grouped_0', bufs=1, align_bytes=64)
+  ve.tensor_copy(out=T67[:].rearrange(S13, i=4), in_=T53[:].rearrange(S14, i=4))
   T65 = PP([128, 2, 256], F, tag='l_2', bufs=1)
   TR(T65[:, 0, 0:128], T16[:].bitcast(F)[:, 0, 0::2], T0[:])
-  T61 = AQ.tile([128, 512], U, tag='w1q_codes_1', bufs=1, align_bytes=64)
-  T62 = AQ.tile([128, 512], U8, tag='w1q_scales_1', bufs=1, align_bytes=64)
-  Q(T61[:, 0:512], T62[:, 0:512], T63[:].rearrange(S9))
-  T81 = AQ.tile([128, 4, 512], B, tag='w1_raw_1', bufs=1)
-  DM(out=T81[:], in_=w1[3].rearrange(S1, j=4))
+  T77 = AQ.tile([128, 4, 512], B, tag='w1_raw_1', bufs=1)
+  DM(out=T77[:], in_=w1[3].rearrange(S1, j=4))
   AC(T54[:, 1, :], T56[:], ACT.Exp)
   TR(T65[:, 0, 128:256], T16[:].bitcast(F)[:, 1, 0::2], T0[:])
   TR(T65[:, 1, 0:128], T16[:].bitcast(F)[:, 0, 1::2], T0[:])
@@ -151,839 +151,763 @@ def tile_tftchannelwisevariableselection_kernel(tc, x, wl_bytes, wl_scale, w1, g
   TR(T66[:, 0, 128:256], T16[:].bitcast(F)[:, 3, 0::2], T0[:])
   TR(T66[:, 1, 0:128], T16[:].bitcast(F)[:, 2, 1::2], T0[:])
   TR(T66[:, 1, 128:256], T16[:].bitcast(F)[:, 3, 1::2], T0[:])
-  T68 = PP([128, 256, 4], B, tag='l_1', bufs=1)
-  MT(T68[:, 0:128, :], lhsT=T3[:], rhs=T53[:, :, 0:128].rearrange(S13), start=True, stop=True)
   AC(T54[:, 3, :], T58[:], ACT.Exp)
-  MT(T68[:, 128:256, :], lhsT=T3[:], rhs=T53[:, :, 128:256].rearrange(S13), start=True, stop=True)
+  T61 = AQ.tile([128, 512], U, tag='w1q_codes_1', bufs=1, align_bytes=64)
+  T62 = AQ.tile([128, 512], U8, tag='w1q_scales_1', bufs=1, align_bytes=64)
+  Q(T61[:, 0:512], T62[:, 0:512], T63[:].rearrange(S9))
+  T83 = PP([128, 2, 256], F, tag='l_1', bufs=1)
+  TR(T83[:, 0, 0:128], T25[:].bitcast(F)[:, 0, 0::2], T0[:])
+  TR(T83[:, 0, 128:256], T25[:].bitcast(F)[:, 1, 0::2], T0[:])
   T64 = AQ.tile([128, 512, 4], B, tag='xg', bufs=1, align_bytes=64)
   SC(T64[:].rearrange(S10).bitcast(F).rearrange(S11, u=2)[:, 0:256, :], T65[:].rearrange(S12))
-  ve.tensor_scalar(out=T54[:], in0=T54[:], scalar1=1.0, scalar2=None, op0=ALU.min)
-  SC(T64[:].rearrange(S10).bitcast(F).rearrange(S11, u=2)[:, 256:512, :], T66[:].rearrange(S12))
-  T69 = PP([128, 256, 4], B, tag='l_2', bufs=1)
-  MT(T69[:, 0:128, :], lhsT=T3[:], rhs=T53[:, :, 256:384].rearrange(S13), start=True, stop=True)
-  MT(T69[:, 128:256, :], lhsT=T3[:], rhs=T53[:, :, 384:512].rearrange(S13), start=True, stop=True)
-  T67 = AQ.tile([128, 512, 4], B, tag='grouped_0', bufs=1, align_bytes=64)
-  SC(T67[:, 0:256, :], T68[:])
-  T133 = PP([128, 128], B, tag='x', bufs=1)
-  TR(T133[:], T5[:], T3[:])
-  T17 = KP([128, 512], U, tag='xq1_codes', bufs=1, align_bytes=64)
-  T18 = KP([128, 512], U8, tag='xq1_scales', bufs=1, align_bytes=64)
-  Q(T17[:, 0:512], T18[:, 0:512], T64[:].rearrange(S9))
-  SC(T67[:, 256:512, :], T69[:])
-  ST(out=T54[:, 0, :], in0=T55[:], scalar=1.0, in1=T54[:, 0, :], op0=ALU.add, op1=ALU.max)
-  T70 = AQ.tile([128, 4, 512], B, tag='wl_wide_1', bufs=1)
-  AC(T70[:, 0, :], T44[:].rearrange(S8)[:, 0, 512:1024].bitcast(E4), ACT.Copy, scale=T2[:, 0, 0:1])
-  T87 = PP([128, 2, 256], F, tag='l_2', bufs=1)
-  TR(T87[:, 0, 0:128], T25[:].bitcast(F)[:, 0, 0::2], T0[:])
-  ST(out=T54[:, 1, :], in0=T56[:], scalar=1.0, in1=T54[:, 1, :], op0=ALU.add, op1=ALU.max)
-  T76 = PP([128, 512], F, tag='h_0', bufs=1)
-  M(T76[:], T61, T62, 0, T17, T18, 1, 1)
-  AC(T70[:, 1, :], T44[:].rearrange(S8)[:, 1, 512:1024].bitcast(E4), ACT.Copy, scale=T2[:, 0, 1:2])
-  TR(T87[:, 0, 128:256], T25[:].bitcast(F)[:, 1, 0::2], T0[:])
-  ST(out=T54[:, 2, :], in0=T57[:], scalar=1.0, in1=T54[:, 2, :], op0=ALU.add, op1=ALU.max)
-  TR(T87[:, 1, 0:128], T25[:].bitcast(F)[:, 0, 1::2], T0[:])
-  T77 = PP([128, 512], F, tag='h_1', bufs=1)
-  M(T77[:], T61, T62, 128, T17, T18, 1, 1)
-  AC(T70[:, 2, :], T44[:].rearrange(S8)[:, 2, 512:1024].bitcast(E4), ACT.Copy, scale=T2[:, 0, 2:3])
-  TR(T87[:, 1, 128:256], T25[:].bitcast(F)[:, 1, 1::2], T0[:])
-  ST(out=T54[:, 3, :], in0=T58[:], scalar=1.0, in1=T54[:, 3, :], op0=ALU.add, op1=ALU.max)
-  T78 = PP([128, 512], F, tag='h_2', bufs=1)
-  M(T78[:], T61, T62, 256, T17, T18, 1, 1)
-  AC(T70[:, 3, :], T44[:].rearrange(S8)[:, 3, 512:1024].bitcast(E4), ACT.Copy, scale=T2[:, 0, 3:4])
   T12 = KP([128, 2048], U, tag='wlq0_codes', bufs=1, align_bytes=64)
   T13 = KP([128, 2048], U8, tag='wlq0_scales', bufs=1, align_bytes=64)
   Q(T12[:, 0:512], T13[:, 0:512], T67[:].rearrange(S9))
-  T79 = PP([128, 512], F, tag='h_3', bufs=1)
-  M(T79[:], T61, T62, 384, T17, T18, 1, 1)
-  T75 = AQ.tile([128, 4, 512], F, tag='f8_1', bufs=1)
-  AC(T75[:, 0, :], T76[:], ACT.Exp)
-  T72 = PP([128, 256, 4], B, tag='l_0', bufs=1)
-  MT(T72[:, 0:128, :], lhsT=T3[:], rhs=T70[:, :, 0:128].rearrange(S13), start=True, stop=True)
-  T82 = AQ.tile([128, 4, 4, 256], U8, tag='wl_raw_0', bufs=1)
-  DM(out=T82[:, 0, :, :], in_=wl_bytes[1536:2048, :].rearrange(S4, t=4, v=4, h=2)[:, 0, :, 0, :])
-  T74 = AQ.tile([128, 512, 4], B, tag='eg', bufs=1, align_bytes=64)
-  ST(out=T74[:], in0=T54[:].rearrange(S14), scalar=-1.0, in1=T6[:, 0:1, :].broadcast_to([128, 512, 4]), op0=ALU.add, op1=ALU.mult)
-  DM(out=T82[:, 1, :, :], in_=wl_bytes[1536:2048, :].rearrange(S4, t=4, v=4, h=2)[:, 1, :, 0, :])
-  DM(out=T82[:, 2, :, :], in_=wl_bytes[1536:2048, :].rearrange(S4, t=4, v=4, h=2)[:, 2, :, 0, :])
-  DM(out=T82[:, 3, :, :], in_=wl_bytes[1536:2048, :].rearrange(S4, t=4, v=4, h=2)[:, 3, :, 0, :])
-  MT(T72[:, 128:256, :], lhsT=T3[:], rhs=T70[:, :, 128:256].rearrange(S13), start=True, stop=True)
-  AC(T75[:, 1, :], T77[:], ACT.Exp)
-  T73 = PP([128, 256, 4], B, tag='l_1', bufs=1)
-  MT(T73[:, 0:128, :], lhsT=T3[:], rhs=T70[:, :, 256:384].rearrange(S13), start=True, stop=True)
-  MT(T73[:, 128:256, :], lhsT=T3[:], rhs=T70[:, :, 384:512].rearrange(S13), start=True, stop=True)
-  T71 = AQ.tile([128, 512, 4], B, tag='grouped_1', bufs=1, align_bytes=64)
-  SC(T71[:, 0:256, :], T72[:])
-  SC(T71[:, 256:512, :], T73[:])
-  T88 = PP([128, 2, 256], F, tag='l_0', bufs=1)
-  TR(T88[:, 0, 0:128], T25[:].bitcast(F)[:, 2, 0::2], T0[:])
-  TR(T88[:, 0, 128:256], T25[:].bitcast(F)[:, 3, 0::2], T0[:])
-  TR(T88[:, 1, 0:128], T25[:].bitcast(F)[:, 2, 1::2], T0[:])
-  TR(T88[:, 1, 128:256], T25[:].bitcast(F)[:, 3, 1::2], T0[:])
-  AC(T75[:, 2, :], T78[:], ACT.Exp)
-  Q(T12[:, 512:1024], T13[:, 512:1024], T71[:].rearrange(S9))
-  AC(T75[:, 3, :], T79[:], ACT.Exp)
+  TR(T83[:, 1, 0:128], T25[:].bitcast(F)[:, 0, 1::2], T0[:])
+  TR(T83[:, 1, 128:256], T25[:].bitcast(F)[:, 1, 1::2], T0[:])
+  SC(T64[:].rearrange(S10).bitcast(F).rearrange(S11, u=2)[:, 256:512, :], T66[:].rearrange(S12))
+  ve.tensor_scalar(out=T54[:], in0=T54[:], scalar1=1.0, scalar2=None, op0=ALU.min)
+  T84 = PP([128, 2, 256], F, tag='l_2', bufs=1)
+  TR(T84[:, 0, 0:128], T25[:].bitcast(F)[:, 2, 0::2], T0[:])
+  TR(T84[:, 0, 128:256], T25[:].bitcast(F)[:, 3, 0::2], T0[:])
+  TR(T84[:, 1, 0:128], T25[:].bitcast(F)[:, 2, 1::2], T0[:])
+  TR(T84[:, 1, 128:256], T25[:].bitcast(F)[:, 3, 1::2], T0[:])
+  T68 = AQ.tile([128, 4, 512], B, tag='wl_wide_1', bufs=1)
+  AC(T68[:, 0, :], T44[:].rearrange(S8)[:, 0, 512:1024].bitcast(E4), ACT.Copy, scale=T2[:, 0, 0:1])
+  T117 = PP([128, 128], B, tag='x', bufs=1)
+  TR(T117[:], T5[:], T3[:])
+  T100 = PP([128, 2, 256], F, tag='l_0', bufs=1)
+  TR(T100[:, 0, 0:128], T34[:].bitcast(F)[:, 0, 0::2], T0[:])
+  TR(T100[:, 0, 128:256], T34[:].bitcast(F)[:, 1, 0::2], T0[:])
+  AC(T68[:, 1, :], T44[:].rearrange(S8)[:, 1, 512:1024].bitcast(E4), ACT.Copy, scale=T2[:, 0, 1:2])
+  T17 = KP([128, 512], U, tag='xq1_codes', bufs=1, align_bytes=64)
+  T18 = KP([128, 512], U8, tag='xq1_scales', bufs=1, align_bytes=64)
+  Q(T17[:, 0:512], T18[:, 0:512], T64[:].rearrange(S9))
+  TR(T100[:, 1, 0:128], T34[:].bitcast(F)[:, 0, 1::2], T0[:])
+  TR(T100[:, 1, 128:256], T34[:].bitcast(F)[:, 1, 1::2], T0[:])
+  AC(T68[:, 2, :], T44[:].rearrange(S8)[:, 2, 512:1024].bitcast(E4), ACT.Copy, scale=T2[:, 0, 2:3])
+  ST(out=T54[:, 0, :], in0=T55[:], scalar=1.0, in1=T54[:, 0, :], op0=ALU.add, op1=ALU.max)
+  AC(T68[:, 3, :], T44[:].rearrange(S8)[:, 3, 512:1024].bitcast(E4), ACT.Copy, scale=T2[:, 0, 3:4])
+  ST(out=T54[:, 1, :], in0=T56[:], scalar=1.0, in1=T54[:, 1, :], op0=ALU.add, op1=ALU.max)
+  T72 = PP([128, 512], F, tag='h_0', bufs=1)
+  M(T72[:], T61, T62, 0, T17, T18, 1, 1)
+  T76 = AQ.tile([128, 4, 512], B, tag='wl_wide_0', bufs=1)
+  AC(T76[:, 0, :], T46[:].rearrange(S8)[:, 0, 0:512].bitcast(E4), ACT.Copy, scale=T2[:, 1, 0:1])
+  ST(out=T54[:, 2, :], in0=T57[:], scalar=1.0, in1=T54[:, 2, :], op0=ALU.add, op1=ALU.max)
+  T78 = AQ.tile([128, 4, 4, 256], U8, tag='wl_raw_0', bufs=1)
+  DM(out=T78[:, 0, :, :], in_=wl_bytes[1536:2048, :].rearrange(S4, t=4, v=4, h=2)[:, 0, :, 0, :])
+  DM(out=T78[:, 1, :, :], in_=wl_bytes[1536:2048, :].rearrange(S4, t=4, v=4, h=2)[:, 1, :, 0, :])
+  DM(out=T78[:, 2, :, :], in_=wl_bytes[1536:2048, :].rearrange(S4, t=4, v=4, h=2)[:, 2, :, 0, :])
+  T73 = PP([128, 512], F, tag='h_1', bufs=1)
+  M(T73[:], T61, T62, 128, T17, T18, 1, 1)
+  DM(out=T78[:, 3, :, :], in_=wl_bytes[1536:2048, :].rearrange(S4, t=4, v=4, h=2)[:, 3, :, 0, :])
+  T71 = AQ.tile([128, 4, 512], F, tag='f8_1', bufs=1)
+  AC(T71[:, 0, :], T72[:], ACT.Exp)
+  ST(out=T54[:, 3, :], in0=T58[:], scalar=1.0, in1=T54[:, 3, :], op0=ALU.add, op1=ALU.max)
+  T74 = PP([128, 512], F, tag='h_2', bufs=1)
+  M(T74[:], T61, T62, 256, T17, T18, 1, 1)
+  AC(T71[:, 1, :], T73[:], ACT.Exp)
+  T69 = AQ.tile([128, 512, 4], B, tag='grouped_1', bufs=1, align_bytes=64)
+  ve.tensor_copy(out=T69[:].rearrange(S13, i=4), in_=T68[:].rearrange(S14, i=4))
+  T75 = PP([128, 512], F, tag='h_3', bufs=1)
+  M(T75[:], T61, T62, 384, T17, T18, 1, 1)
+  AC(T71[:, 2, :], T74[:], ACT.Exp)
+  AC(T71[:, 3, :], T75[:], ACT.Exp)
+  T70 = AQ.tile([128, 512, 4], B, tag='eg', bufs=1, align_bytes=64)
+  ST(out=T70[:], in0=T54[:].rearrange(S15), scalar=-1.0, in1=T6[:, 0:1, :].broadcast_to([128, 512, 4]), op0=ALU.add, op1=ALU.mult)
+  AC(T76[:, 1, :], T46[:].rearrange(S8)[:, 1, 0:512].bitcast(E4), ACT.Copy, scale=T2[:, 1, 1:2])
+  AC(T76[:, 2, :], T46[:].rearrange(S8)[:, 2, 0:512].bitcast(E4), ACT.Copy, scale=T2[:, 1, 2:3])
+  AC(T76[:, 3, :], T46[:].rearrange(S8)[:, 3, 0:512].bitcast(E4), ACT.Copy, scale=T2[:, 1, 3:4])
+  T82 = AQ.tile([128, 512, 4], B, tag='xg', bufs=1, align_bytes=64)
+  SC(T82[:].rearrange(S10).bitcast(F).rearrange(S11, u=2)[:, 0:256, :], T83[:].rearrange(S12))
+  Q(T12[:, 512:1024], T13[:, 512:1024], T69[:].rearrange(S9))
+  SC(T82[:].rearrange(S10).bitcast(F).rearrange(S11, u=2)[:, 256:512, :], T84[:].rearrange(S12))
+  T101 = PP([128, 2, 256], F, tag='l_1', bufs=1)
+  TR(T101[:, 0, 0:128], T34[:].bitcast(F)[:, 2, 0::2], T0[:])
+  TR(T101[:, 0, 128:256], T34[:].bitcast(F)[:, 3, 0::2], T0[:])
   T10 = KP([128, 512], U, tag='eq0_codes', bufs=1, align_bytes=64)
   T11 = KP([128, 512], U8, tag='eq0_scales', bufs=1, align_bytes=64)
-  Q(T10[:, 0:512], T11[:, 0:512], T74[:].rearrange(S9))
-  T80 = AQ.tile([128, 4, 512], B, tag='wl_wide_0', bufs=1)
-  AC(T80[:, 0, :], T46[:].rearrange(S8)[:, 0, 0:512].bitcast(E4), ACT.Copy, scale=T2[:, 1, 0:1])
-  T85 = AQ.tile([128, 512, 4], B, tag='w1g', bufs=1, align_bytes=64)
-  ve.tensor_copy(out=T85[:].rearrange(S6, t=4), in_=T59[:].rearrange(S7, t=4))
-  AC(T80[:, 1, :], T46[:].rearrange(S8)[:, 1, 0:512].bitcast(E4), ACT.Copy, scale=T2[:, 1, 1:2])
-  AC(T80[:, 2, :], T46[:].rearrange(S8)[:, 2, 0:512].bitcast(E4), ACT.Copy, scale=T2[:, 1, 2:3])
-  ve.tensor_scalar(out=T75[:], in0=T75[:], scalar1=1.0, scalar2=None, op0=ALU.min)
-  AC(T80[:, 3, :], T46[:].rearrange(S8)[:, 3, 0:512].bitcast(E4), ACT.Copy, scale=T2[:, 1, 3:4])
-  T86 = AQ.tile([128, 512, 4], B, tag='xg', bufs=1, align_bytes=64)
-  SC(T86[:].rearrange(S10).bitcast(F).rearrange(S11, u=2)[:, 0:256, :], T87[:].rearrange(S12))
-  T90 = PP([128, 256, 4], B, tag='l_1', bufs=1)
-  MT(T90[:, 0:128, :], lhsT=T3[:], rhs=T80[:, :, 0:128].rearrange(S13), start=True, stop=True)
-  T83 = AQ.tile([128, 512], U, tag='w1q_codes_0', bufs=1, align_bytes=64)
-  T84 = AQ.tile([128, 512], U8, tag='w1q_scales_0', bufs=1, align_bytes=64)
-  Q(T83[:, 0:512], T84[:, 0:512], T85[:].rearrange(S9))
-  MT(T90[:, 128:256, :], lhsT=T3[:], rhs=T80[:, :, 128:256].rearrange(S13), start=True, stop=True)
-  SC(T86[:].rearrange(S10).bitcast(F).rearrange(S11, u=2)[:, 256:512, :], T88[:].rearrange(S12))
-  T91 = PP([128, 256, 4], B, tag='l_2', bufs=1)
-  MT(T91[:, 0:128, :], lhsT=T3[:], rhs=T80[:, :, 256:384].rearrange(S13), start=True, stop=True)
-  ST(out=T75[:, 0, :], in0=T76[:], scalar=1.0, in1=T75[:, 0, :], op0=ALU.add, op1=ALU.max)
-  MT(T91[:, 128:256, :], lhsT=T3[:], rhs=T80[:, :, 384:512].rearrange(S13), start=True, stop=True)
-  T89 = AQ.tile([128, 512, 4], B, tag='grouped_2', bufs=1, align_bytes=64)
-  SC(T89[:, 0:256, :], T90[:])
-  ST(out=T75[:, 1, :], in0=T77[:], scalar=1.0, in1=T75[:, 1, :], op0=ALU.add, op1=ALU.max)
-  SC(T89[:, 256:512, :], T91[:])
-  ST(out=T75[:, 2, :], in0=T78[:], scalar=1.0, in1=T75[:, 2, :], op0=ALU.add, op1=ALU.max)
-  T92 = AQ.tile([128, 4, 512], B, tag='wl_wide_1', bufs=1)
-  AC(T92[:, 0, :], T46[:].rearrange(S8)[:, 0, 512:1024].bitcast(E4), ACT.Copy, scale=T2[:, 1, 0:1])
-  T108 = PP([128, 2, 256], F, tag='l_2', bufs=1)
-  TR(T108[:, 0, 0:128], T34[:].bitcast(F)[:, 0, 0::2], T0[:])
-  TR(T108[:, 0, 128:256], T34[:].bitcast(F)[:, 1, 0::2], T0[:])
-  ST(out=T75[:, 3, :], in0=T79[:], scalar=1.0, in1=T75[:, 3, :], op0=ALU.add, op1=ALU.max)
-  TR(T108[:, 1, 0:128], T34[:].bitcast(F)[:, 0, 1::2], T0[:])
-  AC(T92[:, 1, :], T46[:].rearrange(S8)[:, 1, 512:1024].bitcast(E4), ACT.Copy, scale=T2[:, 1, 1:2])
-  TR(T108[:, 1, 128:256], T34[:].bitcast(F)[:, 1, 1::2], T0[:])
+  Q(T10[:, 0:512], T11[:, 0:512], T70[:].rearrange(S9))
+  TR(T101[:, 1, 0:128], T34[:].bitcast(F)[:, 2, 1::2], T0[:])
+  TR(T101[:, 1, 128:256], T34[:].bitcast(F)[:, 3, 1::2], T0[:])
+  T85 = AQ.tile([128, 512, 4], B, tag='grouped_2', bufs=1, align_bytes=64)
+  SC(T85[:].rearrange(S13, i=4), T76[:].rearrange(S14, i=4))
+  T128 = PP([128, 512], F, tag='l_2', bufs=1)
+  M(T128[:], T12, T13, 0, T8, T9, 1, 0)
+  T81 = AQ.tile([128, 512, 4], B, tag='w1g', bufs=1, align_bytes=64)
+  ve.tensor_copy(out=T81[:].rearrange(S6, t=4), in_=T59[:].rearrange(S7, t=4))
+  ve.tensor_scalar(out=T71[:], in0=T71[:], scalar1=1.0, scalar2=None, op0=ALU.min)
+  T86 = AQ.tile([128, 4, 512], B, tag='wl_wide_1', bufs=1)
+  AC(T86[:, 0, :], T46[:].rearrange(S8)[:, 0, 512:1024].bitcast(E4), ACT.Copy, scale=T2[:, 1, 0:1])
+  T79 = AQ.tile([128, 512], U, tag='w1q_codes_0', bufs=1, align_bytes=64)
+  T80 = AQ.tile([128, 512], U8, tag='w1q_scales_0', bufs=1, align_bytes=64)
+  Q(T79[:, 0:512], T80[:, 0:512], T81[:].rearrange(S9))
+  AC(T86[:, 1, :], T46[:].rearrange(S8)[:, 1, 512:1024].bitcast(E4), ACT.Copy, scale=T2[:, 1, 1:2])
+  ST(out=T71[:, 0, :], in0=T72[:], scalar=1.0, in1=T71[:, 0, :], op0=ALU.add, op1=ALU.max)
+  AC(T86[:, 2, :], T46[:].rearrange(S8)[:, 2, 512:1024].bitcast(E4), ACT.Copy, scale=T2[:, 1, 2:3])
+  ST(out=T71[:, 1, :], in0=T73[:], scalar=1.0, in1=T71[:, 1, :], op0=ALU.add, op1=ALU.max)
+  AC(T86[:, 3, :], T46[:].rearrange(S8)[:, 3, 512:1024].bitcast(E4), ACT.Copy, scale=T2[:, 1, 3:4])
+  ST(out=T71[:, 2, :], in0=T74[:], scalar=1.0, in1=T71[:, 2, :], op0=ALU.add, op1=ALU.max)
+  T94 = AQ.tile([128, 4, 512], B, tag='wl_wide_0', bufs=1)
+  AC(T94[:, 0, :], T60[:].rearrange(S8)[:, 0, 0:512].bitcast(E4), ACT.Copy, scale=T2[:, 2, 0:1])
+  T95 = AQ.tile([128, 4, 4, 256], U8, tag='wl_raw_1', bufs=1)
+  DM(out=T95[:, 0, :, :], in_=wl_bytes[0:512, :].rearrange(S4, t=4, v=4, h=2)[:, 0, :, 1, :])
+  DM(out=T95[:, 1, :, :], in_=wl_bytes[0:512, :].rearrange(S4, t=4, v=4, h=2)[:, 1, :, 1, :])
+  DM(out=T95[:, 2, :, :], in_=wl_bytes[0:512, :].rearrange(S4, t=4, v=4, h=2)[:, 2, :, 1, :])
+  ST(out=T71[:, 3, :], in0=T75[:], scalar=1.0, in1=T71[:, 3, :], op0=ALU.add, op1=ALU.max)
+  DM(out=T95[:, 3, :, :], in_=wl_bytes[0:512, :].rearrange(S4, t=4, v=4, h=2)[:, 3, :, 1, :])
+  AC(T94[:, 1, :], T60[:].rearrange(S8)[:, 1, 0:512].bitcast(E4), ACT.Copy, scale=T2[:, 2, 1:2])
   T26 = KP([128, 512], U, tag='xq2_codes', bufs=1, align_bytes=64)
   T27 = KP([128, 512], U8, tag='xq2_scales', bufs=1, align_bytes=64)
-  Q(T26[:, 0:512], T27[:, 0:512], T86[:].rearrange(S9))
-  AC(T92[:, 2, :], T46[:].rearrange(S8)[:, 2, 512:1024].bitcast(E4), ACT.Copy, scale=T2[:, 1, 2:3])
-  T96 = AQ.tile([128, 512, 4], B, tag='eg', bufs=1, align_bytes=64)
-  ST(out=T96[:], in0=T75[:].rearrange(S14), scalar=-1.0, in1=T6[:, 1:2, :].broadcast_to([128, 512, 4]), op0=ALU.add, op1=ALU.mult)
-  AC(T92[:, 3, :], T46[:].rearrange(S8)[:, 3, 512:1024].bitcast(E4), ACT.Copy, scale=T2[:, 1, 3:4])
-  T98 = PP([128, 512], F, tag='h_0', bufs=1)
-  M(T98[:], T83, T84, 0, T26, T27, 1, 1)
-  T99 = PP([128, 512], F, tag='h_1', bufs=1)
-  M(T99[:], T83, T84, 128, T26, T27, 1, 1)
-  T102 = AQ.tile([128, 4, 512], B, tag='wl_wide_0', bufs=1)
-  AC(T102[:, 0, :], T60[:].rearrange(S8)[:, 0, 0:512].bitcast(E4), ACT.Copy, scale=T2[:, 2, 0:1])
-  T100 = PP([128, 512], F, tag='h_2', bufs=1)
-  M(T100[:], T83, T84, 256, T26, T27, 1, 1)
-  T103 = AQ.tile([128, 4, 4, 256], U8, tag='wl_raw_1', bufs=1)
-  DM(out=T103[:, 0, :, :], in_=wl_bytes[0:512, :].rearrange(S4, t=4, v=4, h=2)[:, 0, :, 1, :])
-  DM(out=T103[:, 1, :, :], in_=wl_bytes[0:512, :].rearrange(S4, t=4, v=4, h=2)[:, 1, :, 1, :])
-  DM(out=T103[:, 2, :, :], in_=wl_bytes[0:512, :].rearrange(S4, t=4, v=4, h=2)[:, 2, :, 1, :])
-  DM(out=T103[:, 3, :, :], in_=wl_bytes[0:512, :].rearrange(S4, t=4, v=4, h=2)[:, 3, :, 1, :])
-  T94 = PP([128, 256, 4], B, tag='l_0', bufs=1)
-  MT(T94[:, 0:128, :], lhsT=T3[:], rhs=T92[:, :, 0:128].rearrange(S13), start=True, stop=True)
-  T97 = AQ.tile([128, 4, 512], F, tag='f8_2', bufs=1)
-  AC(T97[:, 0, :], T98[:], ACT.Exp)
-  MT(T94[:, 128:256, :], lhsT=T3[:], rhs=T92[:, :, 128:256].rearrange(S13), start=True, stop=True)
-  T95 = PP([128, 256, 4], B, tag='l_1', bufs=1)
-  MT(T95[:, 0:128, :], lhsT=T3[:], rhs=T92[:, :, 256:384].rearrange(S13), start=True, stop=True)
-  T93 = AQ.tile([128, 512, 4], B, tag='grouped_0', bufs=1, align_bytes=64)
-  SC(T93[:, 0:256, :], T94[:])
-  MT(T95[:, 128:256, :], lhsT=T3[:], rhs=T92[:, :, 384:512].rearrange(S13), start=True, stop=True)
-  T101 = PP([128, 512], F, tag='h_3', bufs=1)
-  M(T101[:], T83, T84, 384, T26, T27, 1, 1)
+  Q(T26[:, 0:512], T27[:, 0:512], T82[:].rearrange(S9))
+  AC(T94[:, 2, :], T60[:].rearrange(S8)[:, 2, 0:512].bitcast(E4), ACT.Copy, scale=T2[:, 2, 2:3])
+  T87 = AQ.tile([128, 512, 4], B, tag='grouped_0', bufs=1, align_bytes=64)
+  ve.tensor_copy(out=T87[:].rearrange(S13, i=4), in_=T86[:].rearrange(S14, i=4))
+  T90 = PP([128, 512], F, tag='h_0', bufs=1)
+  M(T90[:], T79, T80, 0, T26, T27, 1, 1)
+  AC(T94[:, 3, :], T60[:].rearrange(S8)[:, 3, 0:512].bitcast(E4), ACT.Copy, scale=T2[:, 2, 3:4])
+  T91 = PP([128, 512], F, tag='h_1', bufs=1)
+  M(T91[:], T79, T80, 128, T26, T27, 1, 1)
+  T89 = AQ.tile([128, 4, 512], F, tag='f8_2', bufs=1)
+  AC(T89[:, 0, :], T90[:], ACT.Exp)
+  T92 = PP([128, 512], F, tag='h_2', bufs=1)
+  M(T92[:], T79, T80, 256, T26, T27, 1, 1)
+  T93 = PP([128, 512], F, tag='h_3', bufs=1)
+  M(T93[:], T79, T80, 384, T26, T27, 1, 1)
+  T88 = AQ.tile([128, 512, 4], B, tag='eg', bufs=1, align_bytes=64)
+  ST(out=T88[:], in0=T71[:].rearrange(S15), scalar=-1.0, in1=T6[:, 1:2, :].broadcast_to([128, 512, 4]), op0=ALU.add, op1=ALU.mult)
+  AC(T89[:, 1, :], T91[:], ACT.Exp)
+  AC(T89[:, 2, :], T92[:], ACT.Exp)
+  AC(T89[:, 3, :], T93[:], ACT.Exp)
+  T99 = AQ.tile([128, 512, 4], B, tag='xg', bufs=1, align_bytes=64)
+  SC(T99[:].rearrange(S10).bitcast(F).rearrange(S11, u=2)[:, 0:256, :], T100[:].rearrange(S12))
   T21 = KP([128, 2048], U, tag='wlq1_codes', bufs=1, align_bytes=64)
   T22 = KP([128, 2048], U8, tag='wlq1_scales', bufs=1, align_bytes=64)
-  Q(T21[:, 0:512], T22[:, 0:512], T89[:].rearrange(S9))
-  SC(T93[:, 256:512, :], T95[:])
-  T109 = PP([128, 2, 256], F, tag='l_0', bufs=1)
-  TR(T109[:, 0, 0:128], T34[:].bitcast(F)[:, 2, 0::2], T0[:])
-  TR(T109[:, 0, 128:256], T34[:].bitcast(F)[:, 3, 0::2], T0[:])
-  TR(T109[:, 1, 0:128], T34[:].bitcast(F)[:, 2, 1::2], T0[:])
+  Q(T21[:, 0:512], T22[:, 0:512], T85[:].rearrange(S9))
+  SC(T99[:].rearrange(S10).bitcast(F).rearrange(S11, u=2)[:, 256:512, :], T101[:].rearrange(S12))
+  T129 = PP([128, 512], F, tag='l_0', bufs=1)
+  M(T129[:], T12, T13, 256, T8, T9, 1, 0)
   T19 = KP([128, 512], U, tag='eq1_codes', bufs=1, align_bytes=64)
   T20 = KP([128, 512], U8, tag='eq1_scales', bufs=1, align_bytes=64)
-  Q(T19[:, 0:512], T20[:, 0:512], T96[:].rearrange(S9))
-  TR(T109[:, 1, 128:256], T34[:].bitcast(F)[:, 3, 1::2], T0[:])
-  AC(T97[:, 1, :], T99[:], ACT.Exp)
-  Q(T21[:, 512:1024], T22[:, 512:1024], T93[:].rearrange(S9))
-  AC(T97[:, 2, :], T100[:], ACT.Exp)
-  T106 = AQ.tile([128, 512, 4], B, tag='w1g', bufs=1, align_bytes=64)
-  ve.tensor_copy(out=T106[:].rearrange(S6, t=4), in_=T81[:].rearrange(S7, t=4))
-  AC(T97[:, 3, :], T101[:], ACT.Exp)
-  AC(T102[:, 1, :], T60[:].rearrange(S8)[:, 1, 0:512].bitcast(E4), ACT.Copy, scale=T2[:, 2, 1:2])
-  AC(T102[:, 2, :], T60[:].rearrange(S8)[:, 2, 0:512].bitcast(E4), ACT.Copy, scale=T2[:, 2, 2:3])
-  ve.tensor_scalar(out=T97[:], in0=T97[:], scalar1=1.0, scalar2=None, op0=ALU.min)
-  AC(T102[:, 3, :], T60[:].rearrange(S8)[:, 3, 0:512].bitcast(E4), ACT.Copy, scale=T2[:, 2, 3:4])
-  T107 = AQ.tile([128, 512, 4], B, tag='xg', bufs=1, align_bytes=64)
-  SC(T107[:].rearrange(S10).bitcast(F).rearrange(S11, u=2)[:, 0:256, :], T108[:].rearrange(S12))
-  T111 = PP([128, 256, 4], B, tag='l_1', bufs=1)
-  MT(T111[:, 0:128, :], lhsT=T3[:], rhs=T102[:, :, 0:128].rearrange(S13), start=True, stop=True)
-  T104 = AQ.tile([128, 512], U, tag='w1q_codes_1', bufs=1, align_bytes=64)
-  T105 = AQ.tile([128, 512], U8, tag='w1q_scales_1', bufs=1, align_bytes=64)
-  Q(T104[:, 0:512], T105[:, 0:512], T106[:].rearrange(S9))
-  MT(T111[:, 128:256, :], lhsT=T3[:], rhs=T102[:, :, 128:256].rearrange(S13), start=True, stop=True)
-  SC(T107[:].rearrange(S10).bitcast(F).rearrange(S11, u=2)[:, 256:512, :], T109[:].rearrange(S12))
-  ST(out=T97[:, 0, :], in0=T98[:], scalar=1.0, in1=T97[:, 0, :], op0=ALU.add, op1=ALU.max)
-  T112 = PP([128, 256, 4], B, tag='l_2', bufs=1)
-  MT(T112[:, 0:128, :], lhsT=T3[:], rhs=T102[:, :, 256:384].rearrange(S13), start=True, stop=True)
-  MT(T112[:, 128:256, :], lhsT=T3[:], rhs=T102[:, :, 384:512].rearrange(S13), start=True, stop=True)
-  T110 = AQ.tile([128, 512, 4], B, tag='grouped_1', bufs=1, align_bytes=64)
-  SC(T110[:, 0:256, :], T111[:])
-  ST(out=T97[:, 1, :], in0=T99[:], scalar=1.0, in1=T97[:, 1, :], op0=ALU.add, op1=ALU.max)
-  SC(T110[:, 256:512, :], T112[:])
-  ST(out=T97[:, 2, :], in0=T100[:], scalar=1.0, in1=T97[:, 2, :], op0=ALU.add, op1=ALU.max)
-  T113 = AQ.tile([128, 4, 512], B, tag='wl_wide_1', bufs=1)
-  AC(T113[:, 0, :], T60[:].rearrange(S8)[:, 0, 512:1024].bitcast(E4), ACT.Copy, scale=T2[:, 2, 0:1])
-  ST(out=T97[:, 3, :], in0=T101[:], scalar=1.0, in1=T97[:, 3, :], op0=ALU.add, op1=ALU.max)
-  AC(T113[:, 1, :], T60[:].rearrange(S8)[:, 1, 512:1024].bitcast(E4), ACT.Copy, scale=T2[:, 2, 1:2])
+  Q(T19[:, 0:512], T20[:, 0:512], T88[:].rearrange(S9))
+  T102 = AQ.tile([128, 512, 4], B, tag='grouped_1', bufs=1, align_bytes=64)
+  SC(T102[:].rearrange(S13, i=4), T94[:].rearrange(S14, i=4))
+  T130 = PP([128, 512], F, tag='l_1', bufs=1)
+  M(T130[:], T12, T13, 512, T8, T9, 1, 0)
+  M(T128[:], T21, T22, 0, T17, T18, 0, 0)
+  Q(T21[:, 512:1024], T22[:, 512:1024], T87[:].rearrange(S9))
+  M(T129[:], T21, T22, 256, T17, T18, 0, 0)
+  T98 = AQ.tile([128, 512, 4], B, tag='w1g', bufs=1, align_bytes=64)
+  ve.tensor_copy(out=T98[:].rearrange(S6, t=4), in_=T77[:].rearrange(S7, t=4))
+  M(T130[:], T21, T22, 512, T17, T18, 0, 0)
+  ve.tensor_scalar(out=T89[:], in0=T89[:], scalar1=1.0, scalar2=None, op0=ALU.min)
+  T103 = AQ.tile([128, 4, 512], B, tag='wl_wide_1', bufs=1)
+  AC(T103[:, 0, :], T60[:].rearrange(S8)[:, 0, 512:1024].bitcast(E4), ACT.Copy, scale=T2[:, 2, 0:1])
+  AC(T103[:, 1, :], T60[:].rearrange(S8)[:, 1, 512:1024].bitcast(E4), ACT.Copy, scale=T2[:, 2, 1:2])
+  T96 = AQ.tile([128, 512], U, tag='w1q_codes_1', bufs=1, align_bytes=64)
+  T97 = AQ.tile([128, 512], U8, tag='w1q_scales_1', bufs=1, align_bytes=64)
+  Q(T96[:, 0:512], T97[:, 0:512], T98[:].rearrange(S9))
+  AC(T103[:, 2, :], T60[:].rearrange(S8)[:, 2, 512:1024].bitcast(E4), ACT.Copy, scale=T2[:, 2, 2:3])
+  ST(out=T89[:, 0, :], in0=T90[:], scalar=1.0, in1=T89[:, 0, :], op0=ALU.add, op1=ALU.max)
+  AC(T103[:, 3, :], T60[:].rearrange(S8)[:, 3, 512:1024].bitcast(E4), ACT.Copy, scale=T2[:, 2, 3:4])
+  ST(out=T89[:, 1, :], in0=T91[:], scalar=1.0, in1=T89[:, 1, :], op0=ALU.add, op1=ALU.max)
+  T111 = AQ.tile([128, 4, 512], B, tag='wl_wide_0', bufs=1)
+  AC(T111[:, 0, :], T78[:].rearrange(S8)[:, 0, 0:512].bitcast(E4), ACT.Copy, scale=T2[:, 3, 0:1])
+  T112 = AQ.tile([128, 4, 4, 256], U8, tag='wl_raw_2', bufs=1)
+  DM(out=T112[:, 0, :, :], in_=wl_bytes[512:1024, :].rearrange(S4, t=4, v=4, h=2)[:, 0, :, 1, :])
+  DM(out=T112[:, 1, :, :], in_=wl_bytes[512:1024, :].rearrange(S4, t=4, v=4, h=2)[:, 1, :, 1, :])
+  DM(out=T112[:, 2, :, :], in_=wl_bytes[512:1024, :].rearrange(S4, t=4, v=4, h=2)[:, 2, :, 1, :])
+  DM(out=T112[:, 3, :, :], in_=wl_bytes[512:1024, :].rearrange(S4, t=4, v=4, h=2)[:, 3, :, 1, :])
+  ST(out=T89[:, 2, :], in0=T92[:], scalar=1.0, in1=T89[:, 2, :], op0=ALU.add, op1=ALU.max)
+  AC(T111[:, 1, :], T78[:].rearrange(S8)[:, 1, 0:512].bitcast(E4), ACT.Copy, scale=T2[:, 3, 1:2])
+  ST(out=T89[:, 3, :], in0=T93[:], scalar=1.0, in1=T89[:, 3, :], op0=ALU.add, op1=ALU.max)
+  AC(T111[:, 2, :], T78[:].rearrange(S8)[:, 2, 0:512].bitcast(E4), ACT.Copy, scale=T2[:, 3, 2:3])
   T35 = KP([128, 512], U, tag='xq3_codes', bufs=1, align_bytes=64)
   T36 = KP([128, 512], U8, tag='xq3_scales', bufs=1, align_bytes=64)
-  Q(T35[:, 0:512], T36[:, 0:512], T107[:].rearrange(S9))
-  AC(T113[:, 2, :], T60[:].rearrange(S8)[:, 2, 512:1024].bitcast(E4), ACT.Copy, scale=T2[:, 2, 2:3])
-  T117 = AQ.tile([128, 512, 4], B, tag='eg', bufs=1, align_bytes=64)
-  ST(out=T117[:], in0=T97[:].rearrange(S14), scalar=-1.0, in1=T6[:, 2:3, :].broadcast_to([128, 512, 4]), op0=ALU.add, op1=ALU.mult)
-  T119 = PP([128, 512], F, tag='h_0', bufs=1)
-  M(T119[:], T104, T105, 0, T35, T36, 1, 1)
-  AC(T113[:, 3, :], T60[:].rearrange(S8)[:, 3, 512:1024].bitcast(E4), ACT.Copy, scale=T2[:, 2, 3:4])
-  T120 = PP([128, 512], F, tag='h_1', bufs=1)
-  M(T120[:], T104, T105, 128, T35, T36, 1, 1)
-  T121 = PP([128, 512], F, tag='h_2', bufs=1)
-  M(T121[:], T104, T105, 256, T35, T36, 1, 1)
-  T118 = AQ.tile([128, 4, 512], F, tag='f8_3', bufs=1)
-  AC(T118[:, 0, :], T119[:], ACT.Exp)
-  T124 = AQ.tile([128, 4, 4, 256], U8, tag='wl_raw_2', bufs=1)
-  DM(out=T124[:, 0, :, :], in_=wl_bytes[512:1024, :].rearrange(S4, t=4, v=4, h=2)[:, 0, :, 1, :])
-  T115 = PP([128, 256, 4], B, tag='l_0', bufs=1)
-  MT(T115[:, 0:128, :], lhsT=T3[:], rhs=T113[:, :, 0:128].rearrange(S13), start=True, stop=True)
-  DM(out=T124[:, 1, :, :], in_=wl_bytes[512:1024, :].rearrange(S4, t=4, v=4, h=2)[:, 1, :, 1, :])
-  DM(out=T124[:, 2, :, :], in_=wl_bytes[512:1024, :].rearrange(S4, t=4, v=4, h=2)[:, 2, :, 1, :])
-  DM(out=T124[:, 3, :, :], in_=wl_bytes[512:1024, :].rearrange(S4, t=4, v=4, h=2)[:, 3, :, 1, :])
-  MT(T115[:, 128:256, :], lhsT=T3[:], rhs=T113[:, :, 128:256].rearrange(S13), start=True, stop=True)
-  AC(T118[:, 1, :], T120[:], ACT.Exp)
-  T116 = PP([128, 256, 4], B, tag='l_1', bufs=1)
-  MT(T116[:, 0:128, :], lhsT=T3[:], rhs=T113[:, :, 256:384].rearrange(S13), start=True, stop=True)
-  MT(T116[:, 128:256, :], lhsT=T3[:], rhs=T113[:, :, 384:512].rearrange(S13), start=True, stop=True)
-  T114 = AQ.tile([128, 512, 4], B, tag='grouped_2', bufs=1, align_bytes=64)
-  SC(T114[:, 0:256, :], T115[:])
-  T122 = PP([128, 512], F, tag='h_3', bufs=1)
-  M(T122[:], T104, T105, 384, T35, T36, 1, 1)
+  Q(T35[:, 0:512], T36[:, 0:512], T99[:].rearrange(S9))
+  AC(T111[:, 3, :], T78[:].rearrange(S8)[:, 3, 0:512].bitcast(E4), ACT.Copy, scale=T2[:, 3, 3:4])
+  T104 = AQ.tile([128, 512, 4], B, tag='grouped_2', bufs=1, align_bytes=64)
+  ve.tensor_copy(out=T104[:].rearrange(S13, i=4), in_=T103[:].rearrange(S14, i=4))
+  T113 = AQ.tile([128, 512, 4], B, tag='grouped_0', bufs=1, align_bytes=64)
+  SC(T113[:].rearrange(S13, i=4), T111[:].rearrange(S14, i=4))
+  T107 = PP([128, 512], F, tag='h_0', bufs=1)
+  M(T107[:], T96, T97, 0, T35, T36, 1, 1)
+  T108 = PP([128, 512], F, tag='h_1', bufs=1)
+  M(T108[:], T96, T97, 128, T35, T36, 1, 1)
+  T109 = PP([128, 512], F, tag='h_2', bufs=1)
+  M(T109[:], T96, T97, 256, T35, T36, 1, 1)
+  T110 = PP([128, 512], F, tag='h_3', bufs=1)
+  M(T110[:], T96, T97, 384, T35, T36, 1, 1)
+  T105 = AQ.tile([128, 512, 4], B, tag='eg', bufs=1, align_bytes=64)
+  ST(out=T105[:], in0=T89[:].rearrange(S15), scalar=-1.0, in1=T6[:, 2:3, :].broadcast_to([128, 512, 4]), op0=ALU.add, op1=ALU.mult)
+  T106 = AQ.tile([128, 4, 512], F, tag='f8_3', bufs=1)
+  AC(T106[:, 0, :], T107[:], ACT.Exp)
+  AC(T106[:, 1, :], T108[:], ACT.Exp)
   T30 = KP([128, 2048], U, tag='wlq2_codes', bufs=1, align_bytes=64)
   T31 = KP([128, 2048], U8, tag='wlq2_scales', bufs=1, align_bytes=64)
-  Q(T30[:, 0:512], T31[:, 0:512], T110[:].rearrange(S9))
-  SC(T114[:, 256:512, :], T116[:])
+  Q(T30[:, 0:512], T31[:, 0:512], T102[:].rearrange(S9))
+  AC(T106[:, 2, :], T109[:], ACT.Exp)
   T28 = KP([128, 512], U, tag='eq2_codes', bufs=1, align_bytes=64)
   T29 = KP([128, 512], U8, tag='eq2_scales', bufs=1, align_bytes=64)
-  Q(T28[:, 0:512], T29[:, 0:512], T117[:].rearrange(S9))
-  AC(T118[:, 2, :], T121[:], ACT.Exp)
-  Q(T30[:, 512:1024], T31[:, 512:1024], T114[:].rearrange(S9))
-  AC(T118[:, 3, :], T122[:], ACT.Exp)
-  T134 = KP([128, 16], F, tag='gs2', bufs=1)
-  ve.tensor_scalar(out=T134[:], in0=T133[:, 0:16], scalar1=2.0, scalar2=None, op0=ALU.mult)
-  T188 = PP([128, 2, 512], B, tag='x', bufs=1)
-  TR(T188[:, 0, 0:128], T7[:, 0, 0:128], T3[:])
-  T123 = AQ.tile([128, 4, 512], B, tag='wl_wide_0', bufs=1)
-  AC(T123[:, 0, :], T82[:].rearrange(S8)[:, 0, 0:512].bitcast(E4), ACT.Copy, scale=T2[:, 3, 0:1])
-  ve.tensor_scalar(out=T118[:], in0=T118[:], scalar1=1.0, scalar2=None, op0=ALU.min)
-  TR(T188[:, 0, 128:256], T7[:, 1, 0:128], T3[:])
-  TR(T188[:, 0, 256:384], T7[:, 2, 0:128], T3[:])
-  TR(T188[:, 0, 384:512], T7[:, 3, 0:128], T3[:])
-  TR(T188[:, 1, 0:128], T7[:, 0, 128:256], T3[:])
-  TR(T188[:, 1, 128:256], T7[:, 1, 128:256], T3[:])
-  TR(T188[:, 1, 256:384], T7[:, 2, 128:256], T3[:])
-  TR(T188[:, 1, 384:512], T7[:, 3, 128:256], T3[:])
-  AC(T123[:, 1, :], T82[:].rearrange(S8)[:, 1, 0:512].bitcast(E4), ACT.Copy, scale=T2[:, 3, 1:2])
-  AC(T123[:, 2, :], T82[:].rearrange(S8)[:, 2, 0:512].bitcast(E4), ACT.Copy, scale=T2[:, 3, 2:3])
-  ST(out=T118[:, 0, :], in0=T119[:], scalar=1.0, in1=T118[:, 0, :], op0=ALU.add, op1=ALU.max)
-  AC(T123[:, 3, :], T82[:].rearrange(S8)[:, 3, 0:512].bitcast(E4), ACT.Copy, scale=T2[:, 3, 3:4])
-  ST(out=T118[:, 1, :], in0=T120[:], scalar=1.0, in1=T118[:, 1, :], op0=ALU.add, op1=ALU.max)
-  T128 = AQ.tile([128, 4, 512], B, tag='wl_wide_1', bufs=1)
-  AC(T128[:, 0, :], T82[:].rearrange(S8)[:, 0, 512:1024].bitcast(E4), ACT.Copy, scale=T2[:, 3, 0:1])
-  T126 = PP([128, 256, 4], B, tag='l_2', bufs=1)
-  MT(T126[:, 0:128, :], lhsT=T3[:], rhs=T123[:, :, 0:128].rearrange(S13), start=True, stop=True)
-  ST(out=T118[:, 2, :], in0=T121[:], scalar=1.0, in1=T118[:, 2, :], op0=ALU.add, op1=ALU.max)
-  MT(T126[:, 128:256, :], lhsT=T3[:], rhs=T123[:, :, 128:256].rearrange(S13), start=True, stop=True)
-  AC(T128[:, 1, :], T82[:].rearrange(S8)[:, 1, 512:1024].bitcast(E4), ACT.Copy, scale=T2[:, 3, 1:2])
-  T127 = PP([128, 256, 4], B, tag='l_0', bufs=1)
-  MT(T127[:, 0:128, :], lhsT=T3[:], rhs=T123[:, :, 256:384].rearrange(S13), start=True, stop=True)
-  ST(out=T118[:, 3, :], in0=T122[:], scalar=1.0, in1=T118[:, 3, :], op0=ALU.add, op1=ALU.max)
-  MT(T127[:, 128:256, :], lhsT=T3[:], rhs=T123[:, :, 384:512].rearrange(S13), start=True, stop=True)
-  T125 = AQ.tile([128, 512, 4], B, tag='grouped_0', bufs=1, align_bytes=64)
-  SC(T125[:, 0:256, :], T126[:])
-  T132 = AQ.tile([128, 512, 4], B, tag='eg', bufs=1, align_bytes=64)
-  ST(out=T132[:], in0=T118[:].rearrange(S14), scalar=-1.0, in1=T6[:, 3:4, :].broadcast_to([128, 512, 4]), op0=ALU.add, op1=ALU.mult)
-  SC(T125[:, 256:512, :], T127[:])
-  AC(T128[:, 2, :], T82[:].rearrange(S8)[:, 2, 512:1024].bitcast(E4), ACT.Copy, scale=T2[:, 3, 2:3])
-  T144 = PP([128, 512], F, tag='l_0', bufs=1)
-  M(T144[:], T12, T13, 0, T8, T9, 1, 0)
-  M(T144[:], T21, T22, 0, T17, T18, 0, 0)
-  AC(T128[:, 3, :], T82[:].rearrange(S8)[:, 3, 512:1024].bitcast(E4), ACT.Copy, scale=T2[:, 3, 3:4])
-  M(T144[:], T30, T31, 0, T26, T27, 0, 0)
-  T142 = AQ.tile([128, 4, 512], B, tag='wl_wide_0', bufs=1)
-  AC(T142[:, 0, :], T103[:].rearrange(S8)[:, 0, 0:512].bitcast(E4), ACT.Copy, scale=T2[:, 0, 0:1])
-  T130 = PP([128, 256, 4], B, tag='l_1', bufs=1)
-  MT(T130[:, 0:128, :], lhsT=T3[:], rhs=T128[:, :, 0:128].rearrange(S13), start=True, stop=True)
-  T136 = AQ.tile([128, 4, 4, 256], U8, tag='wl_raw_0', bufs=1)
-  DM(out=T136[:, 0, :, :], in_=wl_bytes[1024:1536, :].rearrange(S4, t=4, v=4, h=2)[:, 0, :, 1, :])
-  DM(out=T136[:, 1, :, :], in_=wl_bytes[1024:1536, :].rearrange(S4, t=4, v=4, h=2)[:, 1, :, 1, :])
-  DM(out=T136[:, 2, :, :], in_=wl_bytes[1024:1536, :].rearrange(S4, t=4, v=4, h=2)[:, 2, :, 1, :])
-  DM(out=T136[:, 3, :, :], in_=wl_bytes[1024:1536, :].rearrange(S4, t=4, v=4, h=2)[:, 3, :, 1, :])
+  Q(T28[:, 0:512], T29[:, 0:512], T105[:].rearrange(S9))
+  M(T128[:], T30, T31, 0, T26, T27, 0, 0)
+  AC(T106[:, 3, :], T110[:], ACT.Exp)
+  M(T129[:], T30, T31, 256, T26, T27, 0, 0)
+  Q(T30[:, 512:1024], T31[:, 512:1024], T104[:].rearrange(S9))
+  T114 = AQ.tile([128, 4, 512], B, tag='wl_wide_1', bufs=1)
+  AC(T114[:, 0, :], T78[:].rearrange(S8)[:, 0, 512:1024].bitcast(E4), ACT.Copy, scale=T2[:, 3, 0:1])
+  ve.tensor_scalar(out=T106[:], in0=T106[:], scalar1=1.0, scalar2=None, op0=ALU.min)
+  M(T130[:], T30, T31, 512, T26, T27, 0, 0)
+  AC(T114[:, 1, :], T78[:].rearrange(S8)[:, 1, 512:1024].bitcast(E4), ACT.Copy, scale=T2[:, 3, 1:2])
+  AC(T114[:, 2, :], T78[:].rearrange(S8)[:, 2, 512:1024].bitcast(E4), ACT.Copy, scale=T2[:, 3, 2:3])
   T39 = KP([128, 2048], U, tag='wlq3_codes', bufs=1, align_bytes=64)
   T40 = KP([128, 2048], U8, tag='wlq3_scales', bufs=1, align_bytes=64)
-  Q(T39[:, 0:512], T40[:, 0:512], T125[:].rearrange(S9))
-  MT(T130[:, 128:256, :], lhsT=T3[:], rhs=T128[:, :, 128:256].rearrange(S13), start=True, stop=True)
-  AC(T142[:, 1, :], T103[:].rearrange(S8)[:, 1, 0:512].bitcast(E4), ACT.Copy, scale=T2[:, 0, 1:2])
-  T131 = PP([128, 256, 4], B, tag='l_2', bufs=1)
-  MT(T131[:, 0:128, :], lhsT=T3[:], rhs=T128[:, :, 256:384].rearrange(S13), start=True, stop=True)
-  MT(T131[:, 128:256, :], lhsT=T3[:], rhs=T128[:, :, 384:512].rearrange(S13), start=True, stop=True)
+  Q(T39[:, 0:512], T40[:, 0:512], T113[:].rearrange(S9))
+  AC(T114[:, 3, :], T78[:].rearrange(S8)[:, 3, 512:1024].bitcast(E4), ACT.Copy, scale=T2[:, 3, 3:4])
+  ST(out=T106[:, 0, :], in0=T107[:], scalar=1.0, in1=T106[:, 0, :], op0=ALU.add, op1=ALU.max)
+  M(T128[:], T39, T40, 0, T35, T36, 0, 1)
+  T126 = AQ.tile([128, 4, 512], B, tag='wl_wide_0', bufs=1)
+  AC(T126[:, 0, :], T95[:].rearrange(S8)[:, 0, 0:512].bitcast(E4), ACT.Copy, scale=T2[:, 0, 0:1])
+  T120 = AQ.tile([128, 4, 4, 256], U8, tag='wl_raw_0', bufs=1)
+  DM(out=T120[:, 0, :, :], in_=wl_bytes[1024:1536, :].rearrange(S4, t=4, v=4, h=2)[:, 0, :, 1, :])
+  DM(out=T120[:, 1, :, :], in_=wl_bytes[1024:1536, :].rearrange(S4, t=4, v=4, h=2)[:, 1, :, 1, :])
+  DM(out=T120[:, 2, :, :], in_=wl_bytes[1024:1536, :].rearrange(S4, t=4, v=4, h=2)[:, 2, :, 1, :])
+  M(T129[:], T39, T40, 256, T35, T36, 0, 1)
+  DM(out=T120[:, 3, :, :], in_=wl_bytes[1024:1536, :].rearrange(S4, t=4, v=4, h=2)[:, 3, :, 1, :])
+  ST(out=T106[:, 1, :], in0=T108[:], scalar=1.0, in1=T106[:, 1, :], op0=ALU.add, op1=ALU.max)
+  T115 = AQ.tile([128, 512, 4], B, tag='grouped_1', bufs=1, align_bytes=64)
+  SC(T115[:].rearrange(S13, i=4), T114[:].rearrange(S14, i=4))
+  ST(out=T106[:, 2, :], in0=T109[:], scalar=1.0, in1=T106[:, 2, :], op0=ALU.add, op1=ALU.max)
+  ST(out=T106[:, 3, :], in0=T110[:], scalar=1.0, in1=T106[:, 3, :], op0=ALU.add, op1=ALU.max)
+  T118 = KP([128, 16], F, tag='gs2', bufs=1)
+  ve.tensor_scalar(out=T118[:], in0=T117[:, 0:16], scalar1=2.0, scalar2=None, op0=ALU.mult)
+  T116 = AQ.tile([128, 512, 4], B, tag='eg', bufs=1, align_bytes=64)
+  ST(out=T116[:], in0=T106[:].rearrange(S15), scalar=-1.0, in1=T6[:, 3:4, :].broadcast_to([128, 512, 4]), op0=ALU.add, op1=ALU.mult)
+  T170 = PP([128, 2, 512], B, tag='x', bufs=1)
+  TR(T170[:, 0, 0:128], T7[:, 0, 0:128], T3[:])
+  TR(T170[:, 0, 128:256], T7[:, 1, 0:128], T3[:])
+  TR(T170[:, 0, 256:384], T7[:, 2, 0:128], T3[:])
+  TR(T170[:, 0, 384:512], T7[:, 3, 0:128], T3[:])
+  TR(T170[:, 1, 0:128], T7[:, 0, 128:256], T3[:])
+  TR(T170[:, 1, 128:256], T7[:, 1, 128:256], T3[:])
+  TR(T170[:, 1, 256:384], T7[:, 2, 128:256], T3[:])
+  TR(T170[:, 1, 384:512], T7[:, 3, 128:256], T3[:])
+  AC(T126[:, 1, :], T95[:].rearrange(S8)[:, 1, 0:512].bitcast(E4), ACT.Copy, scale=T2[:, 0, 1:2])
+  AC(T126[:, 2, :], T95[:].rearrange(S8)[:, 2, 0:512].bitcast(E4), ACT.Copy, scale=T2[:, 0, 2:3])
+  AC(T126[:, 3, :], T95[:].rearrange(S8)[:, 3, 0:512].bitcast(E4), ACT.Copy, scale=T2[:, 0, 3:4])
+  Q(T39[:, 512:1024], T40[:, 512:1024], T115[:].rearrange(S9))
+  T127 = AQ.tile([128, 512], F, tag='l0_0', bufs=1)
+  SC(T127[:], T128[:])
   T37 = KP([128, 512], U, tag='eq3_codes', bufs=1, align_bytes=64)
   T38 = KP([128, 512], U8, tag='eq3_scales', bufs=1, align_bytes=64)
-  Q(T37[:, 0:512], T38[:, 0:512], T132[:].rearrange(S9))
-  T129 = AQ.tile([128, 512, 4], B, tag='grouped_1', bufs=1, align_bytes=64)
-  SC(T129[:, 0:256, :], T130[:])
-  M(T144[:], T39, T40, 0, T35, T36, 0, 1)
-  SC(T129[:, 256:512, :], T131[:])
-  T145 = PP([128, 512], F, tag='l_1', bufs=1)
-  M(T145[:], T12, T13, 256, T8, T9, 1, 0)
-  M(T145[:], T21, T22, 256, T17, T18, 0, 0)
-  AC(T142[:, 2, :], T103[:].rearrange(S8)[:, 2, 0:512].bitcast(E4), ACT.Copy, scale=T2[:, 0, 2:3])
-  Q(T39[:, 512:1024], T40[:, 512:1024], T129[:].rearrange(S9))
-  M(T145[:], T30, T31, 256, T26, T27, 0, 0)
-  M(T145[:], T39, T40, 256, T35, T36, 0, 1)
-  AC(T142[:, 3, :], T103[:].rearrange(S8)[:, 3, 0:512].bitcast(E4), ACT.Copy, scale=T2[:, 0, 3:4])
-  T146 = PP([128, 512], F, tag='l_2', bufs=1)
-  M(T146[:], T12, T13, 512, T8, T9, 1, 0)
-  M(T146[:], T21, T22, 512, T17, T18, 0, 0)
-  T143 = AQ.tile([128, 512], F, tag='l0_0', bufs=1)
-  SC(T143[:], T144[:])
-  M(T146[:], T30, T31, 512, T26, T27, 0, 0)
-  T150 = AQ.tile([128, 512, 4], B, tag='grouped_2', bufs=1, align_bytes=64)
-  ve.tensor_copy(out=T150[:], in_=T142[:].rearrange(S13))
-  M(T146[:], T39, T40, 512, T35, T36, 0, 1)
-  T148 = AQ.tile([128, 4, 512], B, tag='wl_wide_1', bufs=1)
-  AC(T148[:, 0, :], T103[:].rearrange(S8)[:, 0, 512:1024].bitcast(E4), ACT.Copy, scale=T2[:, 0, 0:1])
-  T147 = PP([128, 512], F, tag='l_0', bufs=1)
-  M(T147[:], T12, T13, 768, T8, T9, 1, 0)
-  M(T147[:], T21, T22, 768, T17, T18, 0, 0)
-  AC(T148[:, 1, :], T103[:].rearrange(S8)[:, 1, 512:1024].bitcast(E4), ACT.Copy, scale=T2[:, 0, 1:2])
-  M(T147[:], T30, T31, 768, T26, T27, 0, 0)
-  T149 = AQ.tile([128, 512], F, tag='top_0', bufs=1)
-  TT(out=T149[:], in0=T145[:], in1=T143[:], op=ALU.max)
-  M(T147[:], T39, T40, 768, T35, T36, 0, 1)
-  AC(T148[:, 2, :], T103[:].rearrange(S8)[:, 2, 512:1024].bitcast(E4), ACT.Copy, scale=T2[:, 0, 2:3])
-  Q(T12[:, 1024:1536], T13[:, 1024:1536], T150[:].rearrange(S9))
-  AC(T148[:, 3, :], T103[:].rearrange(S8)[:, 3, 512:1024].bitcast(E4), ACT.Copy, scale=T2[:, 0, 3:4])
-  TT(out=T149[:], in0=T146[:], in1=T149[:], op=ALU.max)
-  T157 = AQ.tile([128, 4, 512], B, tag='wl_wide_0', bufs=1)
-  AC(T157[:, 0, :], T124[:].rearrange(S8)[:, 0, 0:512].bitcast(E4), ACT.Copy, scale=T2[:, 1, 0:1])
-  T137 = AQ.tile([128, 4, 4, 256], U8, tag='wl_raw_1', bufs=1)
-  DM(out=T137[:, 0, :, :], in_=wl_bytes[1536:2048, :].rearrange(S4, t=4, v=4, h=2)[:, 0, :, 1, :])
-  DM(out=T137[:, 1, :, :], in_=wl_bytes[1536:2048, :].rearrange(S4, t=4, v=4, h=2)[:, 1, :, 1, :])
-  DM(out=T137[:, 2, :, :], in_=wl_bytes[1536:2048, :].rearrange(S4, t=4, v=4, h=2)[:, 2, :, 1, :])
-  DM(out=T137[:, 3, :, :], in_=wl_bytes[1536:2048, :].rearrange(S4, t=4, v=4, h=2)[:, 3, :, 1, :])
-  T158 = AQ.tile([128, 512, 4], B, tag='grouped_0', bufs=1, align_bytes=64)
-  ve.tensor_copy(out=T158[:], in_=T148[:].rearrange(S13))
-  T138 = AQ.tile([128, 4, 512], B, tag='w2_raw_0', bufs=1)
-  DM(out=T138[:], in_=w2[0, :, 0:512].rearrange(S1, j=4))
-  T139 = AQ.tile([128, 4, 512], B, tag='w2_raw_1', bufs=1)
-  DM(out=T139[:], in_=w2[0, :, 512:1024].rearrange(S1, j=4))
-  T140 = AQ.tile([128, 4, 512], B, tag='w2_raw_2', bufs=1)
-  DM(out=T140[:], in_=w2[1, :, 0:512].rearrange(S1, j=4))
-  AC(T157[:, 1, :], T124[:].rearrange(S8)[:, 1, 0:512].bitcast(E4), ACT.Copy, scale=T2[:, 1, 1:2])
-  AC(T157[:, 2, :], T124[:].rearrange(S8)[:, 2, 0:512].bitcast(E4), ACT.Copy, scale=T2[:, 1, 2:3])
-  TT(out=T149[:], in0=T147[:], in1=T149[:], op=ALU.max)
-  AC(T157[:, 3, :], T124[:].rearrange(S8)[:, 3, 0:512].bitcast(E4), ACT.Copy, scale=T2[:, 1, 3:4])
-  Q(T12[:, 1536:2048], T13[:, 1536:2048], T158[:].rearrange(S9))
-  T159 = AQ.tile([128, 4, 512], B, tag='wl_wide_1', bufs=1)
-  AC(T159[:, 0, :], T124[:].rearrange(S8)[:, 0, 512:1024].bitcast(E4), ACT.Copy, scale=T2[:, 1, 0:1])
-  AC(T159[:, 1, :], T124[:].rearrange(S8)[:, 1, 512:1024].bitcast(E4), ACT.Copy, scale=T2[:, 1, 1:2])
-  T151 = AQ.tile([128, 4, 512], F, tag='f8_0', bufs=1)
-  TT(out=T151[:, 1, :], in0=T145[:], in1=T149[:], op=ALU.subtract)
-  AC(T159[:, 2, :], T124[:].rearrange(S8)[:, 2, 512:1024].bitcast(E4), ACT.Copy, scale=T2[:, 1, 2:3])
-  TT(out=T151[:, 2, :], in0=T146[:], in1=T149[:], op=ALU.subtract)
-  T153 = PP([128, 512], F, tag='l_1', bufs=1)
-  M(T153[:], T12, T13, 128, T8, T9, 1, 0)
-  M(T153[:], T21, T22, 128, T17, T18, 0, 0)
-  TT(out=T151[:, 3, :], in0=T147[:], in1=T149[:], op=ALU.subtract)
-  AC(T159[:, 3, :], T124[:].rearrange(S8)[:, 3, 512:1024].bitcast(E4), ACT.Copy, scale=T2[:, 1, 3:4])
-  M(T153[:], T30, T31, 128, T26, T27, 0, 0)
-  M(T153[:], T39, T40, 128, T35, T36, 0, 1)
-  TT(out=T151[:, 0, :], in0=T143[:], in1=T149[:], op=ALU.subtract)
-  T154 = PP([128, 512], F, tag='l_2', bufs=1)
-  M(T154[:], T12, T13, 384, T8, T9, 1, 0)
-  T152 = AQ.tile([128, 512], F, tag='l0_1', bufs=1)
-  SC(T152[:], T153[:])
-  M(T154[:], T21, T22, 384, T17, T18, 0, 0)
-  T160 = AQ.tile([128, 512, 4], B, tag='grouped_1', bufs=1, align_bytes=64)
-  ve.tensor_copy(out=T160[:], in_=T157[:].rearrange(S13))
-  M(T154[:], T30, T31, 384, T26, T27, 0, 0)
-  AC(T151[:], T151[:], ACT.Exp)
-  M(T154[:], T39, T40, 384, T35, T36, 0, 1)
-  T155 = PP([128, 512], F, tag='l_0', bufs=1)
-  M(T155[:], T12, T13, 640, T8, T9, 1, 0)
-  M(T155[:], T21, T22, 640, T17, T18, 0, 0)
-  M(T155[:], T30, T31, 640, T26, T27, 0, 0)
-  T161 = AQ.tile([128, 512], F, tag='top_1', bufs=1)
-  TT(out=T161[:], in0=T154[:], in1=T152[:], op=ALU.max)
-  M(T155[:], T39, T40, 640, T35, T36, 0, 1)
-  T156 = PP([128, 512], F, tag='l_1', bufs=1)
-  M(T156[:], T12, T13, 896, T8, T9, 1, 0)
-  T164 = AQ.tile([128, 512, 4], B, tag='grouped_2', bufs=1, align_bytes=64)
-  ve.tensor_copy(out=T164[:], in_=T159[:].rearrange(S13))
-  M(T156[:], T21, T22, 896, T17, T18, 0, 0)
-  M(T156[:], T30, T31, 896, T26, T27, 0, 0)
-  T163 = AQ.tile([128, 4, 512], B, tag='wl_wide_0', bufs=1)
-  AC(T163[:, 0, :], T136[:].rearrange(S8)[:, 0, 0:512].bitcast(E4), ACT.Copy, scale=T2[:, 2, 0:1])
-  T135 = KP([128, 4, 512], F, tag='den', bufs=1)
-  nc.gpsimd.tensor_tensor(out=T135[:, 0, :], in0=T151[:, 0, :], in1=T151[:, 1, :], op=ALU.add)
-  M(T156[:], T39, T40, 896, T35, T36, 0, 1)
-  AC(T163[:, 1, :], T136[:].rearrange(S8)[:, 1, 0:512].bitcast(E4), ACT.Copy, scale=T2[:, 2, 1:2])
-  TT(out=T161[:], in0=T155[:], in1=T161[:], op=ALU.max)
-  AC(T163[:, 2, :], T136[:].rearrange(S8)[:, 2, 0:512].bitcast(E4), ACT.Copy, scale=T2[:, 2, 2:3])
-  Q(T21[:, 1024:1536], T22[:, 1024:1536], T160[:].rearrange(S9))
-  nc.gpsimd.tensor_tensor(out=T135[:, 0, :], in0=T135[:, 0, :], in1=T151[:, 2, :], op=ALU.add)
-  AC(T163[:, 3, :], T136[:].rearrange(S8)[:, 3, 0:512].bitcast(E4), ACT.Copy, scale=T2[:, 2, 3:4])
-  TT(out=T161[:], in0=T156[:], in1=T161[:], op=ALU.max)
-  T165 = AQ.tile([128, 4, 512], B, tag='wl_wide_1', bufs=1)
-  AC(T165[:, 0, :], T136[:].rearrange(S8)[:, 0, 512:1024].bitcast(E4), ACT.Copy, scale=T2[:, 2, 0:1])
-  T166 = AQ.tile([128, 512, 4], B, tag='grouped_0', bufs=1, align_bytes=64)
-  ve.tensor_copy(out=T166[:], in_=T163[:].rearrange(S13))
-  nc.gpsimd.tensor_tensor(out=T135[:, 0, :], in0=T135[:, 0, :], in1=T151[:, 3, :], op=ALU.add)
-  AC(T165[:, 1, :], T136[:].rearrange(S8)[:, 1, 512:1024].bitcast(E4), ACT.Copy, scale=T2[:, 2, 1:2])
-  AC(T165[:, 2, :], T136[:].rearrange(S8)[:, 2, 512:1024].bitcast(E4), ACT.Copy, scale=T2[:, 2, 2:3])
-  T162 = AQ.tile([128, 4, 512], F, tag='f8_1', bufs=1)
-  TT(out=T162[:, 1, :], in0=T154[:], in1=T161[:], op=ALU.subtract)
-  AC(T165[:, 3, :], T136[:].rearrange(S8)[:, 3, 512:1024].bitcast(E4), ACT.Copy, scale=T2[:, 2, 3:4])
-  TT(out=T162[:, 2, :], in0=T155[:], in1=T161[:], op=ALU.subtract)
-  T174 = PP([128, 256, 4], B, tag='l_2', bufs=1)
-  MT(T174[:, 0:128, :], lhsT=T3[:], rhs=T139[:, :, 0:128].rearrange(S13), start=True, stop=True)
-  T167 = AQ.tile([128, 4, 512], B, tag='wl_wide_0', bufs=1)
-  AC(T167[:, 0, :], T137[:].rearrange(S8)[:, 0, 0:512].bitcast(E4), ACT.Copy, scale=T2[:, 3, 0:1])
-  MT(T174[:, 128:256, :], lhsT=T3[:], rhs=T139[:, :, 128:256].rearrange(S13), start=True, stop=True)
-  TT(out=T162[:, 3, :], in0=T156[:], in1=T161[:], op=ALU.subtract)
-  T175 = PP([128, 256, 4], B, tag='l_0', bufs=1)
-  MT(T175[:, 0:128, :], lhsT=T3[:], rhs=T139[:, :, 256:384].rearrange(S13), start=True, stop=True)
-  AC(T167[:, 1, :], T137[:].rearrange(S8)[:, 1, 0:512].bitcast(E4), ACT.Copy, scale=T2[:, 3, 1:2])
-  MT(T175[:, 128:256, :], lhsT=T3[:], rhs=T139[:, :, 384:512].rearrange(S13), start=True, stop=True)
-  TT(out=T162[:, 0, :], in0=T152[:], in1=T161[:], op=ALU.subtract)
-  T177 = PP([128, 512], F, tag='l_1', bufs=1)
-  M(T177[:], T12, T13, 1024, T8, T9, 1, 0)
-  AC(T167[:, 2, :], T137[:].rearrange(S8)[:, 2, 0:512].bitcast(E4), ACT.Copy, scale=T2[:, 3, 2:3])
-  M(T177[:], T21, T22, 1024, T17, T18, 0, 0)
-  Q(T21[:, 1536:2048], T22[:, 1536:2048], T164[:].rearrange(S9))
-  AC(T162[:], T162[:], ACT.Exp)
-  T168 = AQ.tile([128, 512, 4], B, tag='grouped_1', bufs=1, align_bytes=64)
-  ve.tensor_copy(out=T168[:], in_=T165[:].rearrange(S13))
-  Q(T30[:, 1024:1536], T31[:, 1024:1536], T166[:].rearrange(S9))
-  AC(T167[:, 3, :], T137[:].rearrange(S8)[:, 3, 0:512].bitcast(E4), ACT.Copy, scale=T2[:, 3, 3:4])
-  nc.gpsimd.tensor_tensor(out=T135[:, 1, :], in0=T162[:, 0, :], in1=T162[:, 1, :], op=ALU.add)
-  Q(T30[:, 1536:2048], T31[:, 1536:2048], T168[:].rearrange(S9))
-  M(T177[:], T30, T31, 1024, T26, T27, 0, 0)
-  T169 = AQ.tile([128, 4, 512], B, tag='wl_wide_1', bufs=1)
-  AC(T169[:, 0, :], T137[:].rearrange(S8)[:, 0, 512:1024].bitcast(E4), ACT.Copy, scale=T2[:, 3, 0:1])
-  T170 = AQ.tile([128, 512, 4], B, tag='grouped_2', bufs=1, align_bytes=64)
-  ve.tensor_copy(out=T170[:], in_=T167[:].rearrange(S13))
-  AC(T169[:, 1, :], T137[:].rearrange(S8)[:, 1, 512:1024].bitcast(E4), ACT.Copy, scale=T2[:, 3, 1:2])
-  nc.gpsimd.tensor_tensor(out=T135[:, 1, :], in0=T135[:, 1, :], in1=T162[:, 2, :], op=ALU.add)
-  AC(T169[:, 2, :], T137[:].rearrange(S8)[:, 2, 512:1024].bitcast(E4), ACT.Copy, scale=T2[:, 3, 2:3])
-  Q(T39[:, 1024:1536], T40[:, 1024:1536], T170[:].rearrange(S9))
-  AC(T169[:, 3, :], T137[:].rearrange(S8)[:, 3, 512:1024].bitcast(E4), ACT.Copy, scale=T2[:, 3, 3:4])
-  nc.gpsimd.tensor_tensor(out=T135[:, 1, :], in0=T135[:, 1, :], in1=T162[:, 3, :], op=ALU.add)
-  T171 = AQ.tile([128, 512, 4], B, tag='grouped_0', bufs=1, align_bytes=64)
-  SC(T171[:], T138[:].rearrange(S13))
-  T172 = AQ.tile([128, 512, 4], B, tag='grouped_1', bufs=1, align_bytes=64)
-  ve.tensor_copy(out=T172[:], in_=T169[:].rearrange(S13))
-  M(T177[:], T39, T40, 1024, T35, T36, 0, 1)
-  Q(T39[:, 1536:2048], T40[:, 1536:2048], T172[:].rearrange(S9))
-  T173 = AQ.tile([128, 512, 4], B, tag='grouped_2', bufs=1, align_bytes=64)
-  SC(T173[:, 0:256, :], T174[:])
-  T141 = AQ.tile([128, 4, 512], B, tag='w2_raw_0', bufs=1)
-  DM(out=T141[:], in_=w2[1, :, 512:1024].rearrange(S1, j=4))
+  Q(T37[:, 0:512], T38[:, 0:512], T116[:].rearrange(S9))
+  M(T130[:], T39, T40, 512, T35, T36, 0, 1)
+  T132 = AQ.tile([128, 4, 512], B, tag='wl_wide_1', bufs=1)
+  AC(T132[:, 0, :], T95[:].rearrange(S8)[:, 0, 512:1024].bitcast(E4), ACT.Copy, scale=T2[:, 0, 0:1])
+  T131 = PP([128, 512], F, tag='l_2', bufs=1)
+  M(T131[:], T12, T13, 768, T8, T9, 1, 0)
+  T133 = AQ.tile([128, 512], F, tag='top_0', bufs=1)
+  TT(out=T133[:], in0=T129[:], in1=T127[:], op=ALU.max)
+  M(T131[:], T21, T22, 768, T17, T18, 0, 0)
+  AC(T132[:, 1, :], T95[:].rearrange(S8)[:, 1, 512:1024].bitcast(E4), ACT.Copy, scale=T2[:, 0, 1:2])
+  M(T131[:], T30, T31, 768, T26, T27, 0, 0)
+  T134 = AQ.tile([128, 512, 4], B, tag='grouped_2', bufs=1, align_bytes=64)
+  ve.tensor_copy(out=T134[:].rearrange(S13, i=4), in_=T126[:].rearrange(S14, i=4))
+  M(T131[:], T39, T40, 768, T35, T36, 0, 1)
+  AC(T132[:, 2, :], T95[:].rearrange(S8)[:, 2, 512:1024].bitcast(E4), ACT.Copy, scale=T2[:, 0, 2:3])
+  AC(T132[:, 3, :], T95[:].rearrange(S8)[:, 3, 512:1024].bitcast(E4), ACT.Copy, scale=T2[:, 0, 3:4])
+  TT(out=T133[:], in0=T130[:], in1=T133[:], op=ALU.max)
+  T141 = AQ.tile([128, 4, 512], B, tag='wl_wide_0', bufs=1)
+  AC(T141[:, 0, :], T112[:].rearrange(S8)[:, 0, 0:512].bitcast(E4), ACT.Copy, scale=T2[:, 1, 0:1])
+  T121 = AQ.tile([128, 4, 4, 256], U8, tag='wl_raw_1', bufs=1)
+  DM(out=T121[:, 0, :, :], in_=wl_bytes[1536:2048, :].rearrange(S4, t=4, v=4, h=2)[:, 0, :, 1, :])
+  DM(out=T121[:, 1, :, :], in_=wl_bytes[1536:2048, :].rearrange(S4, t=4, v=4, h=2)[:, 1, :, 1, :])
+  DM(out=T121[:, 2, :, :], in_=wl_bytes[1536:2048, :].rearrange(S4, t=4, v=4, h=2)[:, 2, :, 1, :])
+  DM(out=T121[:, 3, :, :], in_=wl_bytes[1536:2048, :].rearrange(S4, t=4, v=4, h=2)[:, 3, :, 1, :])
+  T122 = AQ.tile([128, 4, 512], B, tag='w2_raw_0', bufs=1)
+  DM(out=T122[:], in_=w2[0, :, 0:512].rearrange(S1, j=4))
+  T142 = AQ.tile([128, 512, 4], B, tag='grouped_0', bufs=1, align_bytes=64)
+  ve.tensor_copy(out=T142[:].rearrange(S13, i=4), in_=T132[:].rearrange(S14, i=4))
+  T123 = AQ.tile([128, 4, 512], B, tag='w2_raw_1', bufs=1)
+  DM(out=T123[:], in_=w2[0, :, 512:1024].rearrange(S1, j=4))
+  T124 = AQ.tile([128, 4, 512], B, tag='w2_raw_2', bufs=1)
+  DM(out=T124[:], in_=w2[1, :, 0:512].rearrange(S1, j=4))
+  AC(T141[:, 1, :], T112[:].rearrange(S8)[:, 1, 0:512].bitcast(E4), ACT.Copy, scale=T2[:, 1, 1:2])
+  AC(T141[:, 2, :], T112[:].rearrange(S8)[:, 2, 0:512].bitcast(E4), ACT.Copy, scale=T2[:, 1, 2:3])
+  AC(T141[:, 3, :], T112[:].rearrange(S8)[:, 3, 0:512].bitcast(E4), ACT.Copy, scale=T2[:, 1, 3:4])
+  TT(out=T133[:], in0=T131[:], in1=T133[:], op=ALU.max)
+  T143 = AQ.tile([128, 4, 512], B, tag='wl_wide_1', bufs=1)
+  AC(T143[:, 0, :], T112[:].rearrange(S8)[:, 0, 512:1024].bitcast(E4), ACT.Copy, scale=T2[:, 1, 0:1])
+  Q(T12[:, 1024:1536], T13[:, 1024:1536], T134[:].rearrange(S9))
+  AC(T143[:, 1, :], T112[:].rearrange(S8)[:, 1, 512:1024].bitcast(E4), ACT.Copy, scale=T2[:, 1, 1:2])
+  T135 = AQ.tile([128, 4, 512], F, tag='f8_0', bufs=1)
+  TT(out=T135[:, 1, :], in0=T129[:], in1=T133[:], op=ALU.subtract)
+  AC(T143[:, 2, :], T112[:].rearrange(S8)[:, 2, 512:1024].bitcast(E4), ACT.Copy, scale=T2[:, 1, 2:3])
+  TT(out=T135[:, 2, :], in0=T130[:], in1=T133[:], op=ALU.subtract)
+  T137 = PP([128, 512], F, tag='l_0', bufs=1)
+  M(T137[:], T12, T13, 128, T8, T9, 1, 0)
+  M(T137[:], T21, T22, 128, T17, T18, 0, 0)
+  AC(T143[:, 3, :], T112[:].rearrange(S8)[:, 3, 512:1024].bitcast(E4), ACT.Copy, scale=T2[:, 1, 3:4])
+  TT(out=T135[:, 3, :], in0=T131[:], in1=T133[:], op=ALU.subtract)
+  M(T137[:], T30, T31, 128, T26, T27, 0, 0)
+  M(T137[:], T39, T40, 128, T35, T36, 0, 1)
+  TT(out=T135[:, 0, :], in0=T127[:], in1=T133[:], op=ALU.subtract)
+  T138 = PP([128, 512], F, tag='l_1', bufs=1)
+  M(T138[:], T12, T13, 384, T8, T9, 1, 0)
+  T136 = AQ.tile([128, 512], F, tag='l0_1', bufs=1)
+  SC(T136[:], T137[:])
+  M(T138[:], T21, T22, 384, T17, T18, 0, 0)
+  T144 = AQ.tile([128, 512, 4], B, tag='grouped_1', bufs=1, align_bytes=64)
+  ve.tensor_copy(out=T144[:].rearrange(S13, i=4), in_=T141[:].rearrange(S14, i=4))
+  M(T138[:], T30, T31, 384, T26, T27, 0, 0)
+  AC(T135[:], T135[:], ACT.Exp)
+  M(T138[:], T39, T40, 384, T35, T36, 0, 1)
+  T139 = PP([128, 512], F, tag='l_2', bufs=1)
+  M(T139[:], T12, T13, 640, T8, T9, 1, 0)
+  M(T139[:], T21, T22, 640, T17, T18, 0, 0)
+  M(T139[:], T30, T31, 640, T26, T27, 0, 0)
+  T145 = AQ.tile([128, 512], F, tag='top_1', bufs=1)
+  TT(out=T145[:], in0=T138[:], in1=T136[:], op=ALU.max)
+  M(T139[:], T39, T40, 640, T35, T36, 0, 1)
+  T140 = PP([128, 512], F, tag='l_0', bufs=1)
+  M(T140[:], T12, T13, 896, T8, T9, 1, 0)
+  Q(T12[:, 1536:2048], T13[:, 1536:2048], T142[:].rearrange(S9))
+  M(T140[:], T21, T22, 896, T17, T18, 0, 0)
+  M(T140[:], T30, T31, 896, T26, T27, 0, 0)
+  TT(out=T145[:], in0=T139[:], in1=T145[:], op=ALU.max)
+  T147 = AQ.tile([128, 4, 512], B, tag='wl_wide_0', bufs=1)
+  AC(T147[:, 0, :], T120[:].rearrange(S8)[:, 0, 0:512].bitcast(E4), ACT.Copy, scale=T2[:, 2, 0:1])
+  T119 = KP([128, 4, 512], F, tag='den', bufs=1)
+  nc.gpsimd.tensor_tensor(out=T119[:, 0, :], in0=T135[:, 0, :], in1=T135[:, 1, :], op=ALU.add)
+  M(T140[:], T39, T40, 896, T35, T36, 0, 1)
+  T148 = AQ.tile([128, 512, 4], B, tag='grouped_2', bufs=1, align_bytes=64)
+  ve.tensor_copy(out=T148[:].rearrange(S13, i=4), in_=T143[:].rearrange(S14, i=4))
+  AC(T147[:, 1, :], T120[:].rearrange(S8)[:, 1, 0:512].bitcast(E4), ACT.Copy, scale=T2[:, 2, 1:2])
+  AC(T147[:, 2, :], T120[:].rearrange(S8)[:, 2, 0:512].bitcast(E4), ACT.Copy, scale=T2[:, 2, 2:3])
+  nc.gpsimd.tensor_tensor(out=T119[:, 0, :], in0=T119[:, 0, :], in1=T135[:, 2, :], op=ALU.add)
+  AC(T147[:, 3, :], T120[:].rearrange(S8)[:, 3, 0:512].bitcast(E4), ACT.Copy, scale=T2[:, 2, 3:4])
+  TT(out=T145[:], in0=T140[:], in1=T145[:], op=ALU.max)
+  T149 = AQ.tile([128, 4, 512], B, tag='wl_wide_1', bufs=1)
+  AC(T149[:, 0, :], T120[:].rearrange(S8)[:, 0, 512:1024].bitcast(E4), ACT.Copy, scale=T2[:, 2, 0:1])
+  Q(T21[:, 1024:1536], T22[:, 1024:1536], T144[:].rearrange(S9))
+  nc.gpsimd.tensor_tensor(out=T119[:, 0, :], in0=T119[:, 0, :], in1=T135[:, 3, :], op=ALU.add)
+  AC(T149[:, 1, :], T120[:].rearrange(S8)[:, 1, 512:1024].bitcast(E4), ACT.Copy, scale=T2[:, 2, 1:2])
+  T146 = AQ.tile([128, 4, 512], F, tag='f8_1', bufs=1)
+  TT(out=T146[:, 1, :], in0=T138[:], in1=T145[:], op=ALU.subtract)
+  AC(T149[:, 2, :], T120[:].rearrange(S8)[:, 2, 512:1024].bitcast(E4), ACT.Copy, scale=T2[:, 2, 2:3])
+  TT(out=T146[:, 2, :], in0=T139[:], in1=T145[:], op=ALU.subtract)
+  T159 = PP([128, 512], F, tag='l_1', bufs=1)
+  M(T159[:], T12, T13, 1024, T8, T9, 1, 0)
+  AC(T149[:, 3, :], T120[:].rearrange(S8)[:, 3, 512:1024].bitcast(E4), ACT.Copy, scale=T2[:, 2, 3:4])
+  M(T159[:], T21, T22, 1024, T17, T18, 0, 0)
+  TT(out=T146[:, 3, :], in0=T140[:], in1=T145[:], op=ALU.subtract)
+  T160 = PP([128, 512], F, tag='l_2', bufs=1)
+  M(T160[:], T12, T13, 1280, T8, T9, 1, 0)
+  T150 = AQ.tile([128, 512, 4], B, tag='grouped_0', bufs=1, align_bytes=64)
+  SC(T150[:].rearrange(S13, i=4), T147[:].rearrange(S14, i=4))
+  M(T160[:], T21, T22, 1280, T17, T18, 0, 0)
+  TT(out=T146[:, 0, :], in0=T136[:], in1=T145[:], op=ALU.subtract)
+  T161 = PP([128, 512], F, tag='l_0', bufs=1)
+  M(T161[:], T12, T13, 1536, T8, T9, 1, 0)
+  Q(T21[:, 1536:2048], T22[:, 1536:2048], T148[:].rearrange(S9))
+  T152 = AQ.tile([128, 512, 4], B, tag='grouped_1', bufs=1, align_bytes=64)
+  ve.tensor_copy(out=T152[:].rearrange(S13, i=4), in_=T149[:].rearrange(S14, i=4))
+  M(T161[:], T21, T22, 1536, T17, T18, 0, 0)
+  AC(T146[:], T146[:], ACT.Exp)
+  Q(T30[:, 1024:1536], T31[:, 1024:1536], T150[:].rearrange(S9))
+  Q(T30[:, 1536:2048], T31[:, 1536:2048], T152[:].rearrange(S9))
+  M(T159[:], T30, T31, 1024, T26, T27, 0, 0)
+  M(T160[:], T30, T31, 1280, T26, T27, 0, 0)
+  T155 = AQ.tile([128, 512, 4], B, tag='grouped_0', bufs=1, align_bytes=64)
+  ve.tensor_copy(out=T155[:].rearrange(S13, i=4), in_=T122[:].rearrange(S14, i=4))
+  M(T161[:], T30, T31, 1536, T26, T27, 0, 0)
+  T151 = AQ.tile([128, 4, 512], B, tag='wl_wide_0', bufs=1)
+  AC(T151[:, 0, :], T121[:].rearrange(S8)[:, 0, 0:512].bitcast(E4), ACT.Copy, scale=T2[:, 3, 0:1])
+  nc.gpsimd.tensor_tensor(out=T119[:, 1, :], in0=T146[:, 0, :], in1=T146[:, 1, :], op=ALU.add)
+  AC(T151[:, 1, :], T121[:].rearrange(S8)[:, 1, 0:512].bitcast(E4), ACT.Copy, scale=T2[:, 3, 1:2])
+  T125 = AQ.tile([128, 4, 512], B, tag='w2_raw_0', bufs=1)
+  DM(out=T125[:], in_=w2[1, :, 512:1024].rearrange(S1, j=4))
   T14 = KP([128, 1024], U, tag='w2q0_codes', bufs=1, align_bytes=64)
   T15 = KP([128, 1024], U8, tag='w2q0_scales', bufs=1, align_bytes=64)
-  Q(T14[:, 0:512], T15[:, 0:512], T171[:].rearrange(S9))
-  T211 = AQ.tile([128, 4, 512], B, tag='w2_raw_1', bufs=1)
-  DM(out=T211[:], in_=w2[2, :, 0:512].rearrange(S1, j=4))
-  SC(T173[:, 256:512, :], T175[:])
-  T178 = PP([128, 512], F, tag='l_2', bufs=1)
-  M(T178[:], T12, T13, 1280, T8, T9, 1, 0)
-  M(T178[:], T21, T22, 1280, T17, T18, 0, 0)
-  T176 = AQ.tile([128, 512], F, tag='l0_0', bufs=1)
-  SC(T176[:], T177[:])
-  Q(T14[:, 512:1024], T15[:, 512:1024], T173[:].rearrange(S9))
-  M(T178[:], T30, T31, 1280, T26, T27, 0, 0)
-  M(T178[:], T39, T40, 1280, T35, T36, 0, 1)
-  T196 = AQ.tile([128, 512, 4], B, tag='grouped_0', bufs=1, align_bytes=64)
-  SC(T196[:], T140[:].rearrange(S13))
-  T179 = PP([128, 512], F, tag='l_0', bufs=1)
-  M(T179[:], T12, T13, 1536, T8, T9, 1, 0)
-  T181 = AQ.tile([128, 512], F, tag='top_0', bufs=1)
-  TT(out=T181[:], in0=T178[:], in1=T176[:], op=ALU.max)
-  M(T179[:], T21, T22, 1536, T17, T18, 0, 0)
-  M(T179[:], T30, T31, 1536, T26, T27, 0, 0)
-  M(T179[:], T39, T40, 1536, T35, T36, 0, 1)
-  T180 = PP([128, 512], F, tag='l_1', bufs=1)
-  M(T180[:], T12, T13, 1792, T8, T9, 1, 0)
-  TT(out=T181[:], in0=T179[:], in1=T181[:], op=ALU.max)
-  M(T180[:], T21, T22, 1792, T17, T18, 0, 0)
-  M(T180[:], T30, T31, 1792, T26, T27, 0, 0)
-  M(T180[:], T39, T40, 1792, T35, T36, 0, 1)
-  T189 = PP([128, 512], F, tag='h_0', bufs=1)
-  M(T189[:], T14, T15, 512, T10, T11, 1, 1)
-  TT(out=T181[:], in0=T180[:], in1=T181[:], op=ALU.max)
-  T212 = AQ.tile([128, 4, 512], B, tag='w2_raw_2', bufs=1)
-  DM(out=T212[:], in_=w2[2, :, 512:1024].rearrange(S1, j=4))
-  T190 = PP([128, 512], F, tag='h_1', bufs=1)
-  M(T190[:], T14, T15, 0, T10, T11, 1, 1)
-  T191 = AQ.tile([128, 512], F, tag='th_0', bufs=1)
-  AC(T191[:], T189[:], ACT.Tanh, scale=0.5)
-  T193 = PP([128, 512], F, tag='h_2', bufs=1)
-  M(T193[:], T14, T15, 640, T10, T11, 1, 1)
+  Q(T14[:, 0:512], T15[:, 0:512], T155[:].rearrange(S9))
+  AC(T151[:, 2, :], T121[:].rearrange(S8)[:, 2, 0:512].bitcast(E4), ACT.Copy, scale=T2[:, 3, 2:3])
+  T172 = PP([128, 512], F, tag='h_1', bufs=1)
+  M(T172[:], T14, T15, 0, T10, T11, 1, 1)
+  T178 = AQ.tile([128, 512, 4], B, tag='grouped_0', bufs=1, align_bytes=64)
+  ve.tensor_copy(out=T178[:].rearrange(S13, i=4), in_=T124[:].rearrange(S14, i=4))
+  nc.gpsimd.tensor_tensor(out=T119[:, 1, :], in0=T119[:, 1, :], in1=T146[:, 2, :], op=ALU.add)
+  T176 = PP([128, 512], F, tag='h_3', bufs=1)
+  M(T176[:], T14, T15, 128, T10, T11, 1, 1)
+  AC(T151[:, 3, :], T121[:].rearrange(S8)[:, 3, 0:512].bitcast(E4), ACT.Copy, scale=T2[:, 3, 3:4])
+  T153 = AQ.tile([128, 4, 512], B, tag='wl_wide_1', bufs=1)
+  AC(T153[:, 0, :], T121[:].rearrange(S8)[:, 0, 512:1024].bitcast(E4), ACT.Copy, scale=T2[:, 3, 0:1])
+  T154 = AQ.tile([128, 512, 4], B, tag='grouped_2', bufs=1, align_bytes=64)
+  ve.tensor_copy(out=T154[:].rearrange(S13, i=4), in_=T151[:].rearrange(S14, i=4))
+  nc.gpsimd.tensor_tensor(out=T119[:, 1, :], in0=T119[:, 1, :], in1=T146[:, 3, :], op=ALU.add)
+  AC(T153[:, 1, :], T121[:].rearrange(S8)[:, 1, 512:1024].bitcast(E4), ACT.Copy, scale=T2[:, 3, 1:2])
+  AC(T153[:, 2, :], T121[:].rearrange(S8)[:, 2, 512:1024].bitcast(E4), ACT.Copy, scale=T2[:, 3, 2:3])
+  AC(T153[:, 3, :], T121[:].rearrange(S8)[:, 3, 512:1024].bitcast(E4), ACT.Copy, scale=T2[:, 3, 3:4])
   T23 = KP([128, 1024], U, tag='w2q1_codes', bufs=1, align_bytes=64)
   T24 = KP([128, 1024], U8, tag='w2q1_scales', bufs=1, align_bytes=64)
-  Q(T23[:, 0:512], T24[:, 0:512], T196[:].rearrange(S9))
-  T194 = PP([128, 512], F, tag='h_3', bufs=1)
-  M(T194[:], T14, T15, 128, T10, T11, 1, 1)
-  T222 = AQ.tile([128, 512, 4], B, tag='grouped_2', bufs=1, align_bytes=64)
-  SC(T222[:], T211[:].rearrange(S13))
-  T200 = PP([128, 512], F, tag='h_0', bufs=1)
-  M(T200[:], T14, T15, 768, T10, T11, 1, 1)
-  T182 = AQ.tile([128, 4, 512], F, tag='f8_2', bufs=1)
-  TT(out=T182[:, 1, :], in0=T178[:], in1=T181[:], op=ALU.subtract)
-  TT(out=T182[:, 2, :], in0=T179[:], in1=T181[:], op=ALU.subtract)
-  T184 = PP([128, 512], F, tag='l_2', bufs=1)
-  M(T184[:], T12, T13, 1152, T8, T9, 1, 0)
-  M(T184[:], T21, T22, 1152, T17, T18, 0, 0)
-  TT(out=T182[:, 3, :], in0=T180[:], in1=T181[:], op=ALU.subtract)
-  M(T184[:], T30, T31, 1152, T26, T27, 0, 0)
-  M(T184[:], T39, T40, 1152, T35, T36, 0, 1)
-  TT(out=T182[:, 0, :], in0=T176[:], in1=T181[:], op=ALU.subtract)
-  T185 = PP([128, 512], F, tag='l_0', bufs=1)
-  M(T185[:], T12, T13, 1408, T8, T9, 1, 0)
-  M(T185[:], T21, T22, 1408, T17, T18, 0, 0)
-  T192 = AQ.tile([128, 512], F, tag='r_0', bufs=1)
-  ST(out=T192[:], in0=T191[:], scalar=1.0, in1=T190[:], op0=ALU.add, op1=ALU.mult)
-  T183 = AQ.tile([128, 512], F, tag='l0_1', bufs=1)
-  SC(T183[:], T184[:])
-  M(T185[:], T30, T31, 1408, T26, T27, 0, 0)
-  M(T185[:], T39, T40, 1408, T35, T36, 0, 1)
+  Q(T23[:, 0:512], T24[:, 0:512], T178[:].rearrange(S9))
+  T156 = AQ.tile([128, 512, 4], B, tag='grouped_1', bufs=1, align_bytes=64)
+  SC(T156[:].rearrange(S13, i=4), T153[:].rearrange(S14, i=4))
+  Q(T39[:, 1024:1536], T40[:, 1024:1536], T154[:].rearrange(S9))
+  T157 = AQ.tile([128, 512, 4], B, tag='grouped_2', bufs=1, align_bytes=64)
+  ve.tensor_copy(out=T157[:].rearrange(S13, i=4), in_=T123[:].rearrange(S14, i=4))
+  M(T159[:], T39, T40, 1024, T35, T36, 0, 1)
+  M(T160[:], T39, T40, 1280, T35, T36, 0, 1)
+  Q(T14[:, 512:1024], T15[:, 512:1024], T157[:].rearrange(S9))
+  T191 = AQ.tile([128, 4, 512], B, tag='w2_raw_1', bufs=1)
+  DM(out=T191[:], in_=w2[2, :, 0:512].rearrange(S1, j=4))
+  T192 = AQ.tile([128, 4, 512], B, tag='w2_raw_2', bufs=1)
+  DM(out=T192[:], in_=w2[2, :, 512:1024].rearrange(S1, j=4))
+  T158 = AQ.tile([128, 512], F, tag='l0_0', bufs=1)
+  SC(T158[:], T159[:])
+  Q(T39[:, 1536:2048], T40[:, 1536:2048], T156[:].rearrange(S9))
+  T171 = PP([128, 512], F, tag='h_0', bufs=1)
+  M(T171[:], T14, T15, 512, T10, T11, 1, 1)
+  T162 = PP([128, 512], F, tag='l_1', bufs=1)
+  M(T162[:], T12, T13, 1792, T8, T9, 1, 0)
+  T163 = AQ.tile([128, 512], F, tag='top_0', bufs=1)
+  TT(out=T163[:], in0=T160[:], in1=T158[:], op=ALU.max)
+  T185 = AQ.tile([128, 512, 4], B, tag='grouped_1', bufs=1, align_bytes=64)
+  SC(T185[:].rearrange(S13, i=4), T125[:].rearrange(S14, i=4))
+  M(T161[:], T39, T40, 1536, T35, T36, 0, 1)
+  M(T162[:], T21, T22, 1792, T17, T18, 0, 0)
+  TT(out=T163[:], in0=T161[:], in1=T163[:], op=ALU.max)
+  M(T162[:], T30, T31, 1792, T26, T27, 0, 0)
+  M(T162[:], T39, T40, 1792, T35, T36, 0, 1)
+  T175 = PP([128, 512], F, tag='h_2', bufs=1)
+  M(T175[:], T14, T15, 640, T10, T11, 1, 1)
+  TT(out=T163[:], in0=T162[:], in1=T163[:], op=ALU.max)
+  T164 = AQ.tile([128, 4, 512], F, tag='f8_2', bufs=1)
+  TT(out=T164[:, 1, :], in0=T160[:], in1=T163[:], op=ALU.subtract)
+  T173 = AQ.tile([128, 512], F, tag='th_0', bufs=1)
+  AC(T173[:], T171[:], ACT.Tanh, scale=0.5)
+  T213 = AQ.tile([128, 4, 512], B, tag='w2_raw_0', bufs=1)
+  DM(out=T213[:], in_=w2[3, :, 0:512].rearrange(S1, j=4))
+  TT(out=T164[:, 2, :], in0=T161[:], in1=T163[:], op=ALU.subtract)
+  T166 = PP([128, 512], F, tag='l_2', bufs=1)
+  M(T166[:], T12, T13, 1152, T8, T9, 1, 0)
+  T177 = AQ.tile([128, 512], F, tag='th_1', bufs=1)
+  AC(T177[:], T175[:], ACT.Tanh, scale=0.5)
+  M(T166[:], T21, T22, 1152, T17, T18, 0, 0)
+  TT(out=T164[:, 3, :], in0=T162[:], in1=T163[:], op=ALU.subtract)
+  M(T166[:], T30, T31, 1152, T26, T27, 0, 0)
+  T202 = AQ.tile([128, 512, 4], B, tag='grouped_2', bufs=1, align_bytes=64)
+  SC(T202[:].rearrange(S13, i=4), T191[:].rearrange(S14, i=4))
+  M(T166[:], T39, T40, 1152, T35, T36, 0, 1)
+  TT(out=T164[:, 0, :], in0=T158[:], in1=T163[:], op=ALU.subtract)
+  T167 = PP([128, 512], F, tag='l_0', bufs=1)
+  M(T167[:], T12, T13, 1408, T8, T9, 1, 0)
+  M(T167[:], T21, T22, 1408, T17, T18, 0, 0)
+  T174 = AQ.tile([128, 512], F, tag='r_0', bufs=1)
+  ST(out=T174[:], in0=T173[:], scalar=1.0, in1=T172[:], op0=ALU.add, op1=ALU.mult)
+  M(T167[:], T30, T31, 1408, T26, T27, 0, 0)
+  M(T167[:], T39, T40, 1408, T35, T36, 0, 1)
+  T180 = AQ.tile([128, 512], F, tag='r_1', bufs=1)
+  ST(out=T180[:], in0=T177[:], scalar=1.0, in1=T176[:], op0=ALU.add, op1=ALU.mult)
+  T168 = PP([128, 512], F, tag='l_1', bufs=1)
+  M(T168[:], T12, T13, 1664, T8, T9, 1, 0)
+  M(T168[:], T21, T22, 1664, T17, T18, 0, 0)
+  ST(out=T174[:], in0=T170[:, 0, :], scalar=T118[:, 0:1], in1=T174[:], op0=ALU.mult, op1=ALU.add)
+  M(T168[:], T30, T31, 1664, T26, T27, 0, 0)
+  M(T168[:], T39, T40, 1664, T35, T36, 0, 1)
+  ST(out=T180[:], in0=T170[:, 1, :], scalar=T118[:, 1:2], in1=T180[:], op0=ALU.mult, op1=ALU.add)
+  T165 = AQ.tile([128, 512], F, tag='l0_1', bufs=1)
+  SC(T165[:], T166[:])
+  T182 = PP([128, 512], F, tag='h_0', bufs=1)
+  M(T182[:], T14, T15, 768, T10, T11, 1, 1)
+  T214 = AQ.tile([128, 4, 512], B, tag='w2_raw_1', bufs=1)
+  DM(out=T214[:], in_=w2[3, :, 512:1024].rearrange(S1, j=4))
+  T183 = PP([128, 512], F, tag='h_1', bufs=1)
+  M(T183[:], T14, T15, 256, T10, T11, 1, 1)
+  Q(T23[:, 512:1024], T24[:, 512:1024], T185[:].rearrange(S9))
+  AC(T164[:], T164[:], ACT.Exp)
+  T169 = PP([128, 512], F, tag='l_2', bufs=1)
+  M(T169[:], T12, T13, 1920, T8, T9, 1, 0)
+  M(T169[:], T21, T22, 1920, T17, T18, 0, 0)
+  T179 = AQ.tile([128, 512], F, tag='top_1', bufs=1)
+  TT(out=T179[:], in0=T167[:], in1=T165[:], op=ALU.max)
+  M(T169[:], T30, T31, 1920, T26, T27, 0, 0)
+  M(T169[:], T39, T40, 1920, T35, T36, 0, 1)
+  TT(out=T135[:, 0, :], in0=T135[:, 0, :], in1=T174[:], op=ALU.mult)
+  T181 = PP([128, 2, 512], B, tag='x', bufs=1)
+  TR(T181[:, 0, 0:128], T7[:, 0, 256:384], T3[:])
+  TR(T181[:, 0, 128:256], T7[:, 1, 256:384], T3[:])
+  TR(T181[:, 0, 256:384], T7[:, 2, 256:384], T3[:])
+  TT(out=T179[:], in0=T168[:], in1=T179[:], op=ALU.max)
+  TR(T181[:, 0, 384:512], T7[:, 3, 256:384], T3[:])
+  TR(T181[:, 1, 0:128], T7[:, 0, 384:512], T3[:])
+  TR(T181[:, 1, 128:256], T7[:, 1, 384:512], T3[:])
+  TR(T181[:, 1, 256:384], T7[:, 2, 384:512], T3[:])
+  TR(T181[:, 1, 384:512], T7[:, 3, 384:512], T3[:])
+  T188 = PP([128, 512], F, tag='h_2', bufs=1)
+  M(T188[:], T14, T15, 896, T10, T11, 1, 1)
+  TT(out=T146[:, 0, :], in0=T146[:, 0, :], in1=T180[:], op=ALU.mult)
+  T184 = AQ.tile([128, 512], F, tag='th_2', bufs=1)
+  AC(T184[:], T182[:], ACT.Tanh, scale=0.5)
+  T189 = PP([128, 512], F, tag='h_3', bufs=1)
+  M(T189[:], T14, T15, 384, T10, T11, 1, 1)
+  nc.gpsimd.tensor_tensor(out=T119[:, 2, :], in0=T164[:, 0, :], in1=T164[:, 1, :], op=ALU.add)
+  T190 = AQ.tile([128, 512], F, tag='th_0', bufs=1)
+  AC(T190[:], T188[:], ACT.Tanh, scale=0.5)
+  TT(out=T179[:], in0=T169[:], in1=T179[:], op=ALU.max)
+  T195 = PP([128, 512], F, tag='h_0', bufs=1)
+  M(T195[:], T23, T24, 512, T19, T20, 1, 1)
+  T208 = AQ.tile([128, 512, 4], B, tag='grouped_0', bufs=1, align_bytes=64)
+  SC(T208[:].rearrange(S13, i=4), T192[:].rearrange(S14, i=4))
+  T187 = AQ.tile([128, 512], F, tag='r_2', bufs=1)
+  ST(out=T187[:], in0=T184[:], scalar=1.0, in1=T183[:], op0=ALU.add, op1=ALU.mult)
+  T199 = PP([128, 512], F, tag='h_2', bufs=1)
+  M(T199[:], T23, T24, 640, T19, T20, 1, 1)
+  nc.gpsimd.tensor_tensor(out=T119[:, 2, :], in0=T119[:, 2, :], in1=T164[:, 2, :], op=ALU.add)
+  T186 = AQ.tile([128, 4, 512], F, tag='f8_3', bufs=1)
+  TT(out=T186[:, 1, :], in0=T167[:], in1=T179[:], op=ALU.subtract)
+  T196 = PP([128, 512], F, tag='h_1', bufs=1)
+  M(T196[:], T23, T24, 0, T19, T20, 1, 1)
+  TT(out=T186[:, 2, :], in0=T168[:], in1=T179[:], op=ALU.subtract)
+  nc.gpsimd.tensor_tensor(out=T119[:, 2, :], in0=T119[:, 2, :], in1=T164[:, 3, :], op=ALU.add)
+  TT(out=T186[:, 3, :], in0=T169[:], in1=T179[:], op=ALU.subtract)
+  TT(out=T186[:, 0, :], in0=T165[:], in1=T179[:], op=ALU.subtract)
+  T197 = AQ.tile([128, 512], F, tag='th_1', bufs=1)
+  AC(T197[:], T195[:], ACT.Tanh, scale=0.5)
+  T193 = AQ.tile([128, 512], F, tag='r_3', bufs=1)
+  ST(out=T193[:], in0=T190[:], scalar=1.0, in1=T189[:], op0=ALU.add, op1=ALU.mult)
+  AC(T186[:], T186[:], ACT.Exp)
+  T205 = PP([128, 512], F, tag='h_0', bufs=1)
+  M(T205[:], T23, T24, 768, T19, T20, 1, 1)
+  ST(out=T187[:], in0=T181[:, 0, :], scalar=T118[:, 2:3], in1=T187[:], op0=ALU.mult, op1=ALU.add)
+  T200 = PP([128, 512], F, tag='h_3', bufs=1)
+  M(T200[:], T23, T24, 128, T19, T20, 1, 1)
+  T198 = AQ.tile([128, 512], F, tag='r_0', bufs=1)
+  ST(out=T198[:], in0=T197[:], scalar=1.0, in1=T196[:], op0=ALU.add, op1=ALU.mult)
+  ST(out=T193[:], in0=T181[:, 1, :], scalar=T118[:, 3:4], in1=T193[:], op0=ALU.mult, op1=ALU.add)
+  T206 = PP([128, 512], F, tag='h_1', bufs=1)
+  M(T206[:], T23, T24, 256, T19, T20, 1, 1)
+  TT(out=T164[:, 0, :], in0=T164[:, 0, :], in1=T187[:], op=ALU.mult)
+  T194 = PP([128, 2, 512], B, tag='x', bufs=1)
+  TR(T194[:, 0, 0:128], T16[:, 0, 0:128], T3[:])
+  T201 = AQ.tile([128, 512], F, tag='th_2', bufs=1)
+  AC(T201[:], T199[:], ACT.Tanh, scale=0.5)
+  nc.gpsimd.tensor_tensor(out=T119[:, 3, :], in0=T186[:, 0, :], in1=T186[:, 1, :], op=ALU.add)
+  TR(T194[:, 0, 128:256], T16[:, 1, 0:128], T3[:])
+  TR(T194[:, 0, 256:384], T16[:, 2, 0:128], T3[:])
+  TR(T194[:, 0, 384:512], T16[:, 3, 0:128], T3[:])
+  TR(T194[:, 1, 0:128], T16[:, 0, 128:256], T3[:])
   T32 = KP([128, 1024], U, tag='w2q2_codes', bufs=1, align_bytes=64)
   T33 = KP([128, 1024], U8, tag='w2q2_scales', bufs=1, align_bytes=64)
-  Q(T32[:, 0:512], T33[:, 0:512], T222[:].rearrange(S9))
-  AC(T182[:], T182[:], ACT.Exp)
-  T186 = PP([128, 512], F, tag='l_1', bufs=1)
-  M(T186[:], T12, T13, 1664, T8, T9, 1, 0)
-  M(T186[:], T21, T22, 1664, T17, T18, 0, 0)
-  T197 = AQ.tile([128, 512], F, tag='top_1', bufs=1)
-  TT(out=T197[:], in0=T185[:], in1=T183[:], op=ALU.max)
-  M(T186[:], T30, T31, 1664, T26, T27, 0, 0)
-  M(T186[:], T39, T40, 1664, T35, T36, 0, 1)
-  ST(out=T192[:], in0=T188[:, 0, :], scalar=T134[:, 0:1], in1=T192[:], op0=ALU.mult, op1=ALU.add)
-  T187 = PP([128, 512], F, tag='l_2', bufs=1)
-  M(T187[:], T12, T13, 1920, T8, T9, 1, 0)
-  M(T187[:], T21, T22, 1920, T17, T18, 0, 0)
-  TT(out=T197[:], in0=T186[:], in1=T197[:], op=ALU.max)
-  M(T187[:], T30, T31, 1920, T26, T27, 0, 0)
-  M(T187[:], T39, T40, 1920, T35, T36, 0, 1)
-  TT(out=T151[:, 0, :], in0=T151[:, 0, :], in1=T192[:], op=ALU.mult)
-  T195 = AQ.tile([128, 512], F, tag='th_1', bufs=1)
-  AC(T195[:], T193[:], ACT.Tanh, scale=0.5)
-  nc.gpsimd.tensor_tensor(out=T135[:, 2, :], in0=T182[:, 0, :], in1=T182[:, 1, :], op=ALU.add)
-  T201 = PP([128, 512], F, tag='h_1', bufs=1)
-  M(T201[:], T14, T15, 256, T10, T11, 1, 1)
-  TT(out=T197[:], in0=T187[:], in1=T197[:], op=ALU.max)
-  T202 = AQ.tile([128, 512], F, tag='th_2', bufs=1)
-  AC(T202[:], T200[:], ACT.Tanh, scale=0.5)
-  T208 = PP([128, 512], F, tag='h_2', bufs=1)
-  M(T208[:], T14, T15, 896, T10, T11, 1, 1)
-  T198 = AQ.tile([128, 512], F, tag='r_1', bufs=1)
-  ST(out=T198[:], in0=T195[:], scalar=1.0, in1=T194[:], op0=ALU.add, op1=ALU.mult)
-  T228 = AQ.tile([128, 512, 4], B, tag='grouped_0', bufs=1, align_bytes=64)
-  SC(T228[:], T212[:].rearrange(S13))
-  nc.gpsimd.tensor_tensor(out=T135[:, 2, :], in0=T135[:, 2, :], in1=T182[:, 2, :], op=ALU.add)
-  T206 = AQ.tile([128, 4, 512], F, tag='f8_3', bufs=1)
-  TT(out=T206[:, 1, :], in0=T185[:], in1=T197[:], op=ALU.subtract)
-  T209 = PP([128, 512], F, tag='h_3', bufs=1)
-  M(T209[:], T14, T15, 384, T10, T11, 1, 1)
-  TT(out=T206[:, 2, :], in0=T186[:], in1=T197[:], op=ALU.subtract)
-  T204 = PP([128, 256, 4], B, tag='l_0', bufs=1)
-  MT(T204[:, 0:128, :], lhsT=T3[:], rhs=T141[:, :, 0:128].rearrange(S13), start=True, stop=True)
-  MT(T204[:, 128:256, :], lhsT=T3[:], rhs=T141[:, :, 128:256].rearrange(S13), start=True, stop=True)
-  nc.gpsimd.tensor_tensor(out=T135[:, 2, :], in0=T135[:, 2, :], in1=T182[:, 3, :], op=ALU.add)
-  TT(out=T206[:, 3, :], in0=T187[:], in1=T197[:], op=ALU.subtract)
-  T205 = PP([128, 256, 4], B, tag='l_1', bufs=1)
-  MT(T205[:, 0:128, :], lhsT=T3[:], rhs=T141[:, :, 256:384].rearrange(S13), start=True, stop=True)
-  MT(T205[:, 128:256, :], lhsT=T3[:], rhs=T141[:, :, 384:512].rearrange(S13), start=True, stop=True)
-  TT(out=T206[:, 0, :], in0=T183[:], in1=T197[:], op=ALU.subtract)
-  T203 = AQ.tile([128, 512, 4], B, tag='grouped_1', bufs=1, align_bytes=64)
-  SC(T203[:, 0:256, :], T204[:])
-  T233 = AQ.tile([128, 4, 512], B, tag='w2_raw_0', bufs=1)
-  DM(out=T233[:], in_=w2[3, :, 0:512].rearrange(S1, j=4))
-  T234 = AQ.tile([128, 4, 512], B, tag='w2_raw_1', bufs=1)
-  DM(out=T234[:], in_=w2[3, :, 512:1024].rearrange(S1, j=4))
-  T207 = AQ.tile([128, 512], F, tag='r_2', bufs=1)
-  ST(out=T207[:], in0=T202[:], scalar=1.0, in1=T201[:], op0=ALU.add, op1=ALU.mult)
-  SC(T203[:, 256:512, :], T205[:])
-  ST(out=T198[:], in0=T188[:, 1, :], scalar=T134[:, 1:2], in1=T198[:], op0=ALU.mult, op1=ALU.add)
-  T216 = PP([128, 512], F, tag='h_1', bufs=1)
-  M(T216[:], T23, T24, 0, T19, T20, 1, 1)
-  T210 = AQ.tile([128, 512], F, tag='th_0', bufs=1)
-  AC(T210[:], T208[:], ACT.Tanh, scale=0.5)
-  Q(T23[:, 512:1024], T24[:, 512:1024], T203[:].rearrange(S9))
-  T199 = PP([128, 2, 512], B, tag='x', bufs=1)
-  TR(T199[:, 0, 0:128], T7[:, 0, 256:384], T3[:])
-  AC(T206[:], T206[:], ACT.Exp)
-  TR(T199[:, 0, 128:256], T7[:, 1, 256:384], T3[:])
-  TR(T199[:, 0, 256:384], T7[:, 2, 256:384], T3[:])
-  TR(T199[:, 0, 384:512], T7[:, 3, 256:384], T3[:])
-  TR(T199[:, 1, 0:128], T7[:, 0, 384:512], T3[:])
-  T213 = AQ.tile([128, 512], F, tag='r_3', bufs=1)
-  ST(out=T213[:], in0=T210[:], scalar=1.0, in1=T209[:], op0=ALU.add, op1=ALU.mult)
-  TR(T199[:, 1, 128:256], T7[:, 1, 384:512], T3[:])
-  TR(T199[:, 1, 256:384], T7[:, 2, 384:512], T3[:])
-  TR(T199[:, 1, 384:512], T7[:, 3, 384:512], T3[:])
-  T215 = PP([128, 512], F, tag='h_0', bufs=1)
-  M(T215[:], T23, T24, 512, T19, T20, 1, 1)
-  ST(out=T207[:], in0=T199[:, 0, :], scalar=T134[:, 2:3], in1=T207[:], op0=ALU.mult, op1=ALU.add)
-  T219 = PP([128, 512], F, tag='h_2', bufs=1)
-  M(T219[:], T23, T24, 640, T19, T20, 1, 1)
-  T220 = PP([128, 512], F, tag='h_3', bufs=1)
-  M(T220[:], T23, T24, 128, T19, T20, 1, 1)
-  TT(out=T162[:, 0, :], in0=T162[:, 0, :], in1=T198[:], op=ALU.mult)
-  ST(out=T213[:], in0=T199[:, 1, :], scalar=T134[:, 3:4], in1=T213[:], op0=ALU.mult, op1=ALU.add)
-  T245 = PP([128, 256, 4], B, tag='l_2', bufs=1)
-  MT(T245[:, 0:128, :], lhsT=T3[:], rhs=T233[:, :, 0:128].rearrange(S13), start=True, stop=True)
-  T217 = AQ.tile([128, 512], F, tag='th_1', bufs=1)
-  AC(T217[:], T215[:], ACT.Tanh, scale=0.5)
-  nc.gpsimd.tensor_tensor(out=T135[:, 3, :], in0=T206[:, 0, :], in1=T206[:, 1, :], op=ALU.add)
-  MT(T245[:, 128:256, :], lhsT=T3[:], rhs=T233[:, :, 128:256].rearrange(S13), start=True, stop=True)
-  TT(out=T182[:, 0, :], in0=T182[:, 0, :], in1=T207[:], op=ALU.mult)
-  T246 = PP([128, 256, 4], B, tag='l_0', bufs=1)
-  MT(T246[:, 0:128, :], lhsT=T3[:], rhs=T233[:, :, 256:384].rearrange(S13), start=True, stop=True)
-  T221 = AQ.tile([128, 512], F, tag='th_2', bufs=1)
-  AC(T221[:], T219[:], ACT.Tanh, scale=0.5)
-  T214 = PP([128, 2, 512], B, tag='x', bufs=1)
-  TR(T214[:, 0, 0:128], T16[:, 0, 0:128], T3[:])
-  TR(T214[:, 0, 128:256], T16[:, 1, 0:128], T3[:])
-  T218 = AQ.tile([128, 512], F, tag='r_0', bufs=1)
-  ST(out=T218[:], in0=T217[:], scalar=1.0, in1=T216[:], op0=ALU.add, op1=ALU.mult)
-  TR(T214[:, 0, 256:384], T16[:, 2, 0:128], T3[:])
-  TR(T214[:, 0, 384:512], T16[:, 3, 0:128], T3[:])
-  TR(T214[:, 1, 0:128], T16[:, 0, 128:256], T3[:])
-  T244 = AQ.tile([128, 512, 4], B, tag='grouped_1', bufs=1, align_bytes=64)
-  SC(T244[:, 0:256, :], T245[:])
-  TR(T214[:, 1, 128:256], T16[:, 1, 128:256], T3[:])
-  TR(T214[:, 1, 256:384], T16[:, 2, 128:256], T3[:])
-  TR(T214[:, 1, 384:512], T16[:, 3, 128:256], T3[:])
-  T225 = PP([128, 512], F, tag='h_0', bufs=1)
-  M(T225[:], T23, T24, 768, T19, T20, 1, 1)
-  nc.gpsimd.tensor_tensor(out=T135[:, 3, :], in0=T135[:, 3, :], in1=T206[:, 2, :], op=ALU.add)
-  T223 = AQ.tile([128, 512], F, tag='r_1', bufs=1)
-  ST(out=T223[:], in0=T221[:], scalar=1.0, in1=T220[:], op0=ALU.add, op1=ALU.mult)
-  T252 = AQ.tile([128, 512, 4], B, tag='grouped_2', bufs=1, align_bytes=64)
-  SC(T252[:], T234[:].rearrange(S13))
-  T226 = PP([128, 512], F, tag='h_1', bufs=1)
-  M(T226[:], T23, T24, 256, T19, T20, 1, 1)
-  T230 = PP([128, 512], F, tag='h_2', bufs=1)
-  M(T230[:], T23, T24, 896, T19, T20, 1, 1)
-  ST(out=T218[:], in0=T214[:, 0, :], scalar=T134[:, 4:5], in1=T218[:], op0=ALU.mult, op1=ALU.add)
-  T231 = PP([128, 512], F, tag='h_3', bufs=1)
-  M(T231[:], T23, T24, 384, T19, T20, 1, 1)
-  MT(T246[:, 128:256, :], lhsT=T3[:], rhs=T233[:, :, 384:512].rearrange(S13), start=True, stop=True)
-  TT(out=T206[:, 0, :], in0=T206[:, 0, :], in1=T213[:], op=ALU.mult)
-  nc.gpsimd.tensor_tensor(out=T135[:, 3, :], in0=T135[:, 3, :], in1=T206[:, 3, :], op=ALU.add)
-  ST(out=T223[:], in0=T214[:, 1, :], scalar=T134[:, 5:6], in1=T223[:], op0=ALU.mult, op1=ALU.add)
-  Q(T32[:, 512:1024], T33[:, 512:1024], T228[:].rearrange(S9))
-  T224 = PP([128, 2, 512], B, tag='x', bufs=1)
-  TR(T224[:, 0, 0:128], T16[:, 0, 256:384], T3[:])
-  TR(T224[:, 0, 128:256], T16[:, 1, 256:384], T3[:])
-  TR(T224[:, 0, 256:384], T16[:, 2, 256:384], T3[:])
-  T227 = AQ.tile([128, 512], F, tag='th_0', bufs=1)
-  AC(T227[:], T225[:], ACT.Tanh, scale=0.5)
-  TR(T224[:, 0, 384:512], T16[:, 3, 256:384], T3[:])
-  TR(T224[:, 1, 0:128], T16[:, 0, 384:512], T3[:])
-  TT(out=T151[:, 1, :], in0=T151[:, 1, :], in1=T218[:], op=ALU.mult)
-  TR(T224[:, 1, 128:256], T16[:, 1, 384:512], T3[:])
-  TR(T224[:, 1, 256:384], T16[:, 2, 384:512], T3[:])
-  TR(T224[:, 1, 384:512], T16[:, 3, 384:512], T3[:])
-  T232 = AQ.tile([128, 512], F, tag='th_1', bufs=1)
-  AC(T232[:], T230[:], ACT.Tanh, scale=0.5)
-  T237 = PP([128, 512], F, tag='h_0', bufs=1)
-  M(T237[:], T32, T33, 512, T28, T29, 1, 1)
-  T229 = AQ.tile([128, 512], F, tag='r_2', bufs=1)
-  ST(out=T229[:], in0=T227[:], scalar=1.0, in1=T226[:], op0=ALU.add, op1=ALU.mult)
-  nc.gpsimd.tensor_tensor(out=T151[:, 0, :], in0=T151[:, 0, :], in1=T151[:, 1, :], op=ALU.add)
-  SC(T244[:, 256:512, :], T246[:])
-  T241 = PP([128, 512], F, tag='h_2', bufs=1)
-  M(T241[:], T32, T33, 640, T28, T29, 1, 1)
-  T235 = AQ.tile([128, 512], F, tag='r_3', bufs=1)
-  ST(out=T235[:], in0=T232[:], scalar=1.0, in1=T231[:], op0=ALU.add, op1=ALU.mult)
-  T238 = PP([128, 512], F, tag='h_1', bufs=1)
-  M(T238[:], T32, T33, 0, T28, T29, 1, 1)
-  T239 = AQ.tile([128, 512], F, tag='th_2', bufs=1)
-  AC(T239[:], T237[:], ACT.Tanh, scale=0.5)
-  ST(out=T229[:], in0=T224[:, 0, :], scalar=T134[:, 6:7], in1=T229[:], op0=ALU.mult, op1=ALU.add)
-  T242 = PP([128, 512], F, tag='h_3', bufs=1)
-  M(T242[:], T32, T33, 128, T28, T29, 1, 1)
-  T243 = AQ.tile([128, 512], F, tag='th_0', bufs=1)
-  AC(T243[:], T241[:], ACT.Tanh, scale=0.5)
-  T249 = PP([128, 512], F, tag='h_0', bufs=1)
-  M(T249[:], T32, T33, 768, T28, T29, 1, 1)
-  TT(out=T162[:, 1, :], in0=T162[:, 1, :], in1=T223[:], op=ALU.mult)
-  T254 = PP([128, 512], F, tag='h_2', bufs=1)
-  M(T254[:], T32, T33, 896, T28, T29, 1, 1)
-  T251 = AQ.tile([128, 512], F, tag='th_1', bufs=1)
-  AC(T251[:], T249[:], ACT.Tanh, scale=0.5)
-  T240 = AQ.tile([128, 512], F, tag='r_0', bufs=1)
-  ST(out=T240[:], in0=T239[:], scalar=1.0, in1=T238[:], op0=ALU.add, op1=ALU.mult)
-  nc.gpsimd.tensor_tensor(out=T162[:, 0, :], in0=T162[:, 0, :], in1=T162[:, 1, :], op=ALU.add)
-  ST(out=T235[:], in0=T224[:, 1, :], scalar=T134[:, 7:8], in1=T235[:], op0=ALU.mult, op1=ALU.add)
-  T250 = PP([128, 512], F, tag='h_1', bufs=1)
-  M(T250[:], T32, T33, 256, T28, T29, 1, 1)
-  T256 = AQ.tile([128, 512], F, tag='th_2', bufs=1)
-  AC(T256[:], T254[:], ACT.Tanh, scale=0.5)
-  TT(out=T182[:, 1, :], in0=T182[:, 1, :], in1=T229[:], op=ALU.mult)
-  T236 = PP([128, 2, 512], B, tag='x', bufs=1)
-  TR(T236[:, 0, 0:128], T25[:, 0, 0:128], T3[:])
-  AC(T135[:, 0:4, :], T135[:, 0:4, :], ACT.Ln, scale=2.0)
-  TR(T236[:, 0, 128:256], T25[:, 1, 0:128], T3[:])
-  TR(T236[:, 0, 256:384], T25[:, 2, 0:128], T3[:])
-  TR(T236[:, 0, 384:512], T25[:, 3, 0:128], T3[:])
-  TR(T236[:, 1, 0:128], T25[:, 0, 128:256], T3[:])
-  T247 = AQ.tile([128, 512], F, tag='r_1', bufs=1)
-  ST(out=T247[:], in0=T243[:], scalar=1.0, in1=T242[:], op0=ALU.add, op1=ALU.mult)
-  TR(T236[:, 1, 128:256], T25[:, 1, 128:256], T3[:])
-  TR(T236[:, 1, 256:384], T25[:, 2, 128:256], T3[:])
-  nc.gpsimd.tensor_tensor(out=T182[:, 0, :], in0=T182[:, 0, :], in1=T182[:, 1, :], op=ALU.add)
-  TR(T236[:, 1, 384:512], T25[:, 3, 128:256], T3[:])
-  ST(out=T240[:], in0=T236[:, 0, :], scalar=T134[:, 8:9], in1=T240[:], op0=ALU.mult, op1=ALU.add)
-  T255 = PP([128, 512], F, tag='h_3', bufs=1)
-  M(T255[:], T32, T33, 384, T28, T29, 1, 1)
-  TT(out=T206[:, 1, :], in0=T206[:, 1, :], in1=T235[:], op=ALU.mult)
-  T253 = AQ.tile([128, 512], F, tag='r_2', bufs=1)
-  ST(out=T253[:], in0=T251[:], scalar=1.0, in1=T250[:], op0=ALU.add, op1=ALU.mult)
-  nc.gpsimd.tensor_tensor(out=T206[:, 0, :], in0=T206[:, 0, :], in1=T206[:, 1, :], op=ALU.add)
+  Q(T32[:, 0:512], T33[:, 0:512], T202[:].rearrange(S9))
+  TR(T194[:, 1, 128:256], T16[:, 1, 128:256], T3[:])
+  TR(T194[:, 1, 256:384], T16[:, 2, 128:256], T3[:])
+  TR(T194[:, 1, 384:512], T16[:, 3, 128:256], T3[:])
+  T207 = AQ.tile([128, 512], F, tag='th_0', bufs=1)
+  AC(T207[:], T205[:], ACT.Tanh, scale=0.5)
+  T210 = PP([128, 512], F, tag='h_2', bufs=1)
+  M(T210[:], T23, T24, 896, T19, T20, 1, 1)
+  T203 = AQ.tile([128, 512], F, tag='r_1', bufs=1)
+  ST(out=T203[:], in0=T201[:], scalar=1.0, in1=T200[:], op0=ALU.add, op1=ALU.mult)
+  T224 = AQ.tile([128, 512, 4], B, tag='grouped_1', bufs=1, align_bytes=64)
+  SC(T224[:].rearrange(S13, i=4), T213[:].rearrange(S14, i=4))
+  nc.gpsimd.tensor_tensor(out=T119[:, 3, :], in0=T119[:, 3, :], in1=T186[:, 2, :], op=ALU.add)
+  ST(out=T198[:], in0=T194[:, 0, :], scalar=T118[:, 4:5], in1=T198[:], op0=ALU.mult, op1=ALU.add)
+  T211 = PP([128, 512], F, tag='h_3', bufs=1)
+  M(T211[:], T23, T24, 384, T19, T20, 1, 1)
+  TT(out=T186[:, 0, :], in0=T186[:, 0, :], in1=T193[:], op=ALU.mult)
+  T209 = AQ.tile([128, 512], F, tag='r_2', bufs=1)
+  ST(out=T209[:], in0=T207[:], scalar=1.0, in1=T206[:], op0=ALU.add, op1=ALU.mult)
+  nc.gpsimd.tensor_tensor(out=T119[:, 3, :], in0=T119[:, 3, :], in1=T186[:, 3, :], op=ALU.add)
+  ST(out=T203[:], in0=T194[:, 1, :], scalar=T118[:, 5:6], in1=T203[:], op0=ALU.mult, op1=ALU.add)
+  T218 = PP([128, 512], F, tag='h_1', bufs=1)
+  M(T218[:], T32, T33, 0, T28, T29, 1, 1)
+  T212 = AQ.tile([128, 512], F, tag='th_1', bufs=1)
+  AC(T212[:], T210[:], ACT.Tanh, scale=0.5)
+  Q(T32[:, 512:1024], T33[:, 512:1024], T208[:].rearrange(S9))
+  T204 = PP([128, 2, 512], B, tag='x', bufs=1)
+  TR(T204[:, 0, 0:128], T16[:, 0, 256:384], T3[:])
+  TR(T204[:, 0, 128:256], T16[:, 1, 256:384], T3[:])
+  TR(T204[:, 0, 256:384], T16[:, 2, 256:384], T3[:])
+  T230 = AQ.tile([128, 512, 4], B, tag='grouped_2', bufs=1, align_bytes=64)
+  SC(T230[:].rearrange(S13, i=4), T214[:].rearrange(S14, i=4))
+  TR(T204[:, 0, 384:512], T16[:, 3, 256:384], T3[:])
+  TR(T204[:, 1, 0:128], T16[:, 0, 384:512], T3[:])
+  TT(out=T135[:, 1, :], in0=T135[:, 1, :], in1=T198[:], op=ALU.mult)
+  TR(T204[:, 1, 128:256], T16[:, 1, 384:512], T3[:])
+  TR(T204[:, 1, 256:384], T16[:, 2, 384:512], T3[:])
+  TR(T204[:, 1, 384:512], T16[:, 3, 384:512], T3[:])
+  T217 = PP([128, 512], F, tag='h_0', bufs=1)
+  M(T217[:], T32, T33, 512, T28, T29, 1, 1)
+  T215 = AQ.tile([128, 512], F, tag='r_3', bufs=1)
+  ST(out=T215[:], in0=T212[:], scalar=1.0, in1=T211[:], op0=ALU.add, op1=ALU.mult)
+  T221 = PP([128, 512], F, tag='h_2', bufs=1)
+  M(T221[:], T32, T33, 640, T28, T29, 1, 1)
+  nc.gpsimd.tensor_tensor(out=T135[:, 0, :], in0=T135[:, 0, :], in1=T135[:, 1, :], op=ALU.add)
+  ST(out=T209[:], in0=T204[:, 0, :], scalar=T118[:, 6:7], in1=T209[:], op0=ALU.mult, op1=ALU.add)
+  T222 = PP([128, 512], F, tag='h_3', bufs=1)
+  M(T222[:], T32, T33, 128, T28, T29, 1, 1)
+  TT(out=T146[:, 1, :], in0=T146[:, 1, :], in1=T203[:], op=ALU.mult)
+  ST(out=T215[:], in0=T204[:, 1, :], scalar=T118[:, 7:8], in1=T215[:], op0=ALU.mult, op1=ALU.add)
+  nc.gpsimd.tensor_tensor(out=T146[:, 0, :], in0=T146[:, 0, :], in1=T146[:, 1, :], op=ALU.add)
+  T219 = AQ.tile([128, 512], F, tag='th_2', bufs=1)
+  AC(T219[:], T217[:], ACT.Tanh, scale=0.5)
+  TT(out=T164[:, 1, :], in0=T164[:, 1, :], in1=T209[:], op=ALU.mult)
+  T216 = PP([128, 2, 512], B, tag='x', bufs=1)
+  TR(T216[:, 0, 0:128], T25[:, 0, 0:128], T3[:])
+  T223 = AQ.tile([128, 512], F, tag='th_0', bufs=1)
+  AC(T223[:], T221[:], ACT.Tanh, scale=0.5)
+  TR(T216[:, 0, 128:256], T25[:, 1, 0:128], T3[:])
+  TR(T216[:, 0, 256:384], T25[:, 2, 0:128], T3[:])
+  TR(T216[:, 0, 384:512], T25[:, 3, 0:128], T3[:])
+  TR(T216[:, 1, 0:128], T25[:, 0, 128:256], T3[:])
+  T220 = AQ.tile([128, 512], F, tag='r_0', bufs=1)
+  ST(out=T220[:], in0=T219[:], scalar=1.0, in1=T218[:], op0=ALU.add, op1=ALU.mult)
+  TR(T216[:, 1, 128:256], T25[:, 1, 128:256], T3[:])
+  TR(T216[:, 1, 256:384], T25[:, 2, 128:256], T3[:])
+  TR(T216[:, 1, 384:512], T25[:, 3, 128:256], T3[:])
+  nc.gpsimd.tensor_tensor(out=T164[:, 0, :], in0=T164[:, 0, :], in1=T164[:, 1, :], op=ALU.add)
+  T227 = PP([128, 512], F, tag='h_0', bufs=1)
+  M(T227[:], T32, T33, 768, T28, T29, 1, 1)
+  T225 = AQ.tile([128, 512], F, tag='r_1', bufs=1)
+  ST(out=T225[:], in0=T223[:], scalar=1.0, in1=T222[:], op0=ALU.add, op1=ALU.mult)
+  T232 = PP([128, 512], F, tag='h_2', bufs=1)
+  M(T232[:], T32, T33, 896, T28, T29, 1, 1)
+  T229 = AQ.tile([128, 512], F, tag='th_1', bufs=1)
+  AC(T229[:], T227[:], ACT.Tanh, scale=0.5)
+  T228 = PP([128, 512], F, tag='h_1', bufs=1)
+  M(T228[:], T32, T33, 256, T28, T29, 1, 1)
+  ST(out=T220[:], in0=T216[:, 0, :], scalar=T118[:, 8:9], in1=T220[:], op0=ALU.mult, op1=ALU.add)
+  T233 = PP([128, 512], F, tag='h_3', bufs=1)
+  M(T233[:], T32, T33, 384, T28, T29, 1, 1)
+  T234 = AQ.tile([128, 512], F, tag='th_2', bufs=1)
+  AC(T234[:], T232[:], ACT.Tanh, scale=0.5)
+  TT(out=T186[:, 1, :], in0=T186[:, 1, :], in1=T215[:], op=ALU.mult)
+  AC(T119[:, 0:4, :], T119[:, 0:4, :], ACT.Ln, scale=2.0)
+  T231 = AQ.tile([128, 512], F, tag='r_2', bufs=1)
+  ST(out=T231[:], in0=T229[:], scalar=1.0, in1=T228[:], op0=ALU.add, op1=ALU.mult)
+  nc.gpsimd.tensor_tensor(out=T186[:, 0, :], in0=T186[:, 0, :], in1=T186[:, 1, :], op=ALU.add)
   T41 = KP([128, 1024], U, tag='w2q3_codes', bufs=1, align_bytes=64)
   T42 = KP([128, 1024], U8, tag='w2q3_scales', bufs=1, align_bytes=64)
-  Q(T41[:, 0:512], T42[:, 0:512], T244[:].rearrange(S9))
-  ST(out=T247[:], in0=T236[:, 1, :], scalar=T134[:, 9:10], in1=T247[:], op0=ALU.mult, op1=ALU.add)
-  T260 = PP([128, 512], F, tag='h_1', bufs=1)
-  M(T260[:], T41, T42, 0, T37, T38, 1, 1)
-  Q(T41[:, 512:1024], T42[:, 512:1024], T252[:].rearrange(S9))
-  T248 = PP([128, 2, 512], B, tag='x', bufs=1)
-  TR(T248[:, 0, 0:128], T25[:, 0, 256:384], T3[:])
-  AC(T135[:, 0:4, :], T135[:, 0:4, :], ACT.Exp, scale=-1.0)
-  TR(T248[:, 0, 128:256], T25[:, 1, 256:384], T3[:])
-  TR(T248[:, 0, 256:384], T25[:, 2, 256:384], T3[:])
-  TR(T248[:, 0, 384:512], T25[:, 3, 256:384], T3[:])
-  TR(T248[:, 1, 0:128], T25[:, 0, 384:512], T3[:])
-  TT(out=T151[:, 2, :], in0=T151[:, 2, :], in1=T240[:], op=ALU.mult)
-  TR(T248[:, 1, 128:256], T25[:, 1, 384:512], T3[:])
-  TR(T248[:, 1, 256:384], T25[:, 2, 384:512], T3[:])
-  TR(T248[:, 1, 384:512], T25[:, 3, 384:512], T3[:])
-  T259 = PP([128, 512], F, tag='h_0', bufs=1)
-  M(T259[:], T41, T42, 512, T37, T38, 1, 1)
-  T257 = AQ.tile([128, 512], F, tag='r_3', bufs=1)
-  ST(out=T257[:], in0=T256[:], scalar=1.0, in1=T255[:], op0=ALU.add, op1=ALU.mult)
-  T263 = PP([128, 512], F, tag='h_2', bufs=1)
-  M(T263[:], T41, T42, 640, T37, T38, 1, 1)
-  nc.gpsimd.tensor_tensor(out=T151[:, 0, :], in0=T151[:, 0, :], in1=T151[:, 2, :], op=ALU.add)
-  ST(out=T253[:], in0=T248[:, 0, :], scalar=T134[:, 10:11], in1=T253[:], op0=ALU.mult, op1=ALU.add)
-  T264 = PP([128, 512], F, tag='h_3', bufs=1)
-  M(T264[:], T41, T42, 128, T37, T38, 1, 1)
-  TT(out=T162[:, 2, :], in0=T162[:, 2, :], in1=T247[:], op=ALU.mult)
-  ST(out=T257[:], in0=T248[:, 1, :], scalar=T134[:, 11:12], in1=T257[:], op0=ALU.mult, op1=ALU.add)
-  nc.gpsimd.tensor_tensor(out=T162[:, 0, :], in0=T162[:, 0, :], in1=T162[:, 2, :], op=ALU.add)
-  TT(out=T182[:, 2, :], in0=T182[:, 2, :], in1=T253[:], op=ALU.mult)
-  T258 = PP([128, 2, 512], B, tag='x', bufs=1)
-  TR(T258[:, 0, 0:128], T34[:, 0, 0:128], T3[:])
-  TR(T258[:, 0, 128:256], T34[:, 1, 0:128], T3[:])
-  TR(T258[:, 0, 256:384], T34[:, 2, 0:128], T3[:])
-  TR(T258[:, 0, 384:512], T34[:, 3, 0:128], T3[:])
-  TR(T258[:, 1, 0:128], T34[:, 0, 128:256], T3[:])
-  TT(out=T206[:, 2, :], in0=T206[:, 2, :], in1=T257[:], op=ALU.mult)
-  TR(T258[:, 1, 128:256], T34[:, 1, 128:256], T3[:])
-  T261 = AQ.tile([128, 512], F, tag='th_0', bufs=1)
-  AC(T261[:], T259[:], ACT.Tanh, scale=0.5)
-  TR(T258[:, 1, 256:384], T34[:, 2, 128:256], T3[:])
-  TR(T258[:, 1, 384:512], T34[:, 3, 128:256], T3[:])
-  nc.gpsimd.tensor_tensor(out=T182[:, 0, :], in0=T182[:, 0, :], in1=T182[:, 2, :], op=ALU.add)
-  T265 = AQ.tile([128, 512], F, tag='th_1', bufs=1)
-  AC(T265[:], T263[:], ACT.Tanh, scale=0.5)
-  T262 = AQ.tile([128, 512], F, tag='r_0', bufs=1)
-  ST(out=T262[:], in0=T261[:], scalar=1.0, in1=T260[:], op0=ALU.add, op1=ALU.mult)
-  T268 = PP([128, 512], F, tag='h_0', bufs=1)
-  M(T268[:], T41, T42, 768, T37, T38, 1, 1)
-  T272 = PP([128, 512], F, tag='h_2', bufs=1)
-  M(T272[:], T41, T42, 896, T37, T38, 1, 1)
-  T266 = AQ.tile([128, 512], F, tag='r_1', bufs=1)
-  ST(out=T266[:], in0=T265[:], scalar=1.0, in1=T264[:], op0=ALU.add, op1=ALU.mult)
-  T270 = AQ.tile([128, 512], F, tag='th_2', bufs=1)
-  AC(T270[:], T268[:], ACT.Tanh, scale=0.5)
-  nc.gpsimd.tensor_tensor(out=T206[:, 0, :], in0=T206[:, 0, :], in1=T206[:, 2, :], op=ALU.add)
-  T269 = PP([128, 512], F, tag='h_1', bufs=1)
-  M(T269[:], T41, T42, 256, T37, T38, 1, 1)
-  ST(out=T262[:], in0=T258[:, 0, :], scalar=T134[:, 12:13], in1=T262[:], op0=ALU.mult, op1=ALU.add)
-  T274 = AQ.tile([128, 512], F, tag='th_0', bufs=1)
-  AC(T274[:], T272[:], ACT.Tanh, scale=0.5)
-  T273 = PP([128, 512], F, tag='h_3', bufs=1)
-  M(T273[:], T41, T42, 384, T37, T38, 1, 1)
-  T271 = AQ.tile([128, 512], F, tag='r_2', bufs=1)
-  ST(out=T271[:], in0=T270[:], scalar=1.0, in1=T269[:], op0=ALU.add, op1=ALU.mult)
-  ST(out=T266[:], in0=T258[:, 1, :], scalar=T134[:, 13:14], in1=T266[:], op0=ALU.mult, op1=ALU.add)
-  TT(out=T151[:, 3, :], in0=T151[:, 3, :], in1=T262[:], op=ALU.mult)
-  T267 = PP([128, 2, 512], B, tag='x', bufs=1)
-  TR(T267[:, 0, 0:128], T34[:, 0, 256:384], T3[:])
-  TR(T267[:, 0, 128:256], T34[:, 1, 256:384], T3[:])
-  TR(T267[:, 0, 256:384], T34[:, 2, 256:384], T3[:])
-  TR(T267[:, 0, 384:512], T34[:, 3, 256:384], T3[:])
-  TR(T267[:, 1, 0:128], T34[:, 0, 384:512], T3[:])
-  T275 = AQ.tile([128, 512], F, tag='r_3', bufs=1)
-  ST(out=T275[:], in0=T274[:], scalar=1.0, in1=T273[:], op0=ALU.add, op1=ALU.mult)
-  TR(T267[:, 1, 128:256], T34[:, 1, 384:512], T3[:])
-  TR(T267[:, 1, 256:384], T34[:, 2, 384:512], T3[:])
-  TR(T267[:, 1, 384:512], T34[:, 3, 384:512], T3[:])
-  ST(out=T271[:], in0=T267[:, 0, :], scalar=T134[:, 14:15], in1=T271[:], op0=ALU.mult, op1=ALU.add)
-  TT(out=T162[:, 3, :], in0=T162[:, 3, :], in1=T266[:], op=ALU.mult)
-  TT(out=T151[:, 3, :], in0=T151[:, 0, :], in1=T151[:, 3, :], op=ALU.add)
-  ST(out=T275[:], in0=T267[:, 1, :], scalar=T134[:, 15:16], in1=T275[:], op0=ALU.mult, op1=ALU.add)
-  TT(out=T182[:, 3, :], in0=T182[:, 3, :], in1=T271[:], op=ALU.mult)
-  TT(out=T162[:, 3, :], in0=T162[:, 0, :], in1=T162[:, 3, :], op=ALU.add)
-  TT(out=T151[:, 3, :], in0=T151[:, 3, :], in1=T135[:, 0, :], op=ALU.mult)
-  TT(out=T206[:, 3, :], in0=T206[:, 3, :], in1=T275[:], op=ALU.mult)
-  T276 = PP([128, 4, 128], F, tag='l_1', bufs=1)
-  TR(T276[:, 0, :], T151[:, 3, 0:128], T0[:])
-  TR(T276[:, 1, :], T151[:, 3, 128:256], T0[:])
-  TR(T276[:, 2, :], T151[:, 3, 256:384], T0[:])
-  TR(T276[:, 3, :], T151[:, 3, 384:512], T0[:])
-  TT(out=T182[:, 3, :], in0=T182[:, 0, :], in1=T182[:, 3, :], op=ALU.add)
-  T277 = AQ.tile([128, 4, 128], F, tag='rows_0', bufs=1)
-  SC(T277[:], T276[:])
-  TT(out=T162[:, 3, :], in0=T162[:, 3, :], in1=T135[:, 1, :], op=ALU.mult)
-  DM(out=out[:, 0:128].rearrange(S3, p=128), in_=T277[:])
-  TT(out=T206[:, 3, :], in0=T206[:, 0, :], in1=T206[:, 3, :], op=ALU.add)
-  T278 = PP([128, 4, 128], F, tag='l_2', bufs=1)
-  TR(T278[:, 0, :], T162[:, 3, 0:128], T0[:])
-  TR(T278[:, 1, :], T162[:, 3, 128:256], T0[:])
-  TR(T278[:, 2, :], T162[:, 3, 256:384], T0[:])
-  TR(T278[:, 3, :], T162[:, 3, 384:512], T0[:])
-  TT(out=T182[:, 3, :], in0=T182[:, 3, :], in1=T135[:, 2, :], op=ALU.mult)
-  T279 = AQ.tile([128, 4, 128], F, tag='rows_1', bufs=1)
-  SC(T279[:], T278[:])
-  TT(out=T206[:, 3, :], in0=T206[:, 3, :], in1=T135[:, 3, :], op=ALU.mult)
-  T280 = PP([128, 4, 128], F, tag='l_0', bufs=1)
-  TR(T280[:, 0, :], T182[:, 3, 0:128], T0[:])
-  DM(out=out[:, 128:256].rearrange(S3, p=128), in_=T279[:])
-  TR(T280[:, 1, :], T182[:, 3, 128:256], T0[:])
-  TR(T280[:, 2, :], T182[:, 3, 256:384], T0[:])
-  TR(T280[:, 3, :], T182[:, 3, 384:512], T0[:])
-  T282 = PP([128, 4, 128], F, tag='l_1', bufs=1)
-  TR(T282[:, 0, :], T206[:, 3, 0:128], T0[:])
-  TR(T282[:, 1, :], T206[:, 3, 128:256], T0[:])
-  TR(T282[:, 2, :], T206[:, 3, 256:384], T0[:])
-  TR(T282[:, 3, :], T206[:, 3, 384:512], T0[:])
-  T281 = AQ.tile([128, 4, 128], F, tag='rows_0', bufs=1)
-  SC(T281[:], T280[:])
-  DM(out=out[:, 256:384].rearrange(S3, p=128), in_=T281[:])
-  T283 = AQ.tile([128, 4, 128], F, tag='rows_1', bufs=1)
-  SC(T283[:], T282[:])
-  DM(out=out[:, 384:512].rearrange(S3, p=128), in_=T283[:])
+  Q(T41[:, 0:512], T42[:, 0:512], T224[:].rearrange(S9))
+  ST(out=T225[:], in0=T216[:, 1, :], scalar=T118[:, 9:10], in1=T225[:], op0=ALU.mult, op1=ALU.add)
+  T238 = PP([128, 512], F, tag='h_1', bufs=1)
+  M(T238[:], T41, T42, 0, T37, T38, 1, 1)
+  Q(T41[:, 512:1024], T42[:, 512:1024], T230[:].rearrange(S9))
+  T226 = PP([128, 2, 512], B, tag='x', bufs=1)
+  TR(T226[:, 0, 0:128], T25[:, 0, 256:384], T3[:])
+  TR(T226[:, 0, 128:256], T25[:, 1, 256:384], T3[:])
+  TR(T226[:, 0, 256:384], T25[:, 2, 256:384], T3[:])
+  TR(T226[:, 0, 384:512], T25[:, 3, 256:384], T3[:])
+  TR(T226[:, 1, 0:128], T25[:, 0, 384:512], T3[:])
+  TT(out=T135[:, 2, :], in0=T135[:, 2, :], in1=T220[:], op=ALU.mult)
+  TR(T226[:, 1, 128:256], T25[:, 1, 384:512], T3[:])
+  TR(T226[:, 1, 256:384], T25[:, 2, 384:512], T3[:])
+  TR(T226[:, 1, 384:512], T25[:, 3, 384:512], T3[:])
+  T237 = PP([128, 512], F, tag='h_0', bufs=1)
+  M(T237[:], T41, T42, 512, T37, T38, 1, 1)
+  T235 = AQ.tile([128, 512], F, tag='r_3', bufs=1)
+  ST(out=T235[:], in0=T234[:], scalar=1.0, in1=T233[:], op0=ALU.add, op1=ALU.mult)
+  T241 = PP([128, 512], F, tag='h_2', bufs=1)
+  M(T241[:], T41, T42, 640, T37, T38, 1, 1)
+  nc.gpsimd.tensor_tensor(out=T135[:, 0, :], in0=T135[:, 0, :], in1=T135[:, 2, :], op=ALU.add)
+  ST(out=T231[:], in0=T226[:, 0, :], scalar=T118[:, 10:11], in1=T231[:], op0=ALU.mult, op1=ALU.add)
+  T242 = PP([128, 512], F, tag='h_3', bufs=1)
+  M(T242[:], T41, T42, 128, T37, T38, 1, 1)
+  T239 = AQ.tile([128, 512], F, tag='th_0', bufs=1)
+  AC(T239[:], T237[:], ACT.Tanh, scale=0.5)
+  TT(out=T146[:, 2, :], in0=T146[:, 2, :], in1=T225[:], op=ALU.mult)
+  AC(T119[:, 0:4, :], T119[:, 0:4, :], ACT.Exp, scale=-1.0)
+  T246 = PP([128, 512], F, tag='h_0', bufs=1)
+  M(T246[:], T41, T42, 768, T37, T38, 1, 1)
+  T240 = AQ.tile([128, 512], F, tag='r_0', bufs=1)
+  ST(out=T240[:], in0=T239[:], scalar=1.0, in1=T238[:], op0=ALU.add, op1=ALU.mult)
+  nc.gpsimd.tensor_tensor(out=T146[:, 0, :], in0=T146[:, 0, :], in1=T146[:, 2, :], op=ALU.add)
+  ST(out=T235[:], in0=T226[:, 1, :], scalar=T118[:, 11:12], in1=T235[:], op0=ALU.mult, op1=ALU.add)
+  T247 = PP([128, 512], F, tag='h_1', bufs=1)
+  M(T247[:], T41, T42, 256, T37, T38, 1, 1)
+  TT(out=T164[:, 2, :], in0=T164[:, 2, :], in1=T231[:], op=ALU.mult)
+  T236 = PP([128, 2, 512], B, tag='x', bufs=1)
+  TR(T236[:, 0, 0:128], T34[:, 0, 0:128], T3[:])
+  TR(T236[:, 0, 128:256], T34[:, 1, 0:128], T3[:])
+  TR(T236[:, 0, 256:384], T34[:, 2, 0:128], T3[:])
+  TR(T236[:, 0, 384:512], T34[:, 3, 0:128], T3[:])
+  TR(T236[:, 1, 0:128], T34[:, 0, 128:256], T3[:])
+  TT(out=T186[:, 2, :], in0=T186[:, 2, :], in1=T235[:], op=ALU.mult)
+  TR(T236[:, 1, 128:256], T34[:, 1, 128:256], T3[:])
+  TR(T236[:, 1, 256:384], T34[:, 2, 128:256], T3[:])
+  nc.gpsimd.tensor_tensor(out=T164[:, 0, :], in0=T164[:, 0, :], in1=T164[:, 2, :], op=ALU.add)
+  TR(T236[:, 1, 384:512], T34[:, 3, 128:256], T3[:])
+  ST(out=T240[:], in0=T236[:, 0, :], scalar=T118[:, 12:13], in1=T240[:], op0=ALU.mult, op1=ALU.add)
+  TT(out=T135[:, 3, :], in0=T135[:, 3, :], in1=T240[:], op=ALU.mult)
+  nc.gpsimd.tensor_tensor(out=T186[:, 0, :], in0=T186[:, 0, :], in1=T186[:, 2, :], op=ALU.add)
+  T243 = AQ.tile([128, 512], F, tag='th_1', bufs=1)
+  AC(T243[:], T241[:], ACT.Tanh, scale=0.5)
+  TT(out=T135[:, 3, :], in0=T135[:, 0, :], in1=T135[:, 3, :], op=ALU.add)
+  T248 = AQ.tile([128, 512], F, tag='th_2', bufs=1)
+  AC(T248[:], T246[:], ACT.Tanh, scale=0.5)
+  T250 = PP([128, 512], F, tag='h_2', bufs=1)
+  M(T250[:], T41, T42, 896, T37, T38, 1, 1)
+  T244 = AQ.tile([128, 512], F, tag='r_1', bufs=1)
+  ST(out=T244[:], in0=T243[:], scalar=1.0, in1=T242[:], op0=ALU.add, op1=ALU.mult)
+  T252 = AQ.tile([128, 512], F, tag='th_0', bufs=1)
+  AC(T252[:], T250[:], ACT.Tanh, scale=0.5)
+  T249 = AQ.tile([128, 512], F, tag='r_2', bufs=1)
+  ST(out=T249[:], in0=T248[:], scalar=1.0, in1=T247[:], op0=ALU.add, op1=ALU.mult)
+  T251 = PP([128, 512], F, tag='h_3', bufs=1)
+  M(T251[:], T41, T42, 384, T37, T38, 1, 1)
+  ST(out=T244[:], in0=T236[:, 1, :], scalar=T118[:, 13:14], in1=T244[:], op0=ALU.mult, op1=ALU.add)
+  T253 = AQ.tile([128, 512], F, tag='r_3', bufs=1)
+  ST(out=T253[:], in0=T252[:], scalar=1.0, in1=T251[:], op0=ALU.add, op1=ALU.mult)
+  T245 = PP([128, 2, 512], B, tag='x', bufs=1)
+  TR(T245[:, 0, 0:128], T34[:, 0, 256:384], T3[:])
+  TR(T245[:, 0, 128:256], T34[:, 1, 256:384], T3[:])
+  TR(T245[:, 0, 256:384], T34[:, 2, 256:384], T3[:])
+  TR(T245[:, 0, 384:512], T34[:, 3, 256:384], T3[:])
+  TR(T245[:, 1, 0:128], T34[:, 0, 384:512], T3[:])
+  TT(out=T146[:, 3, :], in0=T146[:, 3, :], in1=T244[:], op=ALU.mult)
+  TR(T245[:, 1, 128:256], T34[:, 1, 384:512], T3[:])
+  TR(T245[:, 1, 256:384], T34[:, 2, 384:512], T3[:])
+  TR(T245[:, 1, 384:512], T34[:, 3, 384:512], T3[:])
+  ST(out=T249[:], in0=T245[:, 0, :], scalar=T118[:, 14:15], in1=T249[:], op0=ALU.mult, op1=ALU.add)
+  ST(out=T253[:], in0=T245[:, 1, :], scalar=T118[:, 15:16], in1=T253[:], op0=ALU.mult, op1=ALU.add)
+  TT(out=T164[:, 3, :], in0=T164[:, 3, :], in1=T249[:], op=ALU.mult)
+  TT(out=T146[:, 3, :], in0=T146[:, 0, :], in1=T146[:, 3, :], op=ALU.add)
+  TT(out=T135[:, 3, :], in0=T135[:, 3, :], in1=T119[:, 0, :], op=ALU.mult)
+  TT(out=T186[:, 3, :], in0=T186[:, 3, :], in1=T253[:], op=ALU.mult)
+  T254 = PP([128, 4, 128], F, tag='l_0', bufs=1)
+  TR(T254[:, 0, :], T135[:, 3, 0:128], T0[:])
+  TR(T254[:, 1, :], T135[:, 3, 128:256], T0[:])
+  TR(T254[:, 2, :], T135[:, 3, 256:384], T0[:])
+  TR(T254[:, 3, :], T135[:, 3, 384:512], T0[:])
+  TT(out=T164[:, 3, :], in0=T164[:, 0, :], in1=T164[:, 3, :], op=ALU.add)
+  T255 = AQ.tile([128, 4, 128], F, tag='rows_0', bufs=1)
+  SC(T255[:], T254[:])
+  TT(out=T146[:, 3, :], in0=T146[:, 3, :], in1=T119[:, 1, :], op=ALU.mult)
+  DM(out=out[:, 0:128].rearrange(S3, p=128), in_=T255[:])
+  TT(out=T186[:, 3, :], in0=T186[:, 0, :], in1=T186[:, 3, :], op=ALU.add)
+  T256 = PP([128, 4, 128], F, tag='l_1', bufs=1)
+  TR(T256[:, 0, :], T146[:, 3, 0:128], T0[:])
+  TR(T256[:, 1, :], T146[:, 3, 128:256], T0[:])
+  TR(T256[:, 2, :], T146[:, 3, 256:384], T0[:])
+  TR(T256[:, 3, :], T146[:, 3, 384:512], T0[:])
+  TT(out=T164[:, 3, :], in0=T164[:, 3, :], in1=T119[:, 2, :], op=ALU.mult)
+  T257 = AQ.tile([128, 4, 128], F, tag='rows_1', bufs=1)
+  SC(T257[:], T256[:])
+  TT(out=T186[:, 3, :], in0=T186[:, 3, :], in1=T119[:, 3, :], op=ALU.mult)
+  T258 = PP([128, 4, 128], F, tag='l_2', bufs=1)
+  TR(T258[:, 0, :], T164[:, 3, 0:128], T0[:])
+  DM(out=out[:, 128:256].rearrange(S3, p=128), in_=T257[:])
+  TR(T258[:, 1, :], T164[:, 3, 128:256], T0[:])
+  TR(T258[:, 2, :], T164[:, 3, 256:384], T0[:])
+  TR(T258[:, 3, :], T164[:, 3, 384:512], T0[:])
+  T260 = PP([128, 4, 128], F, tag='l_0', bufs=1)
+  TR(T260[:, 0, :], T186[:, 3, 0:128], T0[:])
+  TR(T260[:, 1, :], T186[:, 3, 128:256], T0[:])
+  TR(T260[:, 2, :], T186[:, 3, 256:384], T0[:])
+  TR(T260[:, 3, :], T186[:, 3, 384:512], T0[:])
+  T259 = AQ.tile([128, 4, 128], F, tag='rows_0', bufs=1)
+  SC(T259[:], T258[:])
+  DM(out=out[:, 256:384].rearrange(S3, p=128), in_=T259[:])
+  T261 = AQ.tile([128, 4, 128], F, tag='rows_1', bufs=1)
+  SC(T261[:], T260[:])
+  DM(out=out[:, 384:512].rearrange(S3, p=128), in_=T261[:])

from contextlib import ExitStack
import concourse.mybir as mybir
from concourse.masks import make_identity
FLOPS = 7516192768
ACT = mybir.ActivationFunctionType
ALU = mybir.AluOpType
F = mybir.dt.float32
B = mybir.dt.bfloat16
U = mybir.dt.uint32
U8 = mybir.dt.uint8
X = mybir.dt.float8_e4m3fn_x4
E4 = mybir.dt.float8_e4m3fn
S0 = '(g p t) o -> p g (t o)'
S1 = '(p j) c -> p j c'
S2 = 'v (p t) -> p v t'
S3 = '(b p) c -> p b c'
S4 = '(p t) (v h c) -> p t v h c'
S5 = 'v (j p) -> (v j) p'
S6 = 'p (t m) j -> p t m j'
S7 = 'p j (m t) -> p t m j'
S8 = 'p t v c -> p t (v c)'
S9 = 'p c t -> p (c t)'
S10 = 'p n t -> p (n t)'
S11 = 'p (n u) -> p n u'
S12 = 'p u n -> p n u'
S13 = 'p (c i) t -> p c t i'
S14 = 'p t (c i) -> p c t i'
S15 = 'p t n -> p n t'

def tile_tftchannelwisevariableselection_kernel(tc, x, wl_bytes, wl_scale, w1, g1, w2, gs, out):
 nc = tc.nc
 ve = nc.vector
 sc = nc.scalar
 te = nc.tensor
 TR = te.transpose
 def M(o, a, b, k, c, d, x, y):
  te.matmul_mx(out=o, lhsT=a[:, k:k+128].bitcast(X), lhsT_scale=b[:, k:k+128], rhs=c[:].bitcast(X), rhs_scale=d[:], start=x == 1, stop=y == 1)
 def Q(o, s, i):
  ve.quantize_mx(out=o.bitcast(X), scales=s, in_=i)
 with ExitStack() as ctx:
  keep_pool = ctx.enter_context(tc.tile_pool(name='keep_pool', bufs=1))
  AQ = ctx.enter_context(tc.tile_pool(name='AQ', bufs=2))
  psum_pool = ctx.enter_context(tc.psum_pool(name='psum_pool', bufs=1))
  ctx.enter_context(tc.manual_schedule())
  KP = keep_pool.tile
  PP = psum_pool.tile
  ST = ve.scalar_tensor_tensor
  TT = ve.tensor_tensor
  DM = nc.sync.dma_start
  MT = te.matmul
  def AC(o, i, f, scale=1.0):
   sc.activation(out=o, in_=i, func=f, scale=scale)
  def SC(o, i):
   sc.copy(out=o, in_=i)
  T0 = KP([128, 128], F, tag='ident_f', bufs=1)
  make_identity(nc, T0[:])
  T1 = KP([128, 1], F, tag='warm', bufs=1)
  ve.memset(T1[:], 0.0)
  T2 = KP([128, 4, 4], F, tag='wl_s', bufs=1)
  nc.gpsimd.dma_start(out=T2[:], in_=wl_scale.rearrange(S0, p=128, t=4))
  T43 = AQ.tile([128, 4, 512], B, tag='w1_raw_0', bufs=1)
  DM(out=T43[:], in_=w1[0].rearrange(S1, j=4))
  T4 = KP([128, 4, 4], B, tag='g1_b', bufs=1)
  nc.gpsimd.dma_start(out=T4[:], in_=g1.rearrange(S2, t=4))
  T7 = KP([128, 4, 512], B, tag='x_raw0', bufs=1)
  DM(out=T7[:], in_=x[:, 0, :].rearrange(S3, p=128))
  T44 = AQ.tile([128, 4, 4, 256], U8, tag='wl_raw_0', bufs=1)
  DM(out=T44[:, 0, :, :], in_=wl_bytes[0:512, :].rearrange(S4, t=4, v=4, h=2)[:, 0, :, 0, :])
  AC(T1[:], T1[:], ACT.Exp)
  DM(out=T44[:, 1, :, :], in_=wl_bytes[0:512, :].rearrange(S4, t=4, v=4, h=2)[:, 1, :, 0, :])
  DM(out=T44[:, 2, :, :], in_=wl_bytes[0:512, :].rearrange(S4, t=4, v=4, h=2)[:, 2, :, 0, :])
  DM(out=T44[:, 3, :, :], in_=wl_bytes[0:512, :].rearrange(S4, t=4, v=4, h=2)[:, 3, :, 0, :])
  T45 = AQ.tile([128, 4, 512], B, tag='w1_raw_1', bufs=1)
  DM(out=T45[:], in_=w1[1].rearrange(S1, j=4))
  T3 = KP([128, 128], B, tag='ident_b', bufs=1)
  make_identity(nc, T3[:])
  T16 = KP([128, 4, 512], B, tag='x_raw1', bufs=1)
  DM(out=T16[:], in_=x[:, 1, :].rearrange(S3, p=128))
  T46 = AQ.tile([128, 4, 4, 256], U8, tag='wl_raw_1', bufs=1)
  DM(out=T46[:, 0, :, :], in_=wl_bytes[512:1024, :].rearrange(S4, t=4, v=4, h=2)[:, 0, :, 0, :])
  DM(out=T46[:, 1, :, :], in_=wl_bytes[512:1024, :].rearrange(S4, t=4, v=4, h=2)[:, 1, :, 0, :])
  DM(out=T46[:, 2, :, :], in_=wl_bytes[512:1024, :].rearrange(S4, t=4, v=4, h=2)[:, 2, :, 0, :])
  DM(out=T46[:, 3, :, :], in_=wl_bytes[512:1024, :].rearrange(S4, t=4, v=4, h=2)[:, 3, :, 0, :])
  T25 = KP([128, 4, 512], B, tag='x_raw2', bufs=1)
  DM(out=T25[:], in_=x[:, 2, :].rearrange(S3, p=128))
  T34 = KP([128, 4, 512], B, tag='x_raw3', bufs=1)
  DM(out=T34[:], in_=x[:, 3, :].rearrange(S3, p=128))
  T5 = KP([128, 128], B, tag='gs_rows', bufs=1)
  nc.gpsimd.memset(T5[:], 0.0)
  nc.gpsimd.dma_start(out=T5[0:16, :], in_=gs.rearrange(S5, p=128))
  T49 = AQ.tile([128, 512, 4], B, tag='w1g', bufs=1, align_bytes=64)
  ve.tensor_copy(out=T49[:].rearrange(S6, t=4), in_=T43[:].rearrange(S7, t=4))
  T6 = KP([128, 4, 4], F, tag='g1_f', bufs=1)
  nc.gpsimd.tensor_copy(out=T6[:], in_=T4[:])
  T51 = PP([128, 2, 256], F, tag='l_0', bufs=1)
  TR(T51[:, 0, 0:128], T7[:].bitcast(F)[:, 0, 0::2], T0[:])
  TR(T51[:, 0, 128:256], T7[:].bitcast(F)[:, 1, 0::2], T0[:])
  TR(T51[:, 1, 0:128], T7[:].bitcast(F)[:, 0, 1::2], T0[:])
  T53 = AQ.tile([128, 4, 512], B, tag='wl_wide_0', bufs=1)
  AC(T53[:, 0, :], T44[:].rearrange(S8)[:, 0, 0:512].bitcast(E4), ACT.Copy, scale=T2[:, 0, 0:1])
  T47 = AQ.tile([128, 512], U, tag='w1q_codes_0', bufs=1, align_bytes=64)
  T48 = AQ.tile([128, 512], U8, tag='w1q_scales_0', bufs=1, align_bytes=64)
  Q(T47[:, 0:512], T48[:, 0:512], T49[:].rearrange(S9))
  T59 = AQ.tile([128, 4, 512], B, tag='w1_raw_0', bufs=1)
  DM(out=T59[:], in_=w1[2].rearrange(S1, j=4))
  TR(T51[:, 1, 128:256], T7[:].bitcast(F)[:, 1, 1::2], T0[:])
  T60 = AQ.tile([128, 4, 4, 256], U8, tag='wl_raw_2', bufs=1)
  DM(out=T60[:, 0, :, :], in_=wl_bytes[1024:1536, :].rearrange(S4, t=4, v=4, h=2)[:, 0, :, 0, :])
  T52 = PP([128, 2, 256], F, tag='l_1', bufs=1)
  TR(T52[:, 0, 0:128], T7[:].bitcast(F)[:, 2, 0::2], T0[:])
  DM(out=T60[:, 1, :, :], in_=wl_bytes[1024:1536, :].rearrange(S4, t=4, v=4, h=2)[:, 1, :, 0, :])
  DM(out=T60[:, 2, :, :], in_=wl_bytes[1024:1536, :].rearrange(S4, t=4, v=4, h=2)[:, 2, :, 0, :])
  TR(T52[:, 0, 128:256], T7[:].bitcast(F)[:, 3, 0::2], T0[:])
  DM(out=T60[:, 3, :, :], in_=wl_bytes[1024:1536, :].rearrange(S4, t=4, v=4, h=2)[:, 3, :, 0, :])
  TR(T52[:, 1, 0:128], T7[:].bitcast(F)[:, 2, 1::2], T0[:])
  T50 = AQ.tile([128, 512, 4], B, tag='xg', bufs=1, align_bytes=64)
  SC(T50[:].rearrange(S10).bitcast(F).rearrange(S11, u=2)[:, 0:256, :], T51[:].rearrange(S12))
  TR(T52[:, 1, 128:256], T7[:].bitcast(F)[:, 3, 1::2], T0[:])
  SC(T50[:].rearrange(S10).bitcast(F).rearrange(S11, u=2)[:, 256:512, :], T52[:].rearrange(S12))
  AC(T53[:, 1, :], T44[:].rearrange(S8)[:, 1, 0:512].bitcast(E4), ACT.Copy, scale=T2[:, 0, 1:2])
  T8 = KP([128, 512], U, tag='xq0_codes', bufs=1, align_bytes=64)
  T9 = KP([128, 512], U8, tag='xq0_scales', bufs=1, align_bytes=64)
  Q(T8[:, 0:512], T9[:, 0:512], T50[:].rearrange(S9))
  AC(T53[:, 2, :], T44[:].rearrange(S8)[:, 2, 0:512].bitcast(E4), ACT.Copy, scale=T2[:, 0, 2:3])
  T63 = AQ.tile([128, 512, 4], B, tag='w1g', bufs=1, align_bytes=64)
  ve.tensor_copy(out=T63[:].rearrange(S6, t=4), in_=T45[:].rearrange(S7, t=4))
  T55 = PP([128, 512], F, tag='h_0', bufs=1)
  M(T55[:], T47, T48, 0, T8, T9, 1, 1)
  AC(T53[:, 3, :], T44[:].rearrange(S8)[:, 3, 0:512].bitcast(E4), ACT.Copy, scale=T2[:, 0, 3:4])
  T56 = PP([128, 512], F, tag='h_1', bufs=1)
  M(T56[:], T47, T48, 128, T8, T9, 1, 1)
  T57 = PP([128, 512], F, tag='h_2', bufs=1)
  M(T57[:], T47, T48, 256, T8, T9, 1, 1)
  T54 = AQ.tile([128, 4, 512], F, tag='f8_0', bufs=1)
  AC(T54[:, 0, :], T55[:], ACT.Exp)
  T58 = PP([128, 512], F, tag='h_3', bufs=1)
  M(T58[:], T47, T48, 384, T8, T9, 1, 1)
  T67 = AQ.tile([128, 512, 4], B, tag='grouped_0', bufs=1, align_bytes=64)
  ve.tensor_copy(out=T67[:].rearrange(S13, i=4), in_=T53[:].rearrange(S14, i=4))
  T65 = PP([128, 2, 256], F, tag='l_2', bufs=1)
  TR(T65[:, 0, 0:128], T16[:].bitcast(F)[:, 0, 0::2], T0[:])
  T77 = AQ.tile([128, 4, 512], B, tag='w1_raw_1', bufs=1)
  DM(out=T77[:], in_=w1[3].rearrange(S1, j=4))
  AC(T54[:, 1, :], T56[:], ACT.Exp)
  TR(T65[:, 0, 128:256], T16[:].bitcast(F)[:, 1, 0::2], T0[:])
  TR(T65[:, 1, 0:128], T16[:].bitcast(F)[:, 0, 1::2], T0[:])
  TR(T65[:, 1, 128:256], T16[:].bitcast(F)[:, 1, 1::2], T0[:])
  T66 = PP([128, 2, 256], F, tag='l_0', bufs=1)
  TR(T66[:, 0, 0:128], T16[:].bitcast(F)[:, 2, 0::2], T0[:])
  AC(T54[:, 2, :], T57[:], ACT.Exp)
  TR(T66[:, 0, 128:256], T16[:].bitcast(F)[:, 3, 0::2], T0[:])
  TR(T66[:, 1, 0:128], T16[:].bitcast(F)[:, 2, 1::2], T0[:])
  TR(T66[:, 1, 128:256], T16[:].bitcast(F)[:, 3, 1::2], T0[:])
  AC(T54[:, 3, :], T58[:], ACT.Exp)
  T61 = AQ.tile([128, 512], U, tag='w1q_codes_1', bufs=1, align_bytes=64)
  T62 = AQ.tile([128, 512], U8, tag='w1q_scales_1', bufs=1, align_bytes=64)
  Q(T61[:, 0:512], T62[:, 0:512], T63[:].rearrange(S9))
  T83 = PP([128, 2, 256], F, tag='l_1', bufs=1)
  TR(T83[:, 0, 0:128], T25[:].bitcast(F)[:, 0, 0::2], T0[:])
  TR(T83[:, 0, 128:256], T25[:].bitcast(F)[:, 1, 0::2], T0[:])
  T64 = AQ.tile([128, 512, 4], B, tag='xg', bufs=1, align_bytes=64)
  SC(T64[:].rearrange(S10).bitcast(F).rearrange(S11, u=2)[:, 0:256, :], T65[:].rearrange(S12))
  T12 = KP([128, 2048], U, tag='wlq0_codes', bufs=1, align_bytes=64)
  T13 = KP([128, 2048], U8, tag='wlq0_scales', bufs=1, align_bytes=64)
  Q(T12[:, 0:512], T13[:, 0:512], T67[:].rearrange(S9))
  TR(T83[:, 1, 0:128], T25[:].bitcast(F)[:, 0, 1::2], T0[:])
  TR(T83[:, 1, 128:256], T25[:].bitcast(F)[:, 1, 1::2], T0[:])
  SC(T64[:].rearrange(S10).bitcast(F).rearrange(S11, u=2)[:, 256:512, :], T66[:].rearrange(S12))
  ve.tensor_scalar(out=T54[:], in0=T54[:], scalar1=1.0, scalar2=None, op0=ALU.min)
  T84 = PP([128, 2, 256], F, tag='l_2', bufs=1)
  TR(T84[:, 0, 0:128], T25[:].bitcast(F)[:, 2, 0::2], T0[:])
  TR(T84[:, 0, 128:256], T25[:].bitcast(F)[:, 3, 0::2], T0[:])
  TR(T84[:, 1, 0:128], T25[:].bitcast(F)[:, 2, 1::2], T0[:])
  TR(T84[:, 1, 128:256], T25[:].bitcast(F)[:, 3, 1::2], T0[:])
  T68 = AQ.tile([128, 4, 512], B, tag='wl_wide_1', bufs=1)
  AC(T68[:, 0, :], T44[:].rearrange(S8)[:, 0, 512:1024].bitcast(E4), ACT.Copy, scale=T2[:, 0, 0:1])
  T117 = PP([128, 128], B, tag='x', bufs=1)
  TR(T117[:], T5[:], T3[:])
  T100 = PP([128, 2, 256], F, tag='l_0', bufs=1)
  TR(T100[:, 0, 0:128], T34[:].bitcast(F)[:, 0, 0::2], T0[:])
  TR(T100[:, 0, 128:256], T34[:].bitcast(F)[:, 1, 0::2], T0[:])
  AC(T68[:, 1, :], T44[:].rearrange(S8)[:, 1, 512:1024].bitcast(E4), ACT.Copy, scale=T2[:, 0, 1:2])
  T17 = KP([128, 512], U, tag='xq1_codes', bufs=1, align_bytes=64)
  T18 = KP([128, 512], U8, tag='xq1_scales', bufs=1, align_bytes=64)
  Q(T17[:, 0:512], T18[:, 0:512], T64[:].rearrange(S9))
  TR(T100[:, 1, 0:128], T34[:].bitcast(F)[:, 0, 1::2], T0[:])
  TR(T100[:, 1, 128:256], T34[:].bitcast(F)[:, 1, 1::2], T0[:])
  AC(T68[:, 2, :], T44[:].rearrange(S8)[:, 2, 512:1024].bitcast(E4), ACT.Copy, scale=T2[:, 0, 2:3])
  ST(out=T54[:, 0, :], in0=T55[:], scalar=1.0, in1=T54[:, 0, :], op0=ALU.add, op1=ALU.max)
  AC(T68[:, 3, :], T44[:].rearrange(S8)[:, 3, 512:1024].bitcast(E4), ACT.Copy, scale=T2[:, 0, 3:4])
  ST(out=T54[:, 1, :], in0=T56[:], scalar=1.0, in1=T54[:, 1, :], op0=ALU.add, op1=ALU.max)
  T72 = PP([128, 512], F, tag='h_0', bufs=1)
  M(T72[:], T61, T62, 0, T17, T18, 1, 1)
  T76 = AQ.tile([128, 4, 512], B, tag='wl_wide_0', bufs=1)
  AC(T76[:, 0, :], T46[:].rearrange(S8)[:, 0, 0:512].bitcast(E4), ACT.Copy, scale=T2[:, 1, 0:1])
  ST(out=T54[:, 2, :], in0=T57[:], scalar=1.0, in1=T54[:, 2, :], op0=ALU.add, op1=ALU.max)
  T78 = AQ.tile([128, 4, 4, 256], U8, tag='wl_raw_0', bufs=1)
  DM(out=T78[:, 0, :, :], in_=wl_bytes[1536:2048, :].rearrange(S4, t=4, v=4, h=2)[:, 0, :, 0, :])
  DM(out=T78[:, 1, :, :], in_=wl_bytes[1536:2048, :].rearrange(S4, t=4, v=4, h=2)[:, 1, :, 0, :])
  DM(out=T78[:, 2, :, :], in_=wl_bytes[1536:2048, :].rearrange(S4, t=4, v=4, h=2)[:, 2, :, 0, :])
  T73 = PP([128, 512], F, tag='h_1', bufs=1)
  M(T73[:], T61, T62, 128, T17, T18, 1, 1)
  DM(out=T78[:, 3, :, :], in_=wl_bytes[1536:2048, :].rearrange(S4, t=4, v=4, h=2)[:, 3, :, 0, :])
  T71 = AQ.tile([128, 4, 512], F, tag='f8_1', bufs=1)
  AC(T71[:, 0, :], T72[:], ACT.Exp)
  ST(out=T54[:, 3, :], in0=T58[:], scalar=1.0, in1=T54[:, 3, :], op0=ALU.add, op1=ALU.max)
  T74 = PP([128, 512], F, tag='h_2', bufs=1)
  M(T74[:], T61, T62, 256, T17, T18, 1, 1)
  AC(T71[:, 1, :], T73[:], ACT.Exp)
  T69 = AQ.tile([128, 512, 4], B, tag='grouped_1', bufs=1, align_bytes=64)
  ve.tensor_copy(out=T69[:].rearrange(S13, i=4), in_=T68[:].rearrange(S14, i=4))
  T75 = PP([128, 512], F, tag='h_3', bufs=1)
  M(T75[:], T61, T62, 384, T17, T18, 1, 1)
  AC(T71[:, 2, :], T74[:], ACT.Exp)
  AC(T71[:, 3, :], T75[:], ACT.Exp)
  T70 = AQ.tile([128, 512, 4], B, tag='eg', bufs=1, align_bytes=64)
  ST(out=T70[:], in0=T54[:].rearrange(S15), scalar=-1.0, in1=T6[:, 0:1, :].broadcast_to([128, 512, 4]), op0=ALU.add, op1=ALU.mult)
  AC(T76[:, 1, :], T46[:].rearrange(S8)[:, 1, 0:512].bitcast(E4), ACT.Copy, scale=T2[:, 1, 1:2])
  AC(T76[:, 2, :], T46[:].rearrange(S8)[:, 2, 0:512].bitcast(E4), ACT.Copy, scale=T2[:, 1, 2:3])
  AC(T76[:, 3, :], T46[:].rearrange(S8)[:, 3, 0:512].bitcast(E4), ACT.Copy, scale=T2[:, 1, 3:4])
  T82 = AQ.tile([128, 512, 4], B, tag='xg', bufs=1, align_bytes=64)
  SC(T82[:].rearrange(S10).bitcast(F).rearrange(S11, u=2)[:, 0:256, :], T83[:].rearrange(S12))
  Q(T12[:, 512:1024], T13[:, 512:1024], T69[:].rearrange(S9))
  SC(T82[:].rearrange(S10).bitcast(F).rearrange(S11, u=2)[:, 256:512, :], T84[:].rearrange(S12))
  T101 = PP([128, 2, 256], F, tag='l_1', bufs=1)
  TR(T101[:, 0, 0:128], T34[:].bitcast(F)[:, 2, 0::2], T0[:])
  TR(T101[:, 0, 128:256], T34[:].bitcast(F)[:, 3, 0::2], T0[:])
  T10 = KP([128, 512], U, tag='eq0_codes', bufs=1, align_bytes=64)
  T11 = KP([128, 512], U8, tag='eq0_scales', bufs=1, align_bytes=64)
  Q(T10[:, 0:512], T11[:, 0:512], T70[:].rearrange(S9))
  TR(T101[:, 1, 0:128], T34[:].bitcast(F)[:, 2, 1::2], T0[:])
  TR(T101[:, 1, 128:256], T34[:].bitcast(F)[:, 3, 1::2], T0[:])
  T85 = AQ.tile([128, 512, 4], B, tag='grouped_2', bufs=1, align_bytes=64)
  SC(T85[:].rearrange(S13, i=4), T76[:].rearrange(S14, i=4))
  T128 = PP([128, 512], F, tag='l_2', bufs=1)
  M(T128[:], T12, T13, 0, T8, T9, 1, 0)
  T81 = AQ.tile([128, 512, 4], B, tag='w1g', bufs=1, align_bytes=64)
  ve.tensor_copy(out=T81[:].rearrange(S6, t=4), in_=T59[:].rearrange(S7, t=4))
  ve.tensor_scalar(out=T71[:], in0=T71[:], scalar1=1.0, scalar2=None, op0=ALU.min)
  T86 = AQ.tile([128, 4, 512], B, tag='wl_wide_1', bufs=1)
  AC(T86[:, 0, :], T46[:].rearrange(S8)[:, 0, 512:1024].bitcast(E4), ACT.Copy, scale=T2[:, 1, 0:1])
  T79 = AQ.tile([128, 512], U, tag='w1q_codes_0', bufs=1, align_bytes=64)
  T80 = AQ.tile([128, 512], U8, tag='w1q_scales_0', bufs=1, align_bytes=64)
  Q(T79[:, 0:512], T80[:, 0:512], T81[:].rearrange(S9))
  AC(T86[:, 1, :], T46[:].rearrange(S8)[:, 1, 512:1024].bitcast(E4), ACT.Copy, scale=T2[:, 1, 1:2])
  ST(out=T71[:, 0, :], in0=T72[:], scalar=1.0, in1=T71[:, 0, :], op0=ALU.add, op1=ALU.max)
  AC(T86[:, 2, :], T46[:].rearrange(S8)[:, 2, 512:1024].bitcast(E4), ACT.Copy, scale=T2[:, 1, 2:3])
  ST(out=T71[:, 1, :], in0=T73[:], scalar=1.0, in1=T71[:, 1, :], op0=ALU.add, op1=ALU.max)
  AC(T86[:, 3, :], T46[:].rearrange(S8)[:, 3, 512:1024].bitcast(E4), ACT.Copy, scale=T2[:, 1, 3:4])
  ST(out=T71[:, 2, :], in0=T74[:], scalar=1.0, in1=T71[:, 2, :], op0=ALU.add, op1=ALU.max)
  T94 = AQ.tile([128, 4, 512], B, tag='wl_wide_0', bufs=1)
  AC(T94[:, 0, :], T60[:].rearrange(S8)[:, 0, 0:512].bitcast(E4), ACT.Copy, scale=T2[:, 2, 0:1])
  T95 = AQ.tile([128, 4, 4, 256], U8, tag='wl_raw_1', bufs=1)
  DM(out=T95[:, 0, :, :], in_=wl_bytes[0:512, :].rearrange(S4, t=4, v=4, h=2)[:, 0, :, 1, :])
  DM(out=T95[:, 1, :, :], in_=wl_bytes[0:512, :].rearrange(S4, t=4, v=4, h=2)[:, 1, :, 1, :])
  DM(out=T95[:, 2, :, :], in_=wl_bytes[0:512, :].rearrange(S4, t=4, v=4, h=2)[:, 2, :, 1, :])
  ST(out=T71[:, 3, :], in0=T75[:], scalar=1.0, in1=T71[:, 3, :], op0=ALU.add, op1=ALU.max)
  DM(out=T95[:, 3, :, :], in_=wl_bytes[0:512, :].rearrange(S4, t=4, v=4, h=2)[:, 3, :, 1, :])
  AC(T94[:, 1, :], T60[:].rearrange(S8)[:, 1, 0:512].bitcast(E4), ACT.Copy, scale=T2[:, 2, 1:2])
  T26 = KP([128, 512], U, tag='xq2_codes', bufs=1, align_bytes=64)
  T27 = KP([128, 512], U8, tag='xq2_scales', bufs=1, align_bytes=64)
  Q(T26[:, 0:512], T27[:, 0:512], T82[:].rearrange(S9))
  AC(T94[:, 2, :], T60[:].rearrange(S8)[:, 2, 0:512].bitcast(E4), ACT.Copy, scale=T2[:, 2, 2:3])
  T87 = AQ.tile([128, 512, 4], B, tag='grouped_0', bufs=1, align_bytes=64)
  ve.tensor_copy(out=T87[:].rearrange(S13, i=4), in_=T86[:].rearrange(S14, i=4))
  T90 = PP([128, 512], F, tag='h_0', bufs=1)
  M(T90[:], T79, T80, 0, T26, T27, 1, 1)
  AC(T94[:, 3, :], T60[:].rearrange(S8)[:, 3, 0:512].bitcast(E4), ACT.Copy, scale=T2[:, 2, 3:4])
  T91 = PP([128, 512], F, tag='h_1', bufs=1)
  M(T91[:], T79, T80, 128, T26, T27, 1, 1)
  T89 = AQ.tile([128, 4, 512], F, tag='f8_2', bufs=1)
  AC(T89[:, 0, :], T90[:], ACT.Exp)
  T92 = PP([128, 512], F, tag='h_2', bufs=1)
  M(T92[:], T79, T80, 256, T26, T27, 1, 1)
  T93 = PP([128, 512], F, tag='h_3', bufs=1)
  M(T93[:], T79, T80, 384, T26, T27, 1, 1)
  T88 = AQ.tile([128, 512, 4], B, tag='eg', bufs=1, align_bytes=64)
  ST(out=T88[:], in0=T71[:].rearrange(S15), scalar=-1.0, in1=T6[:, 1:2, :].broadcast_to([128, 512, 4]), op0=ALU.add, op1=ALU.mult)
  AC(T89[:, 1, :], T91[:], ACT.Exp)
  AC(T89[:, 2, :], T92[:], ACT.Exp)
  AC(T89[:, 3, :], T93[:], ACT.Exp)
  T99 = AQ.tile([128, 512, 4], B, tag='xg', bufs=1, align_bytes=64)
  SC(T99[:].rearrange(S10).bitcast(F).rearrange(S11, u=2)[:, 0:256, :], T100[:].rearrange(S12))
  T21 = KP([128, 2048], U, tag='wlq1_codes', bufs=1, align_bytes=64)
  T22 = KP([128, 2048], U8, tag='wlq1_scales', bufs=1, align_bytes=64)
  Q(T21[:, 0:512], T22[:, 0:512], T85[:].rearrange(S9))
  SC(T99[:].rearrange(S10).bitcast(F).rearrange(S11, u=2)[:, 256:512, :], T101[:].rearrange(S12))
  T129 = PP([128, 512], F, tag='l_0', bufs=1)
  M(T129[:], T12, T13, 256, T8, T9, 1, 0)
  T19 = KP([128, 512], U, tag='eq1_codes', bufs=1, align_bytes=64)
  T20 = KP([128, 512], U8, tag='eq1_scales', bufs=1, align_bytes=64)
  Q(T19[:, 0:512], T20[:, 0:512], T88[:].rearrange(S9))
  T102 = AQ.tile([128, 512, 4], B, tag='grouped_1', bufs=1, align_bytes=64)
  SC(T102[:].rearrange(S13, i=4), T94[:].rearrange(S14, i=4))
  T130 = PP([128, 512], F, tag='l_1', bufs=1)
  M(T130[:], T12, T13, 512, T8, T9, 1, 0)
  M(T128[:], T21, T22, 0, T17, T18, 0, 0)
  Q(T21[:, 512:1024], T22[:, 512:1024], T87[:].rearrange(S9))
  M(T129[:], T21, T22, 256, T17, T18, 0, 0)
  T98 = AQ.tile([128, 512, 4], B, tag='w1g', bufs=1, align_bytes=64)
  ve.tensor_copy(out=T98[:].rearrange(S6, t=4), in_=T77[:].rearrange(S7, t=4))
  M(T130[:], T21, T22, 512, T17, T18, 0, 0)
  ve.tensor_scalar(out=T89[:], in0=T89[:], scalar1=1.0, scalar2=None, op0=ALU.min)
  T103 = AQ.tile([128, 4, 512], B, tag='wl_wide_1', bufs=1)
  AC(T103[:, 0, :], T60[:].rearrange(S8)[:, 0, 512:1024].bitcast(E4), ACT.Copy, scale=T2[:, 2, 0:1])
  AC(T103[:, 1, :], T60[:].rearrange(S8)[:, 1, 512:1024].bitcast(E4), ACT.Copy, scale=T2[:, 2, 1:2])
  T96 = AQ.tile([128, 512], U, tag='w1q_codes_1', bufs=1, align_bytes=64)
  T97 = AQ.tile([128, 512], U8, tag='w1q_scales_1', bufs=1, align_bytes=64)
  Q(T96[:, 0:512], T97[:, 0:512], T98[:].rearrange(S9))
  AC(T103[:, 2, :], T60[:].rearrange(S8)[:, 2, 512:1024].bitcast(E4), ACT.Copy, scale=T2[:, 2, 2:3])
  ST(out=T89[:, 0, :], in0=T90[:], scalar=1.0, in1=T89[:, 0, :], op0=ALU.add, op1=ALU.max)
  AC(T103[:, 3, :], T60[:].rearrange(S8)[:, 3, 512:1024].bitcast(E4), ACT.Copy, scale=T2[:, 2, 3:4])
  ST(out=T89[:, 1, :], in0=T91[:], scalar=1.0, in1=T89[:, 1, :], op0=ALU.add, op1=ALU.max)
  T111 = AQ.tile([128, 4, 512], B, tag='wl_wide_0', bufs=1)
  AC(T111[:, 0, :], T78[:].rearrange(S8)[:, 0, 0:512].bitcast(E4), ACT.Copy, scale=T2[:, 3, 0:1])
  T112 = AQ.tile([128, 4, 4, 256], U8, tag='wl_raw_2', bufs=1)
  DM(out=T112[:, 0, :, :], in_=wl_bytes[512:1024, :].rearrange(S4, t=4, v=4, h=2)[:, 0, :, 1, :])
  DM(out=T112[:, 1, :, :], in_=wl_bytes[512:1024, :].rearrange(S4, t=4, v=4, h=2)[:, 1, :, 1, :])
  DM(out=T112[:, 2, :, :], in_=wl_bytes[512:1024, :].rearrange(S4, t=4, v=4, h=2)[:, 2, :, 1, :])
  DM(out=T112[:, 3, :, :], in_=wl_bytes[512:1024, :].rearrange(S4, t=4, v=4, h=2)[:, 3, :, 1, :])
  ST(out=T89[:, 2, :], in0=T92[:], scalar=1.0, in1=T89[:, 2, :], op0=ALU.add, op1=ALU.max)
  AC(T111[:, 1, :], T78[:].rearrange(S8)[:, 1, 0:512].bitcast(E4), ACT.Copy, scale=T2[:, 3, 1:2])
  ST(out=T89[:, 3, :], in0=T93[:], scalar=1.0, in1=T89[:, 3, :], op0=ALU.add, op1=ALU.max)
  AC(T111[:, 2, :], T78[:].rearrange(S8)[:, 2, 0:512].bitcast(E4), ACT.Copy, scale=T2[:, 3, 2:3])
  T35 = KP([128, 512], U, tag='xq3_codes', bufs=1, align_bytes=64)
  T36 = KP([128, 512], U8, tag='xq3_scales', bufs=1, align_bytes=64)
  Q(T35[:, 0:512], T36[:, 0:512], T99[:].rearrange(S9))
  AC(T111[:, 3, :], T78[:].rearrange(S8)[:, 3, 0:512].bitcast(E4), ACT.Copy, scale=T2[:, 3, 3:4])
  T104 = AQ.tile([128, 512, 4], B, tag='grouped_2', bufs=1, align_bytes=64)
  ve.tensor_copy(out=T104[:].rearrange(S13, i=4), in_=T103[:].rearrange(S14, i=4))
  T113 = AQ.tile([128, 512, 4], B, tag='grouped_0', bufs=1, align_bytes=64)
  SC(T113[:].rearrange(S13, i=4), T111[:].rearrange(S14, i=4))
  T107 = PP([128, 512], F, tag='h_0', bufs=1)
  M(T107[:], T96, T97, 0, T35, T36, 1, 1)
  T108 = PP([128, 512], F, tag='h_1', bufs=1)
  M(T108[:], T96, T97, 128, T35, T36, 1, 1)
  T109 = PP([128, 512], F, tag='h_2', bufs=1)
  M(T109[:], T96, T97, 256, T35, T36, 1, 1)
  T110 = PP([128, 512], F, tag='h_3', bufs=1)
  M(T110[:], T96, T97, 384, T35, T36, 1, 1)
  T105 = AQ.tile([128, 512, 4], B, tag='eg', bufs=1, align_bytes=64)
  ST(out=T105[:], in0=T89[:].rearrange(S15), scalar=-1.0, in1=T6[:, 2:3, :].broadcast_to([128, 512, 4]), op0=ALU.add, op1=ALU.mult)
  T106 = AQ.tile([128, 4, 512], F, tag='f8_3', bufs=1)
  AC(T106[:, 0, :], T107[:], ACT.Exp)
  AC(T106[:, 1, :], T108[:], ACT.Exp)
  T30 = KP([128, 2048], U, tag='wlq2_codes', bufs=1, align_bytes=64)
  T31 = KP([128, 2048], U8, tag='wlq2_scales', bufs=1, align_bytes=64)
  Q(T30[:, 0:512], T31[:, 0:512], T102[:].rearrange(S9))
  AC(T106[:, 2, :], T109[:], ACT.Exp)
  T28 = KP([128, 512], U, tag='eq2_codes', bufs=1, align_bytes=64)
  T29 = KP([128, 512], U8, tag='eq2_scales', bufs=1, align_bytes=64)
  Q(T28[:, 0:512], T29[:, 0:512], T105[:].rearrange(S9))
  M(T128[:], T30, T31, 0, T26, T27, 0, 0)
  AC(T106[:, 3, :], T110[:], ACT.Exp)
  M(T129[:], T30, T31, 256, T26, T27, 0, 0)
  Q(T30[:, 512:1024], T31[:, 512:1024], T104[:].rearrange(S9))
  T114 = AQ.tile([128, 4, 512], B, tag='wl_wide_1', bufs=1)
  AC(T114[:, 0, :], T78[:].rearrange(S8)[:, 0, 512:1024].bitcast(E4), ACT.Copy, scale=T2[:, 3, 0:1])
  ve.tensor_scalar(out=T106[:], in0=T106[:], scalar1=1.0, scalar2=None, op0=ALU.min)
  M(T130[:], T30, T31, 512, T26, T27, 0, 0)
  AC(T114[:, 1, :], T78[:].rearrange(S8)[:, 1, 512:1024].bitcast(E4), ACT.Copy, scale=T2[:, 3, 1:2])
  AC(T114[:, 2, :], T78[:].rearrange(S8)[:, 2, 512:1024].bitcast(E4), ACT.Copy, scale=T2[:, 3, 2:3])
  T39 = KP([128, 2048], U, tag='wlq3_codes', bufs=1, align_bytes=64)
  T40 = KP([128, 2048], U8, tag='wlq3_scales', bufs=1, align_bytes=64)
  Q(T39[:, 0:512], T40[:, 0:512], T113[:].rearrange(S9))
  AC(T114[:, 3, :], T78[:].rearrange(S8)[:, 3, 512:1024].bitcast(E4), ACT.Copy, scale=T2[:, 3, 3:4])
  ST(out=T106[:, 0, :], in0=T107[:], scalar=1.0, in1=T106[:, 0, :], op0=ALU.add, op1=ALU.max)
  M(T128[:], T39, T40, 0, T35, T36, 0, 1)
  T126 = AQ.tile([128, 4, 512], B, tag='wl_wide_0', bufs=1)
  AC(T126[:, 0, :], T95[:].rearrange(S8)[:, 0, 0:512].bitcast(E4), ACT.Copy, scale=T2[:, 0, 0:1])
  T120 = AQ.tile([128, 4, 4, 256], U8, tag='wl_raw_0', bufs=1)
  DM(out=T120[:, 0, :, :], in_=wl_bytes[1024:1536, :].rearrange(S4, t=4, v=4, h=2)[:, 0, :, 1, :])
  DM(out=T120[:, 1, :, :], in_=wl_bytes[1024:1536, :].rearrange(S4, t=4, v=4, h=2)[:, 1, :, 1, :])
  DM(out=T120[:, 2, :, :], in_=wl_bytes[1024:1536, :].rearrange(S4, t=4, v=4, h=2)[:, 2, :, 1, :])
  M(T129[:], T39, T40, 256, T35, T36, 0, 1)
  DM(out=T120[:, 3, :, :], in_=wl_bytes[1024:1536, :].rearrange(S4, t=4, v=4, h=2)[:, 3, :, 1, :])
  ST(out=T106[:, 1, :], in0=T108[:], scalar=1.0, in1=T106[:, 1, :], op0=ALU.add, op1=ALU.max)
  T115 = AQ.tile([128, 512, 4], B, tag='grouped_1', bufs=1, align_bytes=64)
  SC(T115[:].rearrange(S13, i=4), T114[:].rearrange(S14, i=4))
  ST(out=T106[:, 2, :], in0=T109[:], scalar=1.0, in1=T106[:, 2, :], op0=ALU.add, op1=ALU.max)
  ST(out=T106[:, 3, :], in0=T110[:], scalar=1.0, in1=T106[:, 3, :], op0=ALU.add, op1=ALU.max)
  T118 = KP([128, 16], F, tag='gs2', bufs=1)
  ve.tensor_scalar(out=T118[:], in0=T117[:, 0:16], scalar1=2.0, scalar2=None, op0=ALU.mult)
  T116 = AQ.tile([128, 512, 4], B, tag='eg', bufs=1, align_bytes=64)
  ST(out=T116[:], in0=T106[:].rearrange(S15), scalar=-1.0, in1=T6[:, 3:4, :].broadcast_to([128, 512, 4]), op0=ALU.add, op1=ALU.mult)
  T170 = PP([128, 2, 512], B, tag='x', bufs=1)
  TR(T170[:, 0, 0:128], T7[:, 0, 0:128], T3[:])
  TR(T170[:, 0, 128:256], T7[:, 1, 0:128], T3[:])
  TR(T170[:, 0, 256:384], T7[:, 2, 0:128], T3[:])
  TR(T170[:, 0, 384:512], T7[:, 3, 0:128], T3[:])
  TR(T170[:, 1, 0:128], T7[:, 0, 128:256], T3[:])
  TR(T170[:, 1, 128:256], T7[:, 1, 128:256], T3[:])
  TR(T170[:, 1, 256:384], T7[:, 2, 128:256], T3[:])
  TR(T170[:, 1, 384:512], T7[:, 3, 128:256], T3[:])
  AC(T126[:, 1, :], T95[:].rearrange(S8)[:, 1, 0:512].bitcast(E4), ACT.Copy, scale=T2[:, 0, 1:2])
  AC(T126[:, 2, :], T95[:].rearrange(S8)[:, 2, 0:512].bitcast(E4), ACT.Copy, scale=T2[:, 0, 2:3])
  AC(T126[:, 3, :], T95[:].rearrange(S8)[:, 3, 0:512].bitcast(E4), ACT.Copy, scale=T2[:, 0, 3:4])
  Q(T39[:, 512:1024], T40[:, 512:1024], T115[:].rearrange(S9))
  T127 = AQ.tile([128, 512], F, tag='l0_0', bufs=1)
  SC(T127[:], T128[:])
  T37 = KP([128, 512], U, tag='eq3_codes', bufs=1, align_bytes=64)
  T38 = KP([128, 512], U8, tag='eq3_scales', bufs=1, align_bytes=64)
  Q(T37[:, 0:512], T38[:, 0:512], T116[:].rearrange(S9))
  M(T130[:], T39, T40, 512, T35, T36, 0, 1)
  T132 = AQ.tile([128, 4, 512], B, tag='wl_wide_1', bufs=1)
  AC(T132[:, 0, :], T95[:].rearrange(S8)[:, 0, 512:1024].bitcast(E4), ACT.Copy, scale=T2[:, 0, 0:1])
  T131 = PP([128, 512], F, tag='l_2', bufs=1)
  M(T131[:], T12, T13, 768, T8, T9, 1, 0)
  T133 = AQ.tile([128, 512], F, tag='top_0', bufs=1)
  TT(out=T133[:], in0=T129[:], in1=T127[:], op=ALU.max)
  M(T131[:], T21, T22, 768, T17, T18, 0, 0)
  AC(T132[:, 1, :], T95[:].rearrange(S8)[:, 1, 512:1024].bitcast(E4), ACT.Copy, scale=T2[:, 0, 1:2])
  M(T131[:], T30, T31, 768, T26, T27, 0, 0)
  T134 = AQ.tile([128, 512, 4], B, tag='grouped_2', bufs=1, align_bytes=64)
  ve.tensor_copy(out=T134[:].rearrange(S13, i=4), in_=T126[:].rearrange(S14, i=4))
  M(T131[:], T39, T40, 768, T35, T36, 0, 1)
  AC(T132[:, 2, :], T95[:].rearrange(S8)[:, 2, 512:1024].bitcast(E4), ACT.Copy, scale=T2[:, 0, 2:3])
  AC(T132[:, 3, :], T95[:].rearrange(S8)[:, 3, 512:1024].bitcast(E4), ACT.Copy, scale=T2[:, 0, 3:4])
  TT(out=T133[:], in0=T130[:], in1=T133[:], op=ALU.max)
  T141 = AQ.tile([128, 4, 512], B, tag='wl_wide_0', bufs=1)
  AC(T141[:, 0, :], T112[:].rearrange(S8)[:, 0, 0:512].bitcast(E4), ACT.Copy, scale=T2[:, 1, 0:1])
  T121 = AQ.tile([128, 4, 4, 256], U8, tag='wl_raw_1', bufs=1)
  DM(out=T121[:, 0, :, :], in_=wl_bytes[1536:2048, :].rearrange(S4, t=4, v=4, h=2)[:, 0, :, 1, :])
  DM(out=T121[:, 1, :, :], in_=wl_bytes[1536:2048, :].rearrange(S4, t=4, v=4, h=2)[:, 1, :, 1, :])
  DM(out=T121[:, 2, :, :], in_=wl_bytes[1536:2048, :].rearrange(S4, t=4, v=4, h=2)[:, 2, :, 1, :])
  DM(out=T121[:, 3, :, :], in_=wl_bytes[1536:2048, :].rearrange(S4, t=4, v=4, h=2)[:, 3, :, 1, :])
  T122 = AQ.tile([128, 4, 512], B, tag='w2_raw_0', bufs=1)
  DM(out=T122[:], in_=w2[0, :, 0:512].rearrange(S1, j=4))
  T142 = AQ.tile([128, 512, 4], B, tag='grouped_0', bufs=1, align_bytes=64)
  ve.tensor_copy(out=T142[:].rearrange(S13, i=4), in_=T132[:].rearrange(S14, i=4))
  T123 = AQ.tile([128, 4, 512], B, tag='w2_raw_1', bufs=1)
  DM(out=T123[:], in_=w2[0, :, 512:1024].rearrange(S1, j=4))
  T124 = AQ.tile([128, 4, 512], B, tag='w2_raw_2', bufs=1)
  DM(out=T124[:], in_=w2[1, :, 0:512].rearrange(S1, j=4))
  AC(T141[:, 1, :], T112[:].rearrange(S8)[:, 1, 0:512].bitcast(E4), ACT.Copy, scale=T2[:, 1, 1:2])
  AC(T141[:, 2, :], T112[:].rearrange(S8)[:, 2, 0:512].bitcast(E4), ACT.Copy, scale=T2[:, 1, 2:3])
  AC(T141[:, 3, :], T112[:].rearrange(S8)[:, 3, 0:512].bitcast(E4), ACT.Copy, scale=T2[:, 1, 3:4])
  TT(out=T133[:], in0=T131[:], in1=T133[:], op=ALU.max)
  T143 = AQ.tile([128, 4, 512], B, tag='wl_wide_1', bufs=1)
  AC(T143[:, 0, :], T112[:].rearrange(S8)[:, 0, 512:1024].bitcast(E4), ACT.Copy, scale=T2[:, 1, 0:1])
  Q(T12[:, 1024:1536], T13[:, 1024:1536], T134[:].rearrange(S9))
  AC(T143[:, 1, :], T112[:].rearrange(S8)[:, 1, 512:1024].bitcast(E4), ACT.Copy, scale=T2[:, 1, 1:2])
  T135 = AQ.tile([128, 4, 512], F, tag='f8_0', bufs=1)
  TT(out=T135[:, 1, :], in0=T129[:], in1=T133[:], op=ALU.subtract)
  AC(T143[:, 2, :], T112[:].rearrange(S8)[:, 2, 512:1024].bitcast(E4), ACT.Copy, scale=T2[:, 1, 2:3])
  TT(out=T135[:, 2, :], in0=T130[:], in1=T133[:], op=ALU.subtract)
  T137 = PP([128, 512], F, tag='l_0', bufs=1)
  M(T137[:], T12, T13, 128, T8, T9, 1, 0)
  M(T137[:], T21, T22, 128, T17, T18, 0, 0)
  AC(T143[:, 3, :], T112[:].rearrange(S8)[:, 3, 512:1024].bitcast(E4), ACT.Copy, scale=T2[:, 1, 3:4])
  TT(out=T135[:, 3, :], in0=T131[:], in1=T133[:], op=ALU.subtract)
  M(T137[:], T30, T31, 128, T26, T27, 0, 0)
  M(T137[:], T39, T40, 128, T35, T36, 0, 1)
  TT(out=T135[:, 0, :], in0=T127[:], in1=T133[:], op=ALU.subtract)
  T138 = PP([128, 512], F, tag='l_1', bufs=1)
  M(T138[:], T12, T13, 384, T8, T9, 1, 0)
  T136 = AQ.tile([128, 512], F, tag='l0_1', bufs=1)
  SC(T136[:], T137[:])
  M(T138[:], T21, T22, 384, T17, T18, 0, 0)
  T144 = AQ.tile([128, 512, 4], B, tag='grouped_1', bufs=1, align_bytes=64)
  ve.tensor_copy(out=T144[:].rearrange(S13, i=4), in_=T141[:].rearrange(S14, i=4))
  M(T138[:], T30, T31, 384, T26, T27, 0, 0)
  AC(T135[:], T135[:], ACT.Exp)
  M(T138[:], T39, T40, 384, T35, T36, 0, 1)
  T139 = PP([128, 512], F, tag='l_2', bufs=1)
  M(T139[:], T12, T13, 640, T8, T9, 1, 0)
  M(T139[:], T21, T22, 640, T17, T18, 0, 0)
  M(T139[:], T30, T31, 640, T26, T27, 0, 0)
  T145 = AQ.tile([128, 512], F, tag='top_1', bufs=1)
  TT(out=T145[:], in0=T138[:], in1=T136[:], op=ALU.max)
  M(T139[:], T39, T40, 640, T35, T36, 0, 1)
  T140 = PP([128, 512], F, tag='l_0', bufs=1)
  M(T140[:], T12, T13, 896, T8, T9, 1, 0)
  Q(T12[:, 1536:2048], T13[:, 1536:2048], T142[:].rearrange(S9))
  M(T140[:], T21, T22, 896, T17, T18, 0, 0)
  M(T140[:], T30, T31, 896, T26, T27, 0, 0)
  TT(out=T145[:], in0=T139[:], in1=T145[:], op=ALU.max)
  T147 = AQ.tile([128, 4, 512], B, tag='wl_wide_0', bufs=1)
  AC(T147[:, 0, :], T120[:].rearrange(S8)[:, 0, 0:512].bitcast(E4), ACT.Copy, scale=T2[:, 2, 0:1])
  T119 = KP([128, 4, 512], F, tag='den', bufs=1)
  nc.gpsimd.tensor_tensor(out=T119[:, 0, :], in0=T135[:, 0, :], in1=T135[:, 1, :], op=ALU.add)
  M(T140[:], T39, T40, 896, T35, T36, 0, 1)
  T148 = AQ.tile([128, 512, 4], B, tag='grouped_2', bufs=1, align_bytes=64)
  ve.tensor_copy(out=T148[:].rearrange(S13, i=4), in_=T143[:].rearrange(S14, i=4))
  AC(T147[:, 1, :], T120[:].rearrange(S8)[:, 1, 0:512].bitcast(E4), ACT.Copy, scale=T2[:, 2, 1:2])
  AC(T147[:, 2, :], T120[:].rearrange(S8)[:, 2, 0:512].bitcast(E4), ACT.Copy, scale=T2[:, 2, 2:3])
  nc.gpsimd.tensor_tensor(out=T119[:, 0, :], in0=T119[:, 0, :], in1=T135[:, 2, :], op=ALU.add)
  AC(T147[:, 3, :], T120[:].rearrange(S8)[:, 3, 0:512].bitcast(E4), ACT.Copy, scale=T2[:, 2, 3:4])
  TT(out=T145[:], in0=T140[:], in1=T145[:], op=ALU.max)
  T149 = AQ.tile([128, 4, 512], B, tag='wl_wide_1', bufs=1)
  AC(T149[:, 0, :], T120[:].rearrange(S8)[:, 0, 512:1024].bitcast(E4), ACT.Copy, scale=T2[:, 2, 0:1])
  Q(T21[:, 1024:1536], T22[:, 1024:1536], T144[:].rearrange(S9))
  nc.gpsimd.tensor_tensor(out=T119[:, 0, :], in0=T119[:, 0, :], in1=T135[:, 3, :], op=ALU.add)
  AC(T149[:, 1, :], T120[:].rearrange(S8)[:, 1, 512:1024].bitcast(E4), ACT.Copy, scale=T2[:, 2, 1:2])
  T146 = AQ.tile([128, 4, 512], F, tag='f8_1', bufs=1)
  TT(out=T146[:, 1, :], in0=T138[:], in1=T145[:], op=ALU.subtract)
  AC(T149[:, 2, :], T120[:].rearrange(S8)[:, 2, 512:1024].bitcast(E4), ACT.Copy, scale=T2[:, 2, 2:3])
  TT(out=T146[:, 2, :], in0=T139[:], in1=T145[:], op=ALU.subtract)
  T159 = PP([128, 512], F, tag='l_1', bufs=1)
  M(T159[:], T12, T13, 1024, T8, T9, 1, 0)
  AC(T149[:, 3, :], T120[:].rearrange(S8)[:, 3, 512:1024].bitcast(E4), ACT.Copy, scale=T2[:, 2, 3:4])
  M(T159[:], T21, T22, 1024, T17, T18, 0, 0)
  TT(out=T146[:, 3, :], in0=T140[:], in1=T145[:], op=ALU.subtract)
  T160 = PP([128, 512], F, tag='l_2', bufs=1)
  M(T160[:], T12, T13, 1280, T8, T9, 1, 0)
  T150 = AQ.tile([128, 512, 4], B, tag='grouped_0', bufs=1, align_bytes=64)
  SC(T150[:].rearrange(S13, i=4), T147[:].rearrange(S14, i=4))
  M(T160[:], T21, T22, 1280, T17, T18, 0, 0)
  TT(out=T146[:, 0, :], in0=T136[:], in1=T145[:], op=ALU.subtract)
  T161 = PP([128, 512], F, tag='l_0', bufs=1)
  M(T161[:], T12, T13, 1536, T8, T9, 1, 0)
  Q(T21[:, 1536:2048], T22[:, 1536:2048], T148[:].rearrange(S9))
  T152 = AQ.tile([128, 512, 4], B, tag='grouped_1', bufs=1, align_bytes=64)
  ve.tensor_copy(out=T152[:].rearrange(S13, i=4), in_=T149[:].rearrange(S14, i=4))
  M(T161[:], T21, T22, 1536, T17, T18, 0, 0)
  AC(T146[:], T146[:], ACT.Exp)
  Q(T30[:, 1024:1536], T31[:, 1024:1536], T150[:].rearrange(S9))
  Q(T30[:, 1536:2048], T31[:, 1536:2048], T152[:].rearrange(S9))
  M(T159[:], T30, T31, 1024, T26, T27, 0, 0)
  M(T160[:], T30, T31, 1280, T26, T27, 0, 0)
  T155 = AQ.tile([128, 512, 4], B, tag='grouped_0', bufs=1, align_bytes=64)
  ve.tensor_copy(out=T155[:].rearrange(S13, i=4), in_=T122[:].rearrange(S14, i=4))
  M(T161[:], T30, T31, 1536, T26, T27, 0, 0)
  T151 = AQ.tile([128, 4, 512], B, tag='wl_wide_0', bufs=1)
  AC(T151[:, 0, :], T121[:].rearrange(S8)[:, 0, 0:512].bitcast(E4), ACT.Copy, scale=T2[:, 3, 0:1])
  nc.gpsimd.tensor_tensor(out=T119[:, 1, :], in0=T146[:, 0, :], in1=T146[:, 1, :], op=ALU.add)
  AC(T151[:, 1, :], T121[:].rearrange(S8)[:, 1, 0:512].bitcast(E4), ACT.Copy, scale=T2[:, 3, 1:2])
  T125 = AQ.tile([128, 4, 512], B, tag='w2_raw_0', bufs=1)
  DM(out=T125[:], in_=w2[1, :, 512:1024].rearrange(S1, j=4))
  T14 = KP([128, 1024], U, tag='w2q0_codes', bufs=1, align_bytes=64)
  T15 = KP([128, 1024], U8, tag='w2q0_scales', bufs=1, align_bytes=64)
  Q(T14[:, 0:512], T15[:, 0:512], T155[:].rearrange(S9))
  AC(T151[:, 2, :], T121[:].rearrange(S8)[:, 2, 0:512].bitcast(E4), ACT.Copy, scale=T2[:, 3, 2:3])
  T172 = PP([128, 512], F, tag='h_1', bufs=1)
  M(T172[:], T14, T15, 0, T10, T11, 1, 1)
  T178 = AQ.tile([128, 512, 4], B, tag='grouped_0', bufs=1, align_bytes=64)
  ve.tensor_copy(out=T178[:].rearrange(S13, i=4), in_=T124[:].rearrange(S14, i=4))
  nc.gpsimd.tensor_tensor(out=T119[:, 1, :], in0=T119[:, 1, :], in1=T146[:, 2, :], op=ALU.add)
  T176 = PP([128, 512], F, tag='h_3', bufs=1)
  M(T176[:], T14, T15, 128, T10, T11, 1, 1)
  AC(T151[:, 3, :], T121[:].rearrange(S8)[:, 3, 0:512].bitcast(E4), ACT.Copy, scale=T2[:, 3, 3:4])
  T153 = AQ.tile([128, 4, 512], B, tag='wl_wide_1', bufs=1)
  AC(T153[:, 0, :], T121[:].rearrange(S8)[:, 0, 512:1024].bitcast(E4), ACT.Copy, scale=T2[:, 3, 0:1])
  T154 = AQ.tile([128, 512, 4], B, tag='grouped_2', bufs=1, align_bytes=64)
  ve.tensor_copy(out=T154[:].rearrange(S13, i=4), in_=T151[:].rearrange(S14, i=4))
  nc.gpsimd.tensor_tensor(out=T119[:, 1, :], in0=T119[:, 1, :], in1=T146[:, 3, :], op=ALU.add)
  AC(T153[:, 1, :], T121[:].rearrange(S8)[:, 1, 512:1024].bitcast(E4), ACT.Copy, scale=T2[:, 3, 1:2])
  AC(T153[:, 2, :], T121[:].rearrange(S8)[:, 2, 512:1024].bitcast(E4), ACT.Copy, scale=T2[:, 3, 2:3])
  AC(T153[:, 3, :], T121[:].rearrange(S8)[:, 3, 512:1024].bitcast(E4), ACT.Copy, scale=T2[:, 3, 3:4])
  T23 = KP([128, 1024], U, tag='w2q1_codes', bufs=1, align_bytes=64)
  T24 = KP([128, 1024], U8, tag='w2q1_scales', bufs=1, align_bytes=64)
  Q(T23[:, 0:512], T24[:, 0:512], T178[:].rearrange(S9))
  T156 = AQ.tile([128, 512, 4], B, tag='grouped_1', bufs=1, align_bytes=64)
  SC(T156[:].rearrange(S13, i=4), T153[:].rearrange(S14, i=4))
  Q(T39[:, 1024:1536], T40[:, 1024:1536], T154[:].rearrange(S9))
  T157 = AQ.tile([128, 512, 4], B, tag='grouped_2', bufs=1, align_bytes=64)
  ve.tensor_copy(out=T157[:].rearrange(S13, i=4), in_=T123[:].rearrange(S14, i=4))
  M(T159[:], T39, T40, 1024, T35, T36, 0, 1)
  M(T160[:], T39, T40, 1280, T35, T36, 0, 1)
  Q(T14[:, 512:1024], T15[:, 512:1024], T157[:].rearrange(S9))
  T191 = AQ.tile([128, 4, 512], B, tag='w2_raw_1', bufs=1)
  DM(out=T191[:], in_=w2[2, :, 0:512].rearrange(S1, j=4))
  T192 = AQ.tile([128, 4, 512], B, tag='w2_raw_2', bufs=1)
  DM(out=T192[:], in_=w2[2, :, 512:1024].rearrange(S1, j=4))
  T158 = AQ.tile([128, 512], F, tag='l0_0', bufs=1)
  SC(T158[:], T159[:])
  Q(T39[:, 1536:2048], T40[:, 1536:2048], T156[:].rearrange(S9))
  T171 = PP([128, 512], F, tag='h_0', bufs=1)
  M(T171[:], T14, T15, 512, T10, T11, 1, 1)
  T162 = PP([128, 512], F, tag='l_1', bufs=1)
  M(T162[:], T12, T13, 1792, T8, T9, 1, 0)
  T163 = AQ.tile([128, 512], F, tag='top_0', bufs=1)
  TT(out=T163[:], in0=T160[:], in1=T158[:], op=ALU.max)
  T185 = AQ.tile([128, 512, 4], B, tag='grouped_1', bufs=1, align_bytes=64)
  SC(T185[:].rearrange(S13, i=4), T125[:].rearrange(S14, i=4))
  M(T161[:], T39, T40, 1536, T35, T36, 0, 1)
  M(T162[:], T21, T22, 1792, T17, T18, 0, 0)
  TT(out=T163[:], in0=T161[:], in1=T163[:], op=ALU.max)
  M(T162[:], T30, T31, 1792, T26, T27, 0, 0)
  M(T162[:], T39, T40, 1792, T35, T36, 0, 1)
  T175 = PP([128, 512], F, tag='h_2', bufs=1)
  M(T175[:], T14, T15, 640, T10, T11, 1, 1)
  TT(out=T163[:], in0=T162[:], in1=T163[:], op=ALU.max)
  T164 = AQ.tile([128, 4, 512], F, tag='f8_2', bufs=1)
  TT(out=T164[:, 1, :], in0=T160[:], in1=T163[:], op=ALU.subtract)
  T173 = AQ.tile([128, 512], F, tag='th_0', bufs=1)
  AC(T173[:], T171[:], ACT.Tanh, scale=0.5)
  T213 = AQ.tile([128, 4, 512], B, tag='w2_raw_0', bufs=1)
  DM(out=T213[:], in_=w2[3, :, 0:512].rearrange(S1, j=4))
  TT(out=T164[:, 2, :], in0=T161[:], in1=T163[:], op=ALU.subtract)
  T166 = PP([128, 512], F, tag='l_2', bufs=1)
  M(T166[:], T12, T13, 1152, T8, T9, 1, 0)
  T177 = AQ.tile([128, 512], F, tag='th_1', bufs=1)
  AC(T177[:], T175[:], ACT.Tanh, scale=0.5)
  M(T166[:], T21, T22, 1152, T17, T18, 0, 0)
  TT(out=T164[:, 3, :], in0=T162[:], in1=T163[:], op=ALU.subtract)
  M(T166[:], T30, T31, 1152, T26, T27, 0, 0)
  T202 = AQ.tile([128, 512, 4], B, tag='grouped_2', bufs=1, align_bytes=64)
  SC(T202[:].rearrange(S13, i=4), T191[:].rearrange(S14, i=4))
  M(T166[:], T39, T40, 1152, T35, T36, 0, 1)
  TT(out=T164[:, 0, :], in0=T158[:], in1=T163[:], op=ALU.subtract)
  T167 = PP([128, 512], F, tag='l_0', bufs=1)
  M(T167[:], T12, T13, 1408, T8, T9, 1, 0)
  M(T167[:], T21, T22, 1408, T17, T18, 0, 0)
  T174 = AQ.tile([128, 512], F, tag='r_0', bufs=1)
  ST(out=T174[:], in0=T173[:], scalar=1.0, in1=T172[:], op0=ALU.add, op1=ALU.mult)
  M(T167[:], T30, T31, 1408, T26, T27, 0, 0)
  M(T167[:], T39, T40, 1408, T35, T36, 0, 1)
  T180 = AQ.tile([128, 512], F, tag='r_1', bufs=1)
  ST(out=T180[:], in0=T177[:], scalar=1.0, in1=T176[:], op0=ALU.add, op1=ALU.mult)
  T168 = PP([128, 512], F, tag='l_1', bufs=1)
  M(T168[:], T12, T13, 1664, T8, T9, 1, 0)
  M(T168[:], T21, T22, 1664, T17, T18, 0, 0)
  ST(out=T174[:], in0=T170[:, 0, :], scalar=T118[:, 0:1], in1=T174[:], op0=ALU.mult, op1=ALU.add)
  M(T168[:], T30, T31, 1664, T26, T27, 0, 0)
  M(T168[:], T39, T40, 1664, T35, T36, 0, 1)
  ST(out=T180[:], in0=T170[:, 1, :], scalar=T118[:, 1:2], in1=T180[:], op0=ALU.mult, op1=ALU.add)
  T165 = AQ.tile([128, 512], F, tag='l0_1', bufs=1)
  SC(T165[:], T166[:])
  T182 = PP([128, 512], F, tag='h_0', bufs=1)
  M(T182[:], T14, T15, 768, T10, T11, 1, 1)
  T214 = AQ.tile([128, 4, 512], B, tag='w2_raw_1', bufs=1)
  DM(out=T214[:], in_=w2[3, :, 512:1024].rearrange(S1, j=4))
  T183 = PP([128, 512], F, tag='h_1', bufs=1)
  M(T183[:], T14, T15, 256, T10, T11, 1, 1)
  Q(T23[:, 512:1024], T24[:, 512:1024], T185[:].rearrange(S9))
  AC(T164[:], T164[:], ACT.Exp)
  T169 = PP([128, 512], F, tag='l_2', bufs=1)
  M(T169[:], T12, T13, 1920, T8, T9, 1, 0)
  M(T169[:], T21, T22, 1920, T17, T18, 0, 0)
  T179 = AQ.tile([128, 512], F, tag='top_1', bufs=1)
  TT(out=T179[:], in0=T167[:], in1=T165[:], op=ALU.max)
  M(T169[:], T30, T31, 1920, T26, T27, 0, 0)
  M(T169[:], T39, T40, 1920, T35, T36, 0, 1)
  TT(out=T135[:, 0, :], in0=T135[:, 0, :], in1=T174[:], op=ALU.mult)
  T181 = PP([128, 2, 512], B, tag='x', bufs=1)
  TR(T181[:, 0, 0:128], T7[:, 0, 256:384], T3[:])
  TR(T181[:, 0, 128:256], T7[:, 1, 256:384], T3[:])
  TR(T181[:, 0, 256:384], T7[:, 2, 256:384], T3[:])
  TT(out=T179[:], in0=T168[:], in1=T179[:], op=ALU.max)
  TR(T181[:, 0, 384:512], T7[:, 3, 256:384], T3[:])
  TR(T181[:, 1, 0:128], T7[:, 0, 384:512], T3[:])
  TR(T181[:, 1, 128:256], T7[:, 1, 384:512], T3[:])
  TR(T181[:, 1, 256:384], T7[:, 2, 384:512], T3[:])
  TR(T181[:, 1, 384:512], T7[:, 3, 384:512], T3[:])
  T188 = PP([128, 512], F, tag='h_2', bufs=1)
  M(T188[:], T14, T15, 896, T10, T11, 1, 1)
  TT(out=T146[:, 0, :], in0=T146[:, 0, :], in1=T180[:], op=ALU.mult)
  T184 = AQ.tile([128, 512], F, tag='th_2', bufs=1)
  AC(T184[:], T182[:], ACT.Tanh, scale=0.5)
  T189 = PP([128, 512], F, tag='h_3', bufs=1)
  M(T189[:], T14, T15, 384, T10, T11, 1, 1)
  nc.gpsimd.tensor_tensor(out=T119[:, 2, :], in0=T164[:, 0, :], in1=T164[:, 1, :], op=ALU.add)
  T190 = AQ.tile([128, 512], F, tag='th_0', bufs=1)
  AC(T190[:], T188[:], ACT.Tanh, scale=0.5)
  TT(out=T179[:], in0=T169[:], in1=T179[:], op=ALU.max)
  T195 = PP([128, 512], F, tag='h_0', bufs=1)
  M(T195[:], T23, T24, 512, T19, T20, 1, 1)
  T208 = AQ.tile([128, 512, 4], B, tag='grouped_0', bufs=1, align_bytes=64)
  SC(T208[:].rearrange(S13, i=4), T192[:].rearrange(S14, i=4))
  T187 = AQ.tile([128, 512], F, tag='r_2', bufs=1)
  ST(out=T187[:], in0=T184[:], scalar=1.0, in1=T183[:], op0=ALU.add, op1=ALU.mult)
  T199 = PP([128, 512], F, tag='h_2', bufs=1)
  M(T199[:], T23, T24, 640, T19, T20, 1, 1)
  nc.gpsimd.tensor_tensor(out=T119[:, 2, :], in0=T119[:, 2, :], in1=T164[:, 2, :], op=ALU.add)
  T186 = AQ.tile([128, 4, 512], F, tag='f8_3', bufs=1)
  TT(out=T186[:, 1, :], in0=T167[:], in1=T179[:], op=ALU.subtract)
  T196 = PP([128, 512], F, tag='h_1', bufs=1)
  M(T196[:], T23, T24, 0, T19, T20, 1, 1)
  TT(out=T186[:, 2, :], in0=T168[:], in1=T179[:], op=ALU.subtract)
  nc.gpsimd.tensor_tensor(out=T119[:, 2, :], in0=T119[:, 2, :], in1=T164[:, 3, :], op=ALU.add)
  TT(out=T186[:, 3, :], in0=T169[:], in1=T179[:], op=ALU.subtract)
  TT(out=T186[:, 0, :], in0=T165[:], in1=T179[:], op=ALU.subtract)
  T197 = AQ.tile([128, 512], F, tag='th_1', bufs=1)
  AC(T197[:], T195[:], ACT.Tanh, scale=0.5)
  T193 = AQ.tile([128, 512], F, tag='r_3', bufs=1)
  ST(out=T193[:], in0=T190[:], scalar=1.0, in1=T189[:], op0=ALU.add, op1=ALU.mult)
  AC(T186[:], T186[:], ACT.Exp)
  T205 = PP([128, 512], F, tag='h_0', bufs=1)
  M(T205[:], T23, T24, 768, T19, T20, 1, 1)
  ST(out=T187[:], in0=T181[:, 0, :], scalar=T118[:, 2:3], in1=T187[:], op0=ALU.mult, op1=ALU.add)
  T200 = PP([128, 512], F, tag='h_3', bufs=1)
  M(T200[:], T23, T24, 128, T19, T20, 1, 1)
  T198 = AQ.tile([128, 512], F, tag='r_0', bufs=1)
  ST(out=T198[:], in0=T197[:], scalar=1.0, in1=T196[:], op0=ALU.add, op1=ALU.mult)
  ST(out=T193[:], in0=T181[:, 1, :], scalar=T118[:, 3:4], in1=T193[:], op0=ALU.mult, op1=ALU.add)
  T206 = PP([128, 512], F, tag='h_1', bufs=1)
  M(T206[:], T23, T24, 256, T19, T20, 1, 1)
  TT(out=T164[:, 0, :], in0=T164[:, 0, :], in1=T187[:], op=ALU.mult)
  T194 = PP([128, 2, 512], B, tag='x', bufs=1)
  TR(T194[:, 0, 0:128], T16[:, 0, 0:128], T3[:])
  T201 = AQ.tile([128, 512], F, tag='th_2', bufs=1)
  AC(T201[:], T199[:], ACT.Tanh, scale=0.5)
  nc.gpsimd.tensor_tensor(out=T119[:, 3, :], in0=T186[:, 0, :], in1=T186[:, 1, :], op=ALU.add)
  TR(T194[:, 0, 128:256], T16[:, 1, 0:128], T3[:])
  TR(T194[:, 0, 256:384], T16[:, 2, 0:128], T3[:])
  TR(T194[:, 0, 384:512], T16[:, 3, 0:128], T3[:])
  TR(T194[:, 1, 0:128], T16[:, 0, 128:256], T3[:])
  T32 = KP([128, 1024], U, tag='w2q2_codes', bufs=1, align_bytes=64)
  T33 = KP([128, 1024], U8, tag='w2q2_scales', bufs=1, align_bytes=64)
  Q(T32[:, 0:512], T33[:, 0:512], T202[:].rearrange(S9))
  TR(T194[:, 1, 128:256], T16[:, 1, 128:256], T3[:])
  TR(T194[:, 1, 256:384], T16[:, 2, 128:256], T3[:])
  TR(T194[:, 1, 384:512], T16[:, 3, 128:256], T3[:])
  T207 = AQ.tile([128, 512], F, tag='th_0', bufs=1)
  AC(T207[:], T205[:], ACT.Tanh, scale=0.5)
  T210 = PP([128, 512], F, tag='h_2', bufs=1)
  M(T210[:], T23, T24, 896, T19, T20, 1, 1)
  T203 = AQ.tile([128, 512], F, tag='r_1', bufs=1)
  ST(out=T203[:], in0=T201[:], scalar=1.0, in1=T200[:], op0=ALU.add, op1=ALU.mult)
  T224 = AQ.tile([128, 512, 4], B, tag='grouped_1', bufs=1, align_bytes=64)
  SC(T224[:].rearrange(S13, i=4), T213[:].rearrange(S14, i=4))
  nc.gpsimd.tensor_tensor(out=T119[:, 3, :], in0=T119[:, 3, :], in1=T186[:, 2, :], op=ALU.add)
  ST(out=T198[:], in0=T194[:, 0, :], scalar=T118[:, 4:5], in1=T198[:], op0=ALU.mult, op1=ALU.add)
  T211 = PP([128, 512], F, tag='h_3', bufs=1)
  M(T211[:], T23, T24, 384, T19, T20, 1, 1)
  TT(out=T186[:, 0, :], in0=T186[:, 0, :], in1=T193[:], op=ALU.mult)
  T209 = AQ.tile([128, 512], F, tag='r_2', bufs=1)
  ST(out=T209[:], in0=T207[:], scalar=1.0, in1=T206[:], op0=ALU.add, op1=ALU.mult)
  nc.gpsimd.tensor_tensor(out=T119[:, 3, :], in0=T119[:, 3, :], in1=T186[:, 3, :], op=ALU.add)
  ST(out=T203[:], in0=T194[:, 1, :], scalar=T118[:, 5:6], in1=T203[:], op0=ALU.mult, op1=ALU.add)
  T218 = PP([128, 512], F, tag='h_1', bufs=1)
  M(T218[:], T32, T33, 0, T28, T29, 1, 1)
  T212 = AQ.tile([128, 512], F, tag='th_1', bufs=1)
  AC(T212[:], T210[:], ACT.Tanh, scale=0.5)
  Q(T32[:, 512:1024], T33[:, 512:1024], T208[:].rearrange(S9))
  T204 = PP([128, 2, 512], B, tag='x', bufs=1)
  TR(T204[:, 0, 0:128], T16[:, 0, 256:384], T3[:])
  TR(T204[:, 0, 128:256], T16[:, 1, 256:384], T3[:])
  TR(T204[:, 0, 256:384], T16[:, 2, 256:384], T3[:])
  T230 = AQ.tile([128, 512, 4], B, tag='grouped_2', bufs=1, align_bytes=64)
  SC(T230[:].rearrange(S13, i=4), T214[:].rearrange(S14, i=4))
  TR(T204[:, 0, 384:512], T16[:, 3, 256:384], T3[:])
  TR(T204[:, 1, 0:128], T16[:, 0, 384:512], T3[:])
  TT(out=T135[:, 1, :], in0=T135[:, 1, :], in1=T198[:], op=ALU.mult)
  TR(T204[:, 1, 128:256], T16[:, 1, 384:512], T3[:])
  TR(T204[:, 1, 256:384], T16[:, 2, 384:512], T3[:])
  TR(T204[:, 1, 384:512], T16[:, 3, 384:512], T3[:])
  T217 = PP([128, 512], F, tag='h_0', bufs=1)
  M(T217[:], T32, T33, 512, T28, T29, 1, 1)
  T215 = AQ.tile([128, 512], F, tag='r_3', bufs=1)
  ST(out=T215[:], in0=T212[:], scalar=1.0, in1=T211[:], op0=ALU.add, op1=ALU.mult)
  T221 = PP([128, 512], F, tag='h_2', bufs=1)
  M(T221[:], T32, T33, 640, T28, T29, 1, 1)
  nc.gpsimd.tensor_tensor(out=T135[:, 0, :], in0=T135[:, 0, :], in1=T135[:, 1, :], op=ALU.add)
  ST(out=T209[:], in0=T204[:, 0, :], scalar=T118[:, 6:7], in1=T209[:], op0=ALU.mult, op1=ALU.add)
  T222 = PP([128, 512], F, tag='h_3', bufs=1)
  M(T222[:], T32, T33, 128, T28, T29, 1, 1)
  TT(out=T146[:, 1, :], in0=T146[:, 1, :], in1=T203[:], op=ALU.mult)
  ST(out=T215[:], in0=T204[:, 1, :], scalar=T118[:, 7:8], in1=T215[:], op0=ALU.mult, op1=ALU.add)
  nc.gpsimd.tensor_tensor(out=T146[:, 0, :], in0=T146[:, 0, :], in1=T146[:, 1, :], op=ALU.add)
  T219 = AQ.tile([128, 512], F, tag='th_2', bufs=1)
  AC(T219[:], T217[:], ACT.Tanh, scale=0.5)
  TT(out=T164[:, 1, :], in0=T164[:, 1, :], in1=T209[:], op=ALU.mult)
  T216 = PP([128, 2, 512], B, tag='x', bufs=1)
  TR(T216[:, 0, 0:128], T25[:, 0, 0:128], T3[:])
  T223 = AQ.tile([128, 512], F, tag='th_0', bufs=1)
  AC(T223[:], T221[:], ACT.Tanh, scale=0.5)
  TR(T216[:, 0, 128:256], T25[:, 1, 0:128], T3[:])
  TR(T216[:, 0, 256:384], T25[:, 2, 0:128], T3[:])
  TR(T216[:, 0, 384:512], T25[:, 3, 0:128], T3[:])
  TR(T216[:, 1, 0:128], T25[:, 0, 128:256], T3[:])
  T220 = AQ.tile([128, 512], F, tag='r_0', bufs=1)
  ST(out=T220[:], in0=T219[:], scalar=1.0, in1=T218[:], op0=ALU.add, op1=ALU.mult)
  TR(T216[:, 1, 128:256], T25[:, 1, 128:256], T3[:])
  TR(T216[:, 1, 256:384], T25[:, 2, 128:256], T3[:])
  TR(T216[:, 1, 384:512], T25[:, 3, 128:256], T3[:])
  nc.gpsimd.tensor_tensor(out=T164[:, 0, :], in0=T164[:, 0, :], in1=T164[:, 1, :], op=ALU.add)
  T227 = PP([128, 512], F, tag='h_0', bufs=1)
  M(T227[:], T32, T33, 768, T28, T29, 1, 1)
  T225 = AQ.tile([128, 512], F, tag='r_1', bufs=1)
  ST(out=T225[:], in0=T223[:], scalar=1.0, in1=T222[:], op0=ALU.add, op1=ALU.mult)
  T232 = PP([128, 512], F, tag='h_2', bufs=1)
  M(T232[:], T32, T33, 896, T28, T29, 1, 1)
  T229 = AQ.tile([128, 512], F, tag='th_1', bufs=1)
  AC(T229[:], T227[:], ACT.Tanh, scale=0.5)
  T228 = PP([128, 512], F, tag='h_1', bufs=1)
  M(T228[:], T32, T33, 256, T28, T29, 1, 1)
  ST(out=T220[:], in0=T216[:, 0, :], scalar=T118[:, 8:9], in1=T220[:], op0=ALU.mult, op1=ALU.add)
  T233 = PP([128, 512], F, tag='h_3', bufs=1)
  M(T233[:], T32, T33, 384, T28, T29, 1, 1)
  T234 = AQ.tile([128, 512], F, tag='th_2', bufs=1)
  AC(T234[:], T232[:], ACT.Tanh, scale=0.5)
  TT(out=T186[:, 1, :], in0=T186[:, 1, :], in1=T215[:], op=ALU.mult)
  AC(T119[:, 0:4, :], T119[:, 0:4, :], ACT.Ln, scale=2.0)
  T231 = AQ.tile([128, 512], F, tag='r_2', bufs=1)
  ST(out=T231[:], in0=T229[:], scalar=1.0, in1=T228[:], op0=ALU.add, op1=ALU.mult)
  nc.gpsimd.tensor_tensor(out=T186[:, 0, :], in0=T186[:, 0, :], in1=T186[:, 1, :], op=ALU.add)
  T41 = KP([128, 1024], U, tag='w2q3_codes', bufs=1, align_bytes=64)
  T42 = KP([128, 1024], U8, tag='w2q3_scales', bufs=1, align_bytes=64)
  Q(T41[:, 0:512], T42[:, 0:512], T224[:].rearrange(S9))
  ST(out=T225[:], in0=T216[:, 1, :], scalar=T118[:, 9:10], in1=T225[:], op0=ALU.mult, op1=ALU.add)
  T238 = PP([128, 512], F, tag='h_1', bufs=1)
  M(T238[:], T41, T42, 0, T37, T38, 1, 1)
  Q(T41[:, 512:1024], T42[:, 512:1024], T230[:].rearrange(S9))
  T226 = PP([128, 2, 512], B, tag='x', bufs=1)
  TR(T226[:, 0, 0:128], T25[:, 0, 256:384], T3[:])
  TR(T226[:, 0, 128:256], T25[:, 1, 256:384], T3[:])
  TR(T226[:, 0, 256:384], T25[:, 2, 256:384], T3[:])
  TR(T226[:, 0, 384:512], T25[:, 3, 256:384], T3[:])
  TR(T226[:, 1, 0:128], T25[:, 0, 384:512], T3[:])
  TT(out=T135[:, 2, :], in0=T135[:, 2, :], in1=T220[:], op=ALU.mult)
  TR(T226[:, 1, 128:256], T25[:, 1, 384:512], T3[:])
  TR(T226[:, 1, 256:384], T25[:, 2, 384:512], T3[:])
  TR(T226[:, 1, 384:512], T25[:, 3, 384:512], T3[:])
  T237 = PP([128, 512], F, tag='h_0', bufs=1)
  M(T237[:], T41, T42, 512, T37, T38, 1, 1)
  T235 = AQ.tile([128, 512], F, tag='r_3', bufs=1)
  ST(out=T235[:], in0=T234[:], scalar=1.0, in1=T233[:], op0=ALU.add, op1=ALU.mult)
  T241 = PP([128, 512], F, tag='h_2', bufs=1)
  M(T241[:], T41, T42, 640, T37, T38, 1, 1)
  nc.gpsimd.tensor_tensor(out=T135[:, 0, :], in0=T135[:, 0, :], in1=T135[:, 2, :], op=ALU.add)
  ST(out=T231[:], in0=T226[:, 0, :], scalar=T118[:, 10:11], in1=T231[:], op0=ALU.mult, op1=ALU.add)
  T242 = PP([128, 512], F, tag='h_3', bufs=1)
  M(T242[:], T41, T42, 128, T37, T38, 1, 1)
  T239 = AQ.tile([128, 512], F, tag='th_0', bufs=1)
  AC(T239[:], T237[:], ACT.Tanh, scale=0.5)
  TT(out=T146[:, 2, :], in0=T146[:, 2, :], in1=T225[:], op=ALU.mult)
  AC(T119[:, 0:4, :], T119[:, 0:4, :], ACT.Exp, scale=-1.0)
  T246 = PP([128, 512], F, tag='h_0', bufs=1)
  M(T246[:], T41, T42, 768, T37, T38, 1, 1)
  T240 = AQ.tile([128, 512], F, tag='r_0', bufs=1)
  ST(out=T240[:], in0=T239[:], scalar=1.0, in1=T238[:], op0=ALU.add, op1=ALU.mult)
  nc.gpsimd.tensor_tensor(out=T146[:, 0, :], in0=T146[:, 0, :], in1=T146[:, 2, :], op=ALU.add)
  ST(out=T235[:], in0=T226[:, 1, :], scalar=T118[:, 11:12], in1=T235[:], op0=ALU.mult, op1=ALU.add)
  T247 = PP([128, 512], F, tag='h_1', bufs=1)
  M(T247[:], T41, T42, 256, T37, T38, 1, 1)
  TT(out=T164[:, 2, :], in0=T164[:, 2, :], in1=T231[:], op=ALU.mult)
  T236 = PP([128, 2, 512], B, tag='x', bufs=1)
  TR(T236[:, 0, 0:128], T34[:, 0, 0:128], T3[:])
  TR(T236[:, 0, 128:256], T34[:, 1, 0:128], T3[:])
  TR(T236[:, 0, 256:384], T34[:, 2, 0:128], T3[:])
  TR(T236[:, 0, 384:512], T34[:, 3, 0:128], T3[:])
  TR(T236[:, 1, 0:128], T34[:, 0, 128:256], T3[:])
  TT(out=T186[:, 2, :], in0=T186[:, 2, :], in1=T235[:], op=ALU.mult)
  TR(T236[:, 1, 128:256], T34[:, 1, 128:256], T3[:])
  TR(T236[:, 1, 256:384], T34[:, 2, 128:256], T3[:])
  nc.gpsimd.tensor_tensor(out=T164[:, 0, :], in0=T164[:, 0, :], in1=T164[:, 2, :], op=ALU.add)
  TR(T236[:, 1, 384:512], T34[:, 3, 128:256], T3[:])
  ST(out=T240[:], in0=T236[:, 0, :], scalar=T118[:, 12:13], in1=T240[:], op0=ALU.mult, op1=ALU.add)
  TT(out=T135[:, 3, :], in0=T135[:, 3, :], in1=T240[:], op=ALU.mult)
  nc.gpsimd.tensor_tensor(out=T186[:, 0, :], in0=T186[:, 0, :], in1=T186[:, 2, :], op=ALU.add)
  T243 = AQ.tile([128, 512], F, tag='th_1', bufs=1)
  AC(T243[:], T241[:], ACT.Tanh, scale=0.5)
  TT(out=T135[:, 3, :], in0=T135[:, 0, :], in1=T135[:, 3, :], op=ALU.add)
  T248 = AQ.tile([128, 512], F, tag='th_2', bufs=1)
  AC(T248[:], T246[:], ACT.Tanh, scale=0.5)
  T250 = PP([128, 512], F, tag='h_2', bufs=1)
  M(T250[:], T41, T42, 896, T37, T38, 1, 1)
  T244 = AQ.tile([128, 512], F, tag='r_1', bufs=1)
  ST(out=T244[:], in0=T243[:], scalar=1.0, in1=T242[:], op0=ALU.add, op1=ALU.mult)
  T252 = AQ.tile([128, 512], F, tag='th_0', bufs=1)
  AC(T252[:], T250[:], ACT.Tanh, scale=0.5)
  T249 = AQ.tile([128, 512], F, tag='r_2', bufs=1)
  ST(out=T249[:], in0=T248[:], scalar=1.0, in1=T247[:], op0=ALU.add, op1=ALU.mult)
  T251 = PP([128, 512], F, tag='h_3', bufs=1)
  M(T251[:], T41, T42, 384, T37, T38, 1, 1)
  ST(out=T244[:], in0=T236[:, 1, :], scalar=T118[:, 13:14], in1=T244[:], op0=ALU.mult, op1=ALU.add)
  T253 = AQ.tile([128, 512], F, tag='r_3', bufs=1)
  ST(out=T253[:], in0=T252[:], scalar=1.0, in1=T251[:], op0=ALU.add, op1=ALU.mult)
  T245 = PP([128, 2, 512], B, tag='x', bufs=1)
  TR(T245[:, 0, 0:128], T34[:, 0, 256:384], T3[:])
  TR(T245[:, 0, 128:256], T34[:, 1, 256:384], T3[:])
  TR(T245[:, 0, 256:384], T34[:, 2, 256:384], T3[:])
  TR(T245[:, 0, 384:512], T34[:, 3, 256:384], T3[:])
  TR(T245[:, 1, 0:128], T34[:, 0, 384:512], T3[:])
  TT(out=T146[:, 3, :], in0=T146[:, 3, :], in1=T244[:], op=ALU.mult)
  TR(T245[:, 1, 128:256], T34[:, 1, 384:512], T3[:])
  TR(T245[:, 1, 256:384], T34[:, 2, 384:512], T3[:])
  TR(T245[:, 1, 384:512], T34[:, 3, 384:512], T3[:])
  ST(out=T249[:], in0=T245[:, 0, :], scalar=T118[:, 14:15], in1=T249[:], op0=ALU.mult, op1=ALU.add)
  ST(out=T253[:], in0=T245[:, 1, :], scalar=T118[:, 15:16], in1=T253[:], op0=ALU.mult, op1=ALU.add)
  TT(out=T164[:, 3, :], in0=T164[:, 3, :], in1=T249[:], op=ALU.mult)
  TT(out=T146[:, 3, :], in0=T146[:, 0, :], in1=T146[:, 3, :], op=ALU.add)
  TT(out=T135[:, 3, :], in0=T135[:, 3, :], in1=T119[:, 0, :], op=ALU.mult)
  TT(out=T186[:, 3, :], in0=T186[:, 3, :], in1=T253[:], op=ALU.mult)
  T254 = PP([128, 4, 128], F, tag='l_0', bufs=1)
  TR(T254[:, 0, :], T135[:, 3, 0:128], T0[:])
  TR(T254[:, 1, :], T135[:, 3, 128:256], T0[:])
  TR(T254[:, 2, :], T135[:, 3, 256:384], T0[:])
  TR(T254[:, 3, :], T135[:, 3, 384:512], T0[:])
  TT(out=T164[:, 3, :], in0=T164[:, 0, :], in1=T164[:, 3, :], op=ALU.add)
  T255 = AQ.tile([128, 4, 128], F, tag='rows_0', bufs=1)
  SC(T255[:], T254[:])
  TT(out=T146[:, 3, :], in0=T146[:, 3, :], in1=T119[:, 1, :], op=ALU.mult)
  DM(out=out[:, 0:128].rearrange(S3, p=128), in_=T255[:])
  TT(out=T186[:, 3, :], in0=T186[:, 0, :], in1=T186[:, 3, :], op=ALU.add)
  T256 = PP([128, 4, 128], F, tag='l_1', bufs=1)
  TR(T256[:, 0, :], T146[:, 3, 0:128], T0[:])
  TR(T256[:, 1, :], T146[:, 3, 128:256], T0[:])
  TR(T256[:, 2, :], T146[:, 3, 256:384], T0[:])
  TR(T256[:, 3, :], T146[:, 3, 384:512], T0[:])
  TT(out=T164[:, 3, :], in0=T164[:, 3, :], in1=T119[:, 2, :], op=ALU.mult)
  T257 = AQ.tile([128, 4, 128], F, tag='rows_1', bufs=1)
  SC(T257[:], T256[:])
  TT(out=T186[:, 3, :], in0=T186[:, 3, :], in1=T119[:, 3, :], op=ALU.mult)
  T258 = PP([128, 4, 128], F, tag='l_2', bufs=1)
  TR(T258[:, 0, :], T164[:, 3, 0:128], T0[:])
  DM(out=out[:, 128:256].rearrange(S3, p=128), in_=T257[:])
  TR(T258[:, 1, :], T164[:, 3, 128:256], T0[:])
  TR(T258[:, 2, :], T164[:, 3, 256:384], T0[:])
  TR(T258[:, 3, :], T164[:, 3, 384:512], T0[:])
  T260 = PP([128, 4, 128], F, tag='l_0', bufs=1)
  TR(T260[:, 0, :], T186[:, 3, 0:128], T0[:])
  TR(T260[:, 1, :], T186[:, 3, 128:256], T0[:])
  TR(T260[:, 2, :], T186[:, 3, 256:384], T0[:])
  TR(T260[:, 3, :], T186[:, 3, 384:512], T0[:])
  T259 = AQ.tile([128, 4, 128], F, tag='rows_0', bufs=1)
  SC(T259[:], T258[:])
  DM(out=out[:, 256:384].rearrange(S3, p=128), in_=T259[:])
  T261 = AQ.tile([128, 4, 128], F, tag='rows_1', bufs=1)
  SC(T261[:], T260[:])
  DM(out=out[:, 384:512].rearrange(S3, p=128), in_=T261[:])
